import numpy as np, ml_dtypes
CORES = [40,41,42,43,44,45,46,47]
N = 8
BF = ml_dtypes.bfloat16
def gentries(a):
    return np.ascontiguousarray(a.reshape(8, 16, -1).transpose(0, 2, 1)).reshape(8, -1)
def gtable(e):
    e = np.asarray(e); return np.ascontiguousarray(e.reshape(8, -1, 16).transpose(0, 2, 1)).reshape(128, -1).astype(np.int32)
W, R, S, K, M = 4096, 512, 128, 32, 97
V, STEP = W + R, (1, 2, 3)
RO = len(STEP)
def tops(st, s):
    col = np.take_along_axis(st, s[:, :, None], 3); h = np.add.reduce((col > 0).astype(np.int64), axis=2)
    return col, h, np.take_along_axis(col, np.maximum(h - 1, 0)[:, :, None], 2)[:, :, 0]
def aim(b, c):
    return (c - M * b) & (W - 1)
def fill(h, v):
    return np.where(np.arange(16)[:, None] < h, v, 0)
def parts(rng):
    share = np.array([0.0, 0.0, 0.1, 0.1, 0.3, 0.5, 0.8, 0.92])
    q = np.stack([rng.permutation(share) for a in range(N)]).reshape(N, 8, 1, 1); lo = np.stack([rng.permutation(8) for a in range(N)]).reshape(N, 8, 1, 1)
    h = lo + ((17 - lo) * rng.random((N, 8, 1, V))).astype(np.int64); h = np.minimum(np.where(rng.random((N, 8, 1, V)) < q, 16, h), 16)
    v = np.minimum(1 + (255 * rng.random((N, 8, 16, V)) ** rng.choice(np.array([0.5, 1.0, 2.0]), (N, 8, 1, 1))).astype(np.int64), 255)
    first = np.argsort(rng.random((N, 8, 1, V)), axis=-1)[..., :S]; later = W + np.argsort(rng.random((N, 8, RO - 1, R)), axis=-1)[..., :S]
    return fill(h, v), np.concatenate([first, later], axis=2), rng.integers(0, W, (N, 8, RO, K, S))
def pack(st, tr, ca):
    return {"days": np.ascontiguousarray(st.reshape(N, 128, V)).astype(np.float32).astype(BF),
            "trucks": np.stack([gtable(a.reshape(8, -1)) for a in tr]), "cand": np.stack([gtable(a.reshape(8, -1)) for a in ca])}
def setup_inputs(rng):
    return pack(*parts(rng))
def setup_inputs_ties(rng):
    st, tr, ca = parts(rng)
    p = rng.integers(1, 254, (N, 8, 1, 1)); p[0, 0] = 1; p[0, 1] = 253
    v = p + rng.integers(0, 3, st.shape); v[:, 2] = np.broadcast_to(p[:, 2], v[:, 2].shape); st = np.where(st > 0, v, 0)
    ca[:, :, :, K // 2:] = ca[:, :, :, :K // 2]
    e = 1 + np.argsort(rng.random((N, 4, V - 2)), axis=-1)[..., :S]; e[..., 0] = 0; e[..., S - 1] = V - 1; tr[:, 0::2, 0] = e
    e = W + 1 + np.argsort(rng.random((N, 4, RO - 1, R - 2)), axis=-1)[..., :S]; e[..., 0] = V - 1; e[..., S - 1] = W; tr[:, 1::2, 1:] = e
    b = np.roll(tops(st, tr[:, :, 0])[2], STEP[0], axis=0); n = S // 4
    ca[:, :, 0, :, :n] = aim(b[:, :, None, :n], rng.choice(np.array([0, W - 1]), (N, 8, K, n)))
    return pack(st, tr, ca)
def setup_inputs_full(rng):
    st, tr, ca = parts(rng)
    st = fill(np.where(rng.random((N, 8, 1, V)) < 0.8, 16, 15), rng.integers(1, 256, (N, 8, 16, V)))
    for a in range(N):
        for g in range(8):
            x = st[a, g]; s = tr[a, g, 0]
            x[:, s] = np.where(x[:, s] == 0, 7, x[:, s]); x[15, rng.permutation(s)[:S // 2]] = 1
    b = np.roll(tops(st, tr[:, :, 0])[2], STEP[0], axis=0); n = S // 8
    for a in range(N):
        for g in range(8):
            x = st[a, g]; s = tr[a, g, 0]; i = rng.permutation(S); c = ca[a, g, 0]
            rest = rng.permutation(np.setdiff1d(np.arange(W), s)); early, late = rest[:n], rest[n:2 * n]
            x[:, early] = fill(15, 1); x[:, late] = fill(16, 255)
            room = np.setdiff1d(np.nonzero(x[15, :W] == 0)[0], early)
            j = i[:S // 2]; c[:, j] = aim(b[a, g, j], rng.choice(s[s < W], (K, S // 2)))
            j = i[:n]; c[K - 1, j] = aim(b[a, g, j], rng.choice(room, n))
            j = i[S // 2:S // 2 + n]; c[:, j] = aim(b[a, g, j], rng.choice(late, (K, n))); c[K - 1, j] = aim(b[a, g, j], early)
    return pack(st, tr, ca)
def setup_inputs_bare(rng):
    st, tr, ca = parts(rng)
    o = rng.permutation(8); h = rng.integers(0, 4, (N, 8, 1, V)); h[:, o[0]] = 0; h[:, o[1]] = 1; h[:, o[2]] = rng.integers(0, 3, (N, 1, V))
    st = fill(h, rng.integers(1, 256, (N, 8, 16, V)))
    b = np.roll(tops(st, tr[:, :, 0])[2], STEP[0], axis=0)
    for a in range(N):
        for g in o[3:6]:
            s = tr[a, g, 0]; ca[a, g, 0][0] = aim(b[a, g], rng.choice(s[s < W], S))
    return pack(st, tr, ca)
def setup_inputs_crowd(rng):
    st, tr, ca = parts(rng); goals = []; q = int(rng.integers(0, N)); z = (q + STEP[0]) % N
    for a in range(N):
        for g in range(8):
            x = st[a, g]
            if a == z:
                o = int(rng.integers(0, W - S + 1)); o = o - o % S if g < 2 else o
                run = o + rng.permutation(S); x[15, run] = 0
                if g % 2 == 1:
                    tr[a, g, 0] = rng.permutation(run); x[:, run] = fill(rng.integers(1, 16, S), rng.integers(1, 256, S))
            s = tr[a, g, 0]
            if g % 2 == 0 or a == q:
                x[1:, s] = np.where(x[1:, s] > 0, np.maximum(x[1:, s], 2), 0); x[0, s] = 1; x[1, s] = np.maximum(x[1, s], 2)
            if a == z:
                goals.append(run)
            else:
                free = rng.permutation(np.setdiff1d(np.arange(W), s))[:(1, 2, S // 2, 1)[g // 2]]
                if g < 6: x[:, free] = 0
                goals.append(free if g < 6 else s[s < W])
    b = np.roll(tops(st, tr[:, :, 0])[2], STEP[0], axis=0)
    for a in range(N):
        for g in range(8):
            c = ca[a, g, 0]; k = 0 if a == q else int(rng.integers(0, K))
            if a == z: c[:] = aim(b[a, g], goals[8 * a + g])
            elif g < 6: c[k] = aim(b[a, g], rng.choice(goals[8 * a + g], S))
            else: c[:] = aim(b[a, g], rng.choice(goals[8 * a + g], (K, S)))
    ca[:, ::2, 1:] = rng.integers(0, 8, (N, 4, RO - 1, K, S)) + rng.integers(0, W - 8, (N, 4, RO - 1, 1, 1))
    return pack(st, tr, ca)
def setup_inputs_spread(rng):
    st, tr, ca = parts(rng)
    h = np.minimum((17 * rng.random((N, 8, 1, V)) ** rng.choice(np.array([0.2, 0.5, 1.0, 3.0]), (N, 8, 1, 1))).astype(np.int64), 16)
    v = np.minimum(np.maximum((np.exp2(8 * rng.random((N, 8, 1, V))) * rng.random((N, 8, 16, V))).astype(np.int64), 1), 255)
    ca = np.minimum((W * rng.random((N, 8, RO, K, S)) ** rng.choice(np.array([0.5, 1.0, 2.0, 4.0]), (N, 8, RO, 1, 1))).astype(np.int64), W - 1)
    return pack(fill(h, v), tr, ca)
def check_inputs(d):
    bad = []; x = np.asarray(d["days"]).astype(np.float32)
    if not np.all((x >= 0) & (x <= 255) & (x == np.floor(x))): bad.append("days: whole numbers from 0 to 255")
    z = x.reshape(N, 8, 16, V) > 0
    if np.any(z[:, :, 1:] & ~z[:, :, :-1]): bad.append("days: no box above an empty tier")
    s = np.stack([gentries(a) for a in d["trucks"]]).astype(np.int64).reshape(N, 8, RO, S)
    if np.min(s) < 0 or np.max(s) > V - 1 or np.min(s[:, :, 1:]) < W: bad.append("range of trucks")
    o = np.sort(s, axis=-1)
    if np.any(o[..., 1:] == o[..., :-1]): bad.append("trucks: different stacks in a block")
    if np.min(d["cand"]) < 0 or np.max(d["cand"]) > W - 1: bad.append("range of cand")
    return bad
def reference(days, trucks, cand):
    st = np.asarray(days).astype(np.float32).astype(np.int64).reshape(N, 8, 16, V)
    tr = np.stack([gentries(a) for a in trucks]).astype(np.int64).reshape(N, 8, RO, S)
    ca = np.stack([gentries(a) for a in cand]).astype(np.int64).reshape(N, 8, RO, K, S)
    lower = np.tril(np.ones((S, S), bool), -1); s = tr[:, :, 0]
    for t in range(RO):
        col, h, b = tops(st, s)
        asks = np.any((col > 0) & (col < b[:, :, None]), axis=2)
        bb = np.roll(b, STEP[t], axis=0); ask = np.roll(asks, STEP[t], axis=0)
        c = (ca[:, :, t] + M * bb[:, :, None]) & (W - 1)
        cc = np.take_along_axis(st, c.reshape(N, 8, 1, K * S), 3).reshape(N, 8, 16, K, S)
        score = np.add.reduce(((cc > 0) & (cc < bb[:, :, None, None])).astype(np.int64), axis=2) + 16 * (cc[:, :, 15] > 0)
        best = np.argmin(score, axis=2)[:, :, None]
        dst = np.take_along_axis(c, best, 2)[:, :, 0]; low = np.take_along_axis(score, best, 2)[:, :, 0]
        clash = np.any((dst[..., :, None] == dst[..., None, :]) & ask[..., None, :] & lower, axis=3)
        land = ask & (low < 16) & ~clash
        gone = (b > 0) & (~asks | np.roll(land, -STEP[t], axis=0))
        st = st.copy()
        a, g, i = np.nonzero(gone); st[a, g, h[a, g, i] - 1, s[a, g, i]] = 0
        a, g, i = np.nonzero(land); v = dst[a, g, i]
        top = np.add.reduce((st[a, g, :, v] > 0).astype(np.int64), axis=1); st[a, g, top, v] = bb[a, g, i]
        if t + 1 < RO: s = np.where(land, dst, tr[:, :, t + 1])
    return {"y": st.reshape(N, 128, V).astype(np.float32).astype(BF)}

@@ -1,0 +1,654 @@
+from concourse.bass import DstId, RemoteDMATransfer
+from concourse.mybir import AluOpType as A, AxisListType, ActivationFunctionType as F
+
+N, W, V, S, K = 8, 4096, 4608, 128, 32
+STEP = (1, 2, 3)
+KV = 21
+VCH = [(0, 2), (2, 6), (6, 10), (10, 14), (14, 18), (18, 21)]
+SCH = [(21, 25), (25, 29), (29, 32)]
+UNIT = 1 << 18
+SEG = [16 * (q + 1) for q in range(8)]
+SOFF = [(1, 0), (1, 16), (1, 48), (1, 96), (1, 160), (2, 0), (2, 96), (2, 208)]
+TOFF = [0, 16, 48, 96, 160, 240, 336, 448]
+CH = [(0, 1024), (1024, 2048), (2048, 3072), (3072, 4096), (4096, 4608)]
+
+bf, f32, i32, u16, f16 = "bfloat16", "float32", "int32", "uint16", "float16"
+SCRATCH = {}
+WHERE = {}
+for _n, _w, _d in [
+    ("Y", V + S, bf), ("Z", V + S, bf), ("t256", V, bf), ("trk", 24, i32), ("cnd", 768, i32),
+    ("ones", 128, bf), ("I", 128, bf), ("nI", 128, bf), ("I256", 128, bf), ("I15", 128, bf), ("Bo0", 128, bf),
+    ("Bo", 128, bf), ("nBo", 128, bf), ("Bq", 128, bf), ("nUp", 128, bf), ("Up2", 128, bf), ("nDn", 128, bf),
+    ("TopM", 128, bf), ("FstE", 128, bf), ("E0", 128, bf), ("mask", 128, bf), ("rst", 256, bf), ("c26", 8, bf),
+    ("c97", 256, bf), ("Q0", 256, bf), ("Q1", 256, bf), ("Q97", 256, bf), ("turn", 128, bf), ("dfa", 99, bf),
+    ("dfb", 99, bf), ("I16", 128, f16), ("ones16", 128, f16), ("Q16", 16, f16), ("pm16", 128, f16),
+    ("RB", 576, f16), ("nil16", 336, f16), ("tri", 16, f16), ("dif", 99, f16), ("P16", 768, f16), ("X16", 1024, f16),
+    ("Wv", 8, bf), ("Ws", 8, bf), ("W97", 8, bf), ("W23", 8, bf),
+    ("ia", 128, i32), ("ib", 128, i32), ("ic", 16, i32), ("idd", 16, i32), ("ex", 16, u16), ("rowj", 256, bf),
+    ("kp", 792, f32), ("JT", 1280, bf), ("jo", 32, u16),
+    ("jg", 128, bf), ("jm", 256, bf), ("js", 256, bf), ("jv", 256, bf), ("m2", 256, bf),
+    ("md1", 128, bf), ("jx1", 8, u16), ("SL", 72, u16), ("dU", 8, u16),
+    ("PW", 768, bf), ("Wn1", 384, bf), ("Wn2", 384, bf), ("XD0", 384, bf), ("XD1", 384, bf), ("PA", 768, bf),
+    ("PB", 512, bf), ("RA", 768, bf), ("RG", 384, bf), ("PG", 384, bf), ("PN", 256, bf), ("PO", 256, u16),
+    ("RO1", 128, u16), ("RO2", 128, u16), ("p0", 128, bf), ("lrow", 144, bf),
+    ("xm", 128, bf), ("ci", 256, i32), ("cj", 256, i32), ("cu", 256, u16), ("thr", 512, bf), ("cmp", 4096, bf),
+    ("raw", 1536, bf), ("sc", 264, f32), ("ki", 8, i32), ("km", 8, i32), ("A16", 128, f16), ("B16", 128, f16),
+    ("Rm", 256, bf),
+    ("zz", 256, bf), ("tt", 256, bf), ("pr", 384, bf), ("rl", 128, bf), ("geN", 128, bf), ("ed", 128, bf),
+    ("zd", 128, bf), ("fd", 128, bf), ("zp", 128, bf), ("dl", 128, bf), ("uu", 128, bf), ("braw", 128, bf),
+    ("ra", 128, bf), ("rb", 128, bf), ("rc", 128, bf), ("rd", 128, bf), ("td", 128, bf), ("yd", 128, bf),
+]:
+    SCRATCH[_n] = ("sbuf", [128, _w], _d)
+    WHERE[_n] = (_n, 0, _w)
+_c = 0
+for _n, _w in [("cols", 8), ("ngr", 8), ("nL", 8), ("trf", 24), ("jtmp", 32), ("n128", 16), ("n256", 8), ("base", 16),
+               ("doff", 16), ("b16", 48), ("mn", 8), ("land", 16), ("ta", 16), ("tb", 16), ("tc", 16), ("oa", 8),
+               ("ob", 8)]:
+    WHERE[_n] = ("small", _c, _w)
+    _c += _w
+SCRATCH["small"] = ("sbuf", [128, _c], f32)
+for _b in range(8):
+    SCRATCH["B%d" % _b] = ("psum", [128, 512], f32)
+    WHERE["B%d" % _b] = ("B%d" % _b, 0, 512)
+
+ARR = ["b0", "ma0", "ma1", "ma2", "mb0", "mb1", "mw0", "mw1", "mo0", "mo1", "mg0", "mg1", "mg2", "mn0", "mn1"]
+SEMAPHORES = ["ev", "es", "ep", "eg", "sent"] + ["d%d" % _i for _i in range(10)] + ARR
+
+
+def rank_program(g, core, T, topo):
+    rank = T.rank_of(core)
+    if rank is None:
+        return
+    Q = {"v": g.vector, "s": g.scalar, "p": g.tensor, "g": g, "y": g.sync}
+    ESEM = {"v": "ev", "s": "es", "p": "ep", "g": "eg"}
+    cnt = {"ev": 0, "es": 0, "ep": 0, "eg": 0}
+    known = {e: {} for e in Q}
+    clock = {}
+    hist = {}
+    sent = [0]
+    ndma = [0]
+
+    def R(name, lo=0, hi=None, step=1, parts=128, p0=0):
+        buf, c0, w = WHERE[name]
+        lo, hi = c0 + lo, c0 + (w if hi is None else hi)
+        ap = T[buf][p0:parts, lo:hi] if step == 1 else T[buf][p0:parts, lo:hi:step]
+        return (ap, [(buf, lo, hi)])
+
+    def IND(win, off):
+        return (win[0].indirect(off[0]), win[1], off[1])
+
+    def need(e, toks):
+        kn = known[e]
+        best = {}
+        for (s, c) in toks:
+            if kn.get(s, 0) < c and best.get(s, 0) < c:
+                best[s] = c
+        for s in sorted(best, key=lambda x: -len(clock.get((x, best[x]), {}))):
+            c = best[s]
+            if kn.get(s, 0) >= c:
+                continue
+            Q[e].wait_ge(T.sem[s], c)
+            kn[s] = c
+            for s2, c2 in clock.get((s, c), {}).items():
+                if kn.get(s2, 0) < c2:
+                    kn[s2] = c2
+
+    def order(e, reads, writes):
+        toks = []
+        for regs, wr in ((reads, False), (writes, True)):
+            for (n, lo, hi) in regs:
+                ps = SCRATCH[n][0] == "psum"
+                for (l2, h2, w2, e2, tok) in hist.get(n, []):
+                    if ps and e2 != e:
+                        toks.append(tok)
+                    elif ps and e == "p":
+                        continue
+                    elif lo < h2 and l2 < hi and (wr or w2):
+                        toks.append(tok)
+        need(e, toks)
+
+    def note(e, reads, writes, tok):
+        clock[tok] = dict(known[e]) if e in known else {}
+        for regs, wr in ((reads, False), (writes, True)):
+            for (n, lo, hi) in regs:
+                hist.setdefault(n, []).append((lo, hi, wr, e, tok))
+
+    def op(e, call, out, ins):
+        reads, writes = [], list(out[1])
+        if len(out) == 3:
+            reads += out[2]
+        for x in ins:
+            if isinstance(x, tuple):
+                reads += x[1]
+                if len(x) == 3:
+                    reads += x[2]
+        order(e, reads, writes)
+        s = ESEM[e]
+        cnt[s] += 1
+        call().then_inc(T.sem[s], 1)
+        note(e, reads, writes, (s, cnt[s]))
+
+    def ap(x):
+        return x[0] if isinstance(x, tuple) else x
+
+    def mset(o, c):
+        op("v", lambda: g.vector.memset(o[0], c), o, [])
+
+    def cp(o, i):
+        op("v", lambda: g.vector.tensor_copy(o[0], i[0]), o, [i])
+
+    def tt(o, a, b, f):
+        op("v", lambda: g.vector.tensor_tensor(o[0], a[0], b[0], f), o, [a, b])
+
+    def ts(o, a, s1, f0, s2=None, f1=None):
+        if f1 is None:
+            op("v", lambda: g.vector.tensor_scalar(o[0], a[0], ap(s1), None, f0), o, [a, s1])
+        else:
+            op("v", lambda: g.vector.tensor_scalar(o[0], a[0], ap(s1), ap(s2), f0, f1), o, [a, s1, s2])
+
+    def scan(o, d0, d1, f0, f1):
+        op("v", lambda: g.vector.tensor_tensor_scan(o[0], d0[0], d1[0], 0.0, f0, f1), o, [d0, d1])
+
+    def act(o, i, fn, bias=0.0, scale=1.0):
+        op("s", lambda: g.scalar.activation(o[0], i[0], fn, bias=bias, scale=ap(scale)), o, [i, scale])
+
+    def mm(o, l, r, start=True, stop=True):
+        op("p", lambda: g.tensor.matmul(o[0], l[0], r[0], start, stop), o, [l, r])
+
+    def iota(o, pat, base, cm, fl=False):
+        if fl:
+            op("g", lambda: g.iota(o[0], pat, base, cm, allow_small_or_imprecise_dtypes=True), o, [])
+        else:
+            op("g", lambda: g.iota(o[0], pat, base, cm), o, [])
+
+    def sel(o, i, pat, cmpop, base, cm, fill=0.0):
+        op("g", lambda: g.affine_select(o[0], i[0], pat, cmpop, fill, base, cm), o, [i])
+
+    def dma(e, o, i, reads, writes):
+        s = "d%d" % ndma[0]
+        ndma[0] += 1
+        order(e, reads, writes)
+        Q[e].dma_start(o, i).then_inc(T.sem[s], 16)
+        note(e, reads, writes, (s, 16))
+        return (s, 16)
+
+    def lanes(d, part, of):
+        en = topo.engines(core, T.cores[(rank + d) % N])
+        n = len(en) // of
+        m = 0
+        for x in en[part * n:(part + 1) * n]:
+            m |= 1 << x
+        return m, n
+
+    def send(items):
+        order("g", [r for it in items for r in it[1][1]], [])
+        if len(items) == 1:
+            d, src, dst, s = items[0]
+            rid, pid, _ = topo.addr(T.cores[(rank + d) % N])
+            m, n = lanes(d, 0, 1)
+            g.remote_dma(dst[0], src[0], T.sem[s], T.sem.sent, pid, rid, m)
+            sent[0] += n
+            return
+        trs = []
+        for j, (d, src, dst, s) in enumerate(items):
+            rid, pid, _ = topo.addr(T.cores[(rank + d) % N])
+            m, n = lanes(d, j, len(items))
+            trs.append(RemoteDMATransfer(dst_ids=[DstId(rid=rid, pnc=pid)], dma_engine_mask=m,
+                                         remote_sem=T.sem[s], src=src[0], dst=dst[0]))
+            sent[0] += n
+        g.remote_dma_fused(trs, local_sem=T.sem.sent)
+
+    arrivals = []
+
+    def arrive(dst, s, d, of):
+        src = T.cores[(rank - d) % N]
+        n = len(topo.engines(src, core)) // of
+        note("r" + s, [], dst[1], (s, n))
+        arrivals.append((s, n))
+
+    def beta(t):
+        return R("PW", 256 * t + 128, 256 * t + 256)
+
+    Wn = {1: "Wn1", 2: "Wn2"}
+    RO = {1: "RO1", 2: "RO2"}
+    XD = {0: "XD0", 1: "XD1"}
+    arrive(beta(0), "b0", STEP[0], 1)
+    for t in range(3):
+        arrive(R("RA", 256 * t, 256 * t + 256), "ma%d" % t, STEP[t], 1)
+        arrive(R("RG", 128 * t, 128 * t + 128), "mg%d" % t, -STEP[t], 1)
+    for t in range(2):
+        arrive(R(XD[t], 128, 384), "mb%d" % t, STEP[t], 2)
+        arrive(R(Wn[t + 1], 128, 384), "mw%d" % t, STEP[t + 1], 2)
+        arrive(R(Wn[t + 1], 0, 128), "mn%d" % t, STEP[t + 1] - STEP[t], 2)
+        arrive(R(RO[t + 1]), "mo%d" % t, STEP[t + 1], 2)
+
+    def src_list(t, wide=False):
+        lo = 24 * t + 8
+        return R("SL", lo, lo + (16 if wide else 8))
+
+    dma("s", T.trk[:], T.trucks[:], [], [("trk", 0, 24)])
+    for (lo, hi) in CH:
+        dma("y", T.Y[:, lo:hi], T.days[:, lo:hi], [], [("Y", lo, hi)])
+    dma("y", T.cnd[:], T.cand[:], [], [("cnd", 0, 768)])
+
+    mset(R("ones"), 1.0)
+    mset(R("Q0"), -97.0)
+    iota(R("ic", 0, 1), [[0, 1]], 0, 1)
+    sel(R("I"), R("ones"), [[-1, 128]], A.is_equal, 0, 1)
+    iota(R("ia"), [[1, 128]], 128, -1)
+    iota(R("nL"), [[16, 8]], 0, 0, True)
+    sel(R("Bo0"), R("ones"), [[-16, 8], [0, 16]], A.is_ge, 0, 1)
+    iota(R("idd"), [[0, 2], [1, 8]], 0, 0)
+    sel(R("Bo"), R("Bo0"), [[16, 8], [0, 16]], A.is_ge, 15, -1)
+    act(R("nI"), R("I"), F.Identity, scale=-1.0)
+    act(R("nBo"), R("Bo"), F.Identity, scale=-1.0)
+    iota(R("jv"), [[0, 2], [1, 128]], 0, 0, True)
+    sel(R("nUp"), R("nBo"), [[-1, 128]], A.is_equal, -1, 1)
+    sel(R("Up2"), R("Bo"), [[-1, 128]], A.is_equal, -2, 1)
+    sel(R("TopM"), R("nUp"), [[-1, 128]], A.not_equal, 0, 1, 1.0)
+    sel(R("turn"), R("ones"), [[-1, 16], [-16, 8]], A.is_equal, 0, 1)
+    sel(R("dfa"), R("ones", 0, 99), [[-32, 3], [-1, 33]], A.is_equal, 1, 1)
+    sel(R("dfb"), R("ones", 0, 99), [[-32, 3], [-1, 33]], A.is_equal, 0, 1)
+    sel(R("Q1"), R("Q0"), [[0, 32], [-16, 8]], A.is_ge, 0, 1)
+    sel(R("nDn"), R("nBo"), [[-1, 128]], A.is_equal, 1, 1)
+    sel(R("Q97"), R("Q1"), [[0, 32], [16, 8]], A.is_ge, 15, -1)
+    sel(R("FstE"), R("nDn"), [[-1, 128]], A.not_equal, 0, 1, 1.0)
+    iota(R("rowj"), [[1, 256]], 0, 0, True)
+
+    mset(R("dif", 0, 99, 1, 128, 96), -16.0)
+    mset(R("rst"), 1.0)
+    ts(R("ic", 2, 3), R("ic", 0, 1), 15, A.bitwise_and)
+    mset(R("dif", 0, 99, 33, 128, 96), 32800.0)
+    mset(R("JT"), 256.0)
+    cp(R("cols", 0, 1), R("ic", 2, 3))
+    mset(R("dif", KV, 99, 33, 128, 96), -15888.0)
+    mset(R("c97"), 24832.0)
+    ts(R("cols", 3, 4), R("cols", 0, 1), 15.0, A.is_equal, 15.0, A.mult)
+    mset(R("dif", 32, 99, 33, 128, 96), 16368.0)
+    ts(R("cols", 1, 2), R("cols", 0, 1), 15.0, A.is_lt)
+    ts(R("cols", 2, 3), R("cols", 0, 1), 0.0, A.is_equal)
+    ts(R("cols", 6, 7), R("cols", 0, 1), 0.0, A.is_equal, -97.0, A.mult)
+    ts(R("cols", 7, 8), R("cols", 0, 1), 0.0, A.is_equal, float(1 << 23), A.mult)
+    ts(R("cols", 4, 5), R("cols", 3, 4), 1.0, A.add, float(UNIT), A.mult)
+    ts(R("cols", 5, 6), R("cols", 3, 4), 1.0, A.add, float(UNIT // 2), A.mult)
+    ts(R("ib"), R("ia"), 15, A.bitwise_and)
+    mset(R("rst", 0, 256, 16), 0.0)
+    mset(R("Z", V, V + S), 0.0)
+    mset(R("Y", V, V + S), 0.0)
+    ts(R("mask"), R("ib"), 0.0, A.is_equal)
+    ts(R("nL"), R("nL"), R("cols", 0, 1), A.add)
+    cp(R("I16"), R("I"))
+    cp(R("trf"), R("trk"))
+    cp(R("SL", 8, 24), R("trk", 0, 16))
+    cp(R("SL", 40, 48), R("trk", 16, 24))
+    grp = R("Bo", 0, 128, 16)
+    act(R("Bq"), R("Bo"), F.Identity, scale=-1.0 / 256)
+    act(R("I15"), R("I"), F.Identity, scale=R("cols", 1, 2))
+    act(R("I256"), R("I"), F.Identity, scale=256.0)
+    act(R("E0"), R("Bo"), F.Identity, scale=R("cols", 2, 3))
+    act(R("Wv"), grp, F.Identity, scale=R("cols", 4, 5))
+    act(R("Ws"), grp, F.Identity, scale=R("cols", 5, 6))
+    act(R("W97"), grp, F.Identity, scale=R("cols", 6, 7))
+    act(R("W23"), grp, F.Identity, scale=R("cols", 7, 8))
+
+    def mirror(c):
+        lo = 512 * c
+        bk = "B%d" % (4 + c % 3)
+        mm(R(bk), R("I"), R("t256", lo, lo + 512), True, False)
+        mm(R(bk), R("nI"), R("Y", lo, lo + 512), False, True)
+        act(R("Z", lo, lo + 512), R(bk), F.Identity)
+
+    def marks(j):
+        lo, hi = CH[j]
+        ts(R("t256", lo, hi), R("Y", lo, hi), 256.0, A.mult, 256.0, A.min)
+
+    ts(R("jtmp", 0, 8), R("trf", 0, 8), float(W), A.is_ge)
+    ts(R("jtmp", 8, 16), R("trf", 0, 8), float(W - S), A.subtract)
+    ts(R("jo", 8, 16), R("trf", 8, 16), float(W - S - 640), A.subtract)
+    tt(R("jtmp", 16, 24), R("jtmp", 8, 16), R("nL"), A.subtract)
+    ts(R("jo", 16, 24), R("trf", 8, 16), float(W - S), A.subtract)
+    tt(R("jtmp", 24, 32), R("jtmp", 16, 24), R("jtmp", 0, 8), A.mult)
+    ts(R("jo", 24, 32), R("trf", 16, 24), float(W - S - 640), A.subtract)
+    tt(R("jtmp", 8, 16), R("jtmp", 24, 32), R("nL"), A.add)
+    cp(R("m2", 0, 128), R("mask"))
+    cp(R("jo", 0, 8), R("jtmp", 8, 16))
+    cp(R("m2", 128, 256), R("mask"))
+    marks(0)
+    mirror(0)
+    mirror(1)
+    cp(IND(R("JT"), R("jo", 0, 16)), R("jv"))
+    marks(1)
+    mirror(2)
+    mirror(3)
+    tt(R("jm"), IND(R("JT"), R("jo", 16, 32)), R("m2"), A.mult)
+    ts(R("n128", 0, 8), R("nL"), 128.0, A.add)
+    ts(R("n128", 8, 16), R("nL"), 128.0, A.add)
+    marks(2)
+    mirror(4)
+    mirror(5)
+    mset(R("X16", 0, 1024, 1, 128, 96), 8.0)
+    mset(R("ones16"), 1.0)
+    mset(R("nil16"), 0.0)
+    marks(3)
+    mirror(6)
+
+    Yw, Zw = R("Y", 0, V), R("Z", 0, V)
+    ts(R("ra"), IND(Yw, src_list(0)), 256.0, A.mult, 256.0, A.min)
+    mm(R("B7", 0, 128), R("TopM"), R("ra"))
+    tt(R("rb"), IND(Yw, src_list(0)), R("ra"), A.subtract)
+    tt(R("rc"), R("B7", 0, 128), R("rb"), A.mult)
+    mm(R("B7", 128, 256), R("Bq"), R("rc"))
+    marks(4)
+    cp(R("p0"), R("B7", 128, 256))
+    send([(STEP[0], R("p0"), beta(0), "b0")])
+    mirror(7)
+    mirror(8)
+
+    def step1_a(t):
+        w = 256 if t < 2 else 128
+        act(R("zz", 0, w), IND(Zw, src_list(t, t < 2)), F.Identity)
+        act(R("tt", 0, w), R("zz", 0, w), F.Sign)
+        mm(R("B5", 0, w), R("TopM"), R("tt", 0, w))
+        if t < 2:
+            mm(R("B5", 256, 384), R("nUp"), R("tt", 0, 128), True, False)
+            mm(R("B5", 256, 384), R("Up2"), R("tt", 0, 128), False, True)
+
+    def step1_b(t):
+        w = 256 if t < 2 else 128
+        tt(R("pr", 0, w), R("B5", 0, w), R("zz", 0, w), A.mult)
+        mm(R("B7", 0, 128), R("I"), R("zz", 0, 128), True, False)
+        mm(R("B7", 0, 128), R("nBo"), R("pr", 0, 128), False, True)
+        if t < 2:
+            tt(R("pr", 256, 384), R("B5", 256, 384), R("zz", 0, 128), A.mult)
+
+    def step1_c(t):
+        act(R("rl"), R("B7", 0, 128), F.Relu)
+        mm(R("B7", 128, 256), R("E0"), R("ones"), True, False)
+        mm(R("B7", 128, 256), R("nBo"), R("rl"), False, True)
+        mm(R("B7", 256, 384), R("E0"), R("tt", 0, 128), True, False)
+        mm(R("B7", 256, 384), R("nBo"), R("rl"), False, True)
+        if t < 2:
+            mm(R("B6", 384, 512), R("nBo"), R("pr", 256, 384), True, False)
+            mm(R("B6", 384, 512), R("nBo"), R("pr", 0, 128), False, True)
+            mm(R("B5", 0, 128), R("Bo"), R("pr", 128, 256))
+
+    def step1_d(t):
+        pa = R("PA", 256 * t, 256 * t + 256)
+        act(pa, R("B7", 128, 384), F.Relu)
+        send([(STEP[t], pa, R("RA", 256 * t, 256 * t + 256), "ma%d" % t)])
+        if t < 2:
+            act(R("PW", 256 * t, 256 * t + 128), R("B5", 0, 128), F.Identity)
+
+    def step1_e(t):
+        tt(R("PB", 256 * t, 256 * t + 128), R("B6", 384, 512), R("mask"), A.mult)
+        tt(R("PB", 256 * t + 128, 256 * t + 256), R("B6", 384, 512), R("PA", 256 * t + 128, 256 * t + 256), A.mult)
+        send([(STEP[t], R("PB", 256 * t, 256 * t + 256), R(XD[t], 128, 384), "mb%d" % t),
+              (STEP[t + 1], R("PW", 256 * t, 256 * t + 256), R(Wn[t + 1], 128, 384), "mw%d" % t)])
+
+    def step1_ge():
+        mm(R("B7", 384, 512), R("nUp"), R("tt", 0, 128))
+        act(R("geN"), R("B7", 384, 512), F.Identity, bias=-1.0, scale=-1.0)
+
+    def key_steps(t, bank):
+        for gg in range(8):
+            mm(R(bank, 33 * gg, 33 * gg + 33), R("X16", gg, 1024, 8), R("dif", 33 * t, 33 * t + 33))
+        act(R("kp", 264 * t, 264 * t + 264), R(bank, 0, 264), F.Identity)
+
+    cp(R("pm16"), R("turn"))
+    ts(R("P16"), R("cnd"), 2048.0, A.subtract)
+    for q in range(8):
+        c0 = (q % 4) * 128
+        mm(R("B%d" % (1 + q // 4), c0, c0 + 128, 1, 96), R("P16", q, 768, 8), R("pm16"))
+    step1_a(0)
+    tt(R("dif", 0, 99, 1, 96), R("dfa", 0, 99, 1, 96), R("dfb", 0, 99, 1, 96), A.subtract)
+    cp(R("ex"), R("idd"))
+    cp(R("dif", 32, 99, 33, 96), R("dfa", 32, 99, 33, 96))
+    cp(R("X16", 0, 512, 1, 96), R("B1", 0, 512, 1, 96))
+    cp(R("X16", 512, 1024, 1, 96), R("B2", 0, 512, 1, 96))
+    step1_b(0)
+    step1_c(0)
+    key_steps(0, "B1")
+    ts(R("ngr"), grp, -1.0, A.mult)
+    ts(R("tri"), R("rowj", 0, 16), R("cols", 0, 1), A.is_ge, 32768.0, A.mult)
+    cp(R("Q16", 0, 8), grp)
+    mset(R("B0", 32, 264, 33), float(3 << 22))
+    mset(R("tri", 15, 16), 6144.0)
+    cp(R("Q16", 8, 16), grp)
+    mset(R("c26"), 26880.0)
+    mset(R("lrow", 128, 144), 0.0)
+    mset(R("PO"), 0)
+
+    def clash_constants():
+        for q in range(8):
+            ts(R("RB", TOFF[q], TOFF[q] + SEG[q]), R("ones16", 0, SEG[q]), R("ngr", q, q + 1), A.mult)
+
+    def landing_constants():
+        cp(R("XD0", 0, 128), R("mask"))
+        scan(R("js"), R("rst"), R("jm"), A.mult, A.add)
+        ts(R("n256"), R("nL"), 256.0, A.add)
+        tt(R("base"), R("js", 15, 256, 16), R("n128"), A.min)
+
+    def list_constants():
+        cp(R("XD1", 0, 128), R("mask"))
+        ts(R("b16", 16, 24), R("nL"), float(V), A.add)
+        cp(R("b16", 24, 32), R("trf", 16, 24))
+        ts(R("b16", 32, 40), R("nL"), float(V), A.add)
+
+    def relink_constants():
+        tt(R("jg"), R("rowj", 128, 256), R("mask"), A.mult)
+        ts(R("jx1"), R("base", 8, 16), 128.0, A.min)
+        tt(R("md1"), R("jg"), R("jm", 128, 256), A.subtract)
+
+    def relink():
+        scan(R("js", 0, 128), R("rst", 0, 128), R("jm", 0, 128), A.mult, A.add)
+        tt(R("base", 8, 16), R("base", 8, 16), R("js", 15, 128, 16), A.add)
+
+    def as_days(o, z, tmark, bank, lo):
+        mm(R(bank, lo, lo + 128), R("I256"), tmark, True, False)
+        mm(R(bank, lo, lo + 128), R("nI"), z, False, True)
+        act(o, R(bank, lo, lo + 128), F.Identity)
+
+    Yall, Zall = R("Y"), R("Z")
+
+    def put_days(t, buf, half):
+        lo = 24 * t + 8 + 4 * half
+        cp(IND(Yall, R("SL", lo, lo + 4)), R(buf, 64 * half, 64 * half + 64))
+
+    for t in range(3):
+        last = t == 2
+        bt = beta(t)
+        mm(R("B3", 128, 384), R("I"), R("c97"), True, False)
+        if t > 0:
+            act(bt, IND(R(Wn[t]), R(RO[t], 0, 8)), F.Identity)
+            tt(R("uu"), R("RG", 128 * (t - 1), 128 * t), R("dl"), A.mult)
+        else:
+            step1_d(0)
+        mm(R("B6", 0, 128), bt, R("I"))
+        for j in range(4):
+            mm(R("B4", 128 * j, 128 * j + 128), R("I15"), bt)
+        tt(R("xm"), R("B6", 0, 128), R("mask"), A.mult)
+        mm(R("B3", 128, 384), R("xm"), R("Q97"), False, True)
+        if t > 0:
+            tt(IND(Zall, src_list(t - 1)), R("zp"), R("uu"), A.add)
+        else:
+            step1_e(0)
+        act(R("thr"), R("B4"), F.Identity)
+        halves = [(0, 128), (128, 256)]
+        for (lo, hi) in halves:
+            tt(R("ci", lo, hi), R("B3", 128 + lo, 128 + hi), R("cnd", 256 * t + lo, 256 * t + hi), A.add)
+        if t > 0:
+            step1_a(t)
+        for (lo, hi) in halves:
+            ts(R("cj", lo, hi), R("ci", lo, hi), W - 1, A.bitwise_and)
+        for (lo, hi) in halves:
+            cp(R("cu", lo, hi), R("cj", lo, hi))
+        Zc = R("Z", 0, W)
+
+        def vchunk(c):
+            k0, k1 = VCH[c]
+            tt(R("cmp", 128 * k0, 128 * k1), IND(Zc, R("cu", 8 * k0, 8 * k1)), R("thr", 0, 128 * (k1 - k0)), A.is_gt)
+
+        def score(ks, wts):
+            for k in range(ks[0], ks[1]):
+                mm(R("B0", k, 264, 33), R("cmp", 128 * k, 128 * k + 128), R(wts))
+
+        def sgather(j):
+            k0, k1 = SCH[j]
+            n = 128 * (k1 - k0)
+            bk = R("B%d" % (1 + j % 2), 0, n)
+            act(R("raw", 512 * j, 512 * j + n), IND(Zc, R("cu", 8 * k0, 8 * k1)), F.Identity)
+            mm(bk, R("nI"), R("thr", 0, n), True, False)
+            mm(bk, R("I"), R("raw", 512 * j, 512 * j + n), False, True)
+
+        def ssign(j):
+            k0, k1 = SCH[j]
+            act(R("cmp", 128 * k0, 128 * k1), R("B%d" % (1 + j % 2), 0, 128 * (k1 - k0)), F.Sign, bias=-0.5)
+
+        vchunk(0)
+        if t > 0:
+            step1_b(t)
+        sgather(0)
+        if t > 0:
+            step1_c(t)
+        score(VCH[0], "Wv")
+        vchunk(1)
+        if t == 0:
+            sgather(1)
+        ssign(0)
+        if t > 0:
+            step1_d(t)
+        score(VCH[1], "Wv")
+        vchunk(2)
+        if t > 0:
+            sgather(1)
+        score(SCH[0], "Ws")
+        if t == 1:
+            step1_e(1)
+        score(VCH[2], "Wv")
+        vchunk(3)
+        sgather(2)
+        ssign(1)
+        score(VCH[3], "Wv")
+        vchunk(4)
+        mm(R("B3", 384, 392), R("I"), R("c26"), True, False)
+        mm(R("B3", 384, 392), bt, R("W97"), False, False)
+        mm(R("B3", 384, 392), R("RA", 256 * t, 256 * t + 128), R("W23"), False, True)
+        score(SCH[1], "Ws")
+        ssign(2)
+        score(VCH[4], "Wv")
+        vchunk(5)
+        score(SCH[2], "Ws")
+        score(VCH[5], "Wv")
+        if t == 0:
+            clash_constants()
+        if t == 1:
+            tt(R("jm", 0, 128), IND(R("lrow"), R("jx1")), R("md1"), A.mult)
+        if last:
+            as_days(R("rd"), R("zz", 0, 128), R("tt", 0, 128), "B6", 256)
+        scan(R("sc"), R("kp", 264 * t, 264 * t + 264), R("B0", 0, 264), A.add, A.min)
+        if t > 0:
+            act(R("ra"), IND(Zw, src_list(t - 1)), F.Identity)
+            act(R("rb"), R("ra"), F.Sign)
+        mm(R("B1", 0, 240), R("I16"), R("nil16", 0, 240), True, False)
+        mm(R("B2", 0, 336), R("I16"), R("nil16", 0, 336), True, False)
+        for q in range(8):
+            bk, c0 = SOFF[q]
+            mm(R("B%d" % bk, c0 + SEG[q] - 16, c0 + SEG[q]), R("I16"), R("tri"), False, False)
+        tt(R("ki"), R("B3", 384, 392), R("sc", 32, 264, 33), A.add)
+        ts(R("km"), R("ki"), (3 << 22) | (W - 1), A.bitwise_and)
+        ts(R("A16"), IND(R("km"), R("ex", 0, 8)), 8192.0, A.min, 2048.0, A.subtract)
+        tt(R("B16"), R("A16"), R("mask"), A.mult)
+        for q in range(8):
+            bk, c0 = SOFF[q]
+            mm(R("B%d" % bk, c0, c0 + SEG[q] - 1), R("A16"), R("I16", 0, SEG[q] - 1), False, False)
+        mm(R("B1", 0, 240), R("B16"), R("RB", 0, 240), False, True)
+        mm(R("B2", 0, 336), R("B16"), R("RB", 240, 576), False, True)
+        mm(R("B3", 392, 408), R("B16"), R("Q16"))
+        mm(R("B4", 0, 128), R("I"), R("RA", 256 * t + 128, 256 * t + 256), True, False)
+        if not last:
+            mm(R("B5", 0, 128), R("I"), bt, True, False)
+            mm(R("B5", 0, 128), R("I"), R(XD[t], 256, 384), False, False)
+        if t > 0:
+            as_days(R("rc"), R("ra"), R("rb"), "B6", 128)
+        step1_ge()
+        if t == 0:
+            landing_constants()
+        if t == 1:
+            relink()
+        if last:
+            put_days(2, "rd", 0)
+            act(R("braw"), bt, F.Identity, bias=256.0, scale=-1.0)
+        for q in range(8):
+            bk, c0 = SOFF[q]
+            o, i = R("mn", q, q + 1), R("B%d" % bk, c0, c0 + SEG[q])
+            op("v", lambda: g.vector.tensor_reduce(o[0], i[0], AxisListType.X, A.min, apply_absolute_value=True), o, [i])
+        ts(R("dU"), R("B3", 392, 400), 2048.0, A.add, float(W - 1), A.min)
+        ts(R("land", 0, 8), R("mn"), 0.0, A.is_gt)
+        act(R("zd"), IND(Zc, R("dU")), F.Identity)
+        act(R("ed"), R("zd"), F.Relu, bias=1.0, scale=-1.0)
+        if last:
+            tt(R("Rm", 0, 128), IND(R("land", 0, 8), R("ex", 0, 8)), R("mask"), A.mult)
+        else:
+            tt(R("doff", 0, 8), R("n256"), R("base", 8 * t, 8 * t + 8), A.subtract)
+            tt(R("Rm"), IND(R("land", 0, 8), R("ex")), R(XD[t], 0, 256), A.mult)
+            mm(R("B5", 0, 128), R("Bo"), R("Rm", 128, 256), False, True)
+        mm(R("B4", 0, 128), R("Bo"), R("Rm", 0, 128), False, True)
+        pg = R("PG", 128 * t, 128 * t + 128)
+        act(pg, R("B4", 0, 128), F.Identity)
+        if not last:
+            tt(R("oa"), R("land", 0, 8), R("doff", 0, 8), A.mult)
+            ts(R("ta"), R("B3", 392, 408), 2048.0, A.add)
+            tt(R("ob"), R("oa"), R("base", 8 * t, 8 * t + 8), A.add)
+            pn = R("PN", 128 * t, 128 * t + 128)
+            cp(pn, R("B5", 0, 128))
+            cp(R("PO", 128 * t, 128 * t + 8), R("ob"))
+            send([(STEP[t + 1] - STEP[t], pn, R(Wn[t + 1], 0, 128), "mn%d" % t),
+                  (STEP[t + 1], R("PO", 128 * t, 128 * t + 128), R(RO[t + 1]), "mo%d" % t)])
+        send([(-STEP[t], pg, R("RG", 128 * t, 128 * t + 128), "mg%d" % t)])
+        mm(R("B6", 0, 128), R("FstE"), R("ed"))
+        if last:
+            act(R("td"), R("zd"), F.Sign)
+            as_days(R("yd"), R("zd"), R("td"), "B7", 0)
+        if t == 0:
+            mm(R("B7", 0, 128), R("Bo"), R("Rm", 0, 128))
+            act(R("lrow", 0, 128), R("B7", 0, 128), F.Identity)
+            ts(R("b16", 0, 8), R("nL"), float(V), A.add)
+            cp(R("b16", 8, 16), R("trf", 8, 16))
+        if not last:
+            key_steps(t + 1, "B1")
+        w = 8 if last else 16
+        bs = R("b16", 16 * t, 16 * t + w)
+        if last:
+            ts(R("ta", 0, w), R("B3", 392, 392 + w), 2048.0, A.add)
+            put_days(2, "rd", 1)
+        else:
+            ts(R("land", 8, 16), R("mn"), 0.0, A.is_gt)
+        tt(R("tb", 0, w), R("ta", 0, w), bs, A.subtract)
+        if last:
+            put_days(1, "rc", 0)
+        tt(R("tc", 0, w), R("tb", 0, w), R("land", 0, w), A.mult)
+        if last:
+            put_days(1, "rc", 1)
+        tt(R("ta", 0, w), R("tc", 0, w), bs, A.add)
+        tt(R("fd"), R("B6", 0, 128), R("braw") if last else bt, A.mult)
+        lo = 0 if last else 24 * (t + 1)
+        cp(R("SL", lo, lo + w), R("ta", 0, w))
+        St, Sw = (Yall, Yw) if last else (Zall, Zw)
+        tt(IND(St, R("SL", lo, lo + 8)), R("yd") if last else R("zd"), R("fd"), A.add)
+        cp(R("zp"), IND(Sw, src_list(t)))
+        mm(R("B6", 128, 256), R("TopM"), R("zp"))
+        if t == 0:
+            list_constants()
+        if t == 1:
+            put_days(0, "rc", 0)
+        tt(R("dl"), R("B6", 128, 256), R("geN"), A.mult)
+        if t == 0:
+            relink_constants()
+        if t == 1:
+            put_days(0, "rc", 1)
+
+    tt(R("uu"), R("RG", 256, 384), R("dl"), A.mult)
+    tt(IND(Yall, src_list(2)), R("zp"), R("uu"), A.add)
+    tok = dma("y", T.y[:], T.Y[:, 0:V], [("Y", 0, V)], [])
+    need("y", [tok])
+    need("g", arrivals + [(s, c) for s, c in cnt.items()] + [("d%d" % i, 16) for i in range(ndma[0] - 1)] + [("sent", sent[0])])

@@ -3,14 +3,15 @@ from concourse.mybir import AluOpType as A, AxisListType, ActivationFunctionType
 
 N, W, V, S, K = 8, 4096, 4608, 128, 32
 STEP = (1, 2, 3)
-KV = 21
-VCH = [(0, 2), (2, 6), (6, 10), (10, 14), (14, 18), (18, 21)]
-SCH = [(21, 25), (25, 29), (29, 32)]
+KV = 20
+VCH = [(0, 2), (2, 6), (6, 10), (10, 14), (14, 18), (18, KV)]
+SCH = [(KV, KV + 4), (KV + 4, KV + 8), (KV + 8, K)]
 UNIT = 1 << 18
 SEG = [16 * (q + 1) for q in range(8)]
 SOFF = [(1, 0), (1, 16), (1, 48), (1, 96), (1, 160), (2, 0), (2, 96), (2, 208)]
 TOFF = [0, 16, 48, 96, 160, 240, 336, 448]
-CH = [(0, 1024), (1024, 2048), (2048, 3072), (3072, 4096), (4096, 4608)]
+LOADS = [(4096, 4608), (0, 2048), (2048, 3072), (3072, 4096)]
+CH = [(4096, 4608), (0, 1024), (1024, 2048), (2048, 3072), (3072, 4096)]
 
 bf, f32, i32, u16, f16 = "bfloat16", "float32", "int32", "uint16", "float16"
 SCRATCH = {}
@@ -22,10 +23,10 @@ for _n, _w, _d in [
     ("TopM", 128, bf), ("FstE", 128, bf), ("E0", 128, bf), ("mask", 128, bf), ("rst", 256, bf), ("c26", 8, bf),
     ("c97", 256, bf), ("Q0", 256, bf), ("Q1", 256, bf), ("Q97", 256, bf), ("turn", 128, bf), ("dfa", 99, bf),
     ("dfb", 99, bf), ("I16", 128, f16), ("ones16", 128, f16), ("Q16", 16, f16), ("pm16", 128, f16),
-    ("RB", 576, f16), ("nil16", 336, f16), ("tri", 16, f16), ("dif", 99, f16), ("P16", 768, f16), ("X16", 1024, f16),
-    ("Wv", 8, bf), ("Ws", 8, bf), ("W97", 8, bf), ("W23", 8, bf),
-    ("ia", 128, i32), ("ib", 128, i32), ("ic", 16, i32), ("idd", 16, i32), ("ex", 16, u16), ("rowj", 256, bf),
-    ("kp", 792, f32), ("JT", 1280, bf), ("jo", 32, u16),
+    ("RB", 576, f16), ("nil16", 336, f16), ("tri", 16, f16), ("dif", 99, f16), ("dcn", 264, f16), ("eight", 128, f16),
+    ("P16", 768, f16), ("X16", 1024, f16), ("Wv", 8, bf), ("Ws", 8, bf), ("W97", 8, bf), ("W23", 8, bf),
+    ("ia", 128, i32), ("ib", 128, i32), ("ic", 16, i32), ("idd", 16, i32), ("ex", 16, u16), ("rowj", 128, bf),
+    ("kp", 792, f32), ("JT", 1280, bf), ("jo", 32, u16), ("ro", 8, u16),
     ("jg", 128, bf), ("jm", 256, bf), ("js", 256, bf), ("jv", 256, bf), ("m2", 256, bf),
     ("md1", 128, bf), ("jx1", 8, u16), ("SL", 72, u16), ("dU", 8, u16),
     ("PW", 768, bf), ("Wn1", 384, bf), ("Wn2", 384, bf), ("XD0", 384, bf), ("XD1", 384, bf), ("PA", 768, bf),
@@ -51,7 +52,7 @@ for _b in range(8):
     SCRATCH["B%d" % _b] = ("psum", [128, 512], f32)
     WHERE["B%d" % _b] = ("B%d" % _b, 0, 512)
 
-ARR = ["b0", "ma0", "ma1", "ma2", "mb0", "mb1", "mw0", "mw1", "mo0", "mo1", "mg0", "mg1", "mg2", "mn0", "mn1"]
+ARR = ["b0", "me", "ma0", "ma1", "ma2", "mb0", "mb1", "mw0", "mw1", "mo0", "mo1", "mg0", "mg1", "mg2", "mn0", "mn1"]
 SEMAPHORES = ["ev", "es", "ep", "eg", "sent"] + ["d%d" % _i for _i in range(10)] + ARR
 
 
@@ -68,10 +69,10 @@ def rank_program(g, core, T, topo):
     sent = [0]
     ndma = [0]
 
-    def R(name, lo=0, hi=None, step=1, parts=128, p0=0):
+    def R(name, lo=0, hi=None, step=1, parts=128):
         buf, c0, w = WHERE[name]
         lo, hi = c0 + lo, c0 + (w if hi is None else hi)
-        ap = T[buf][p0:parts, lo:hi] if step == 1 else T[buf][p0:parts, lo:hi:step]
+        ap = T[buf][0:parts, lo:hi] if step == 1 else T[buf][0:parts, lo:hi:step]
         return (ap, [(buf, lo, hi)])
 
     def IND(win, off):
@@ -216,9 +217,12 @@ def rank_program(g, core, T, topo):
     for t in range(3):
         arrive(R("RA", 256 * t, 256 * t + 256), "ma%d" % t, STEP[t], 1)
         arrive(R("RG", 128 * t, 128 * t + 128), "mg%d" % t, -STEP[t], 1)
+    arrive(R("Wn1", 128, 256), "me", STEP[1], 1)
+    arrive(R("Wn1", 256, 384), "mw0", STEP[1], 1)
+    arrive(R("XD0", 128, 384), "mb0", STEP[0], 1)
+    arrive(R("Wn2", 128, 384), "mw1", STEP[2], 2)
+    arrive(R("XD1", 128, 384), "mb1", STEP[1], 2)
     for t in range(2):
-        arrive(R(XD[t], 128, 384), "mb%d" % t, STEP[t], 2)
-        arrive(R(Wn[t + 1], 128, 384), "mw%d" % t, STEP[t + 1], 2)
         arrive(R(Wn[t + 1], 0, 128), "mn%d" % t, STEP[t + 1] - STEP[t], 2)
         arrive(R(RO[t + 1]), "mo%d" % t, STEP[t + 1], 2)
 
@@ -227,59 +231,56 @@ def rank_program(g, core, T, topo):
         return R("SL", lo, lo + (16 if wide else 8))
 
     dma("s", T.trk[:], T.trucks[:], [], [("trk", 0, 24)])
-    for (lo, hi) in CH:
+    for (lo, hi) in LOADS:
         dma("y", T.Y[:, lo:hi], T.days[:, lo:hi], [], [("Y", lo, hi)])
     dma("y", T.cnd[:], T.cand[:], [], [("cnd", 0, 768)])
 
     mset(R("ones"), 1.0)
-    mset(R("Q0"), -97.0)
     iota(R("ic", 0, 1), [[0, 1]], 0, 1)
     sel(R("I"), R("ones"), [[-1, 128]], A.is_equal, 0, 1)
-    iota(R("ia"), [[1, 128]], 128, -1)
-    iota(R("nL"), [[16, 8]], 0, 0, True)
     sel(R("Bo0"), R("ones"), [[-16, 8], [0, 16]], A.is_ge, 0, 1)
-    iota(R("idd"), [[0, 2], [1, 8]], 0, 0)
+    iota(R("nL"), [[16, 8]], 0, 0, True)
     sel(R("Bo"), R("Bo0"), [[16, 8], [0, 16]], A.is_ge, 15, -1)
+    iota(R("ia"), [[1, 128]], 128, -1)
     act(R("nI"), R("I"), F.Identity, scale=-1.0)
     act(R("nBo"), R("Bo"), F.Identity, scale=-1.0)
-    iota(R("jv"), [[0, 2], [1, 128]], 0, 0, True)
     sel(R("nUp"), R("nBo"), [[-1, 128]], A.is_equal, -1, 1)
-    sel(R("Up2"), R("Bo"), [[-1, 128]], A.is_equal, -2, 1)
+    iota(R("idd"), [[0, 2], [1, 8]], 0, 0)
     sel(R("TopM"), R("nUp"), [[-1, 128]], A.not_equal, 0, 1, 1.0)
-    sel(R("turn"), R("ones"), [[-1, 16], [-16, 8]], A.is_equal, 0, 1)
+    iota(R("jv"), [[0, 2], [1, 128]], 0, 0, True)
     sel(R("dfa"), R("ones", 0, 99), [[-32, 3], [-1, 33]], A.is_equal, 1, 1)
     sel(R("dfb"), R("ones", 0, 99), [[-32, 3], [-1, 33]], A.is_equal, 0, 1)
-    sel(R("Q1"), R("Q0"), [[0, 32], [-16, 8]], A.is_ge, 0, 1)
-    sel(R("nDn"), R("nBo"), [[-1, 128]], A.is_equal, 1, 1)
-    sel(R("Q97"), R("Q1"), [[0, 32], [16, 8]], A.is_ge, 15, -1)
-    sel(R("FstE"), R("nDn"), [[-1, 128]], A.not_equal, 0, 1, 1.0)
-    iota(R("rowj"), [[1, 256]], 0, 0, True)
+    sel(R("turn"), R("ones"), [[-1, 16], [-16, 8]], A.is_equal, 0, 1)
+    sel(R("Up2"), R("Bo"), [[-1, 128]], A.is_equal, -2, 1)
 
-    mset(R("dif", 0, 99, 1, 128, 96), -16.0)
+    mset(R("dcn", 0, 264, 1, 32), -16.0)
     mset(R("rst"), 1.0)
     ts(R("ic", 2, 3), R("ic", 0, 1), 15, A.bitwise_and)
-    mset(R("dif", 0, 99, 33, 128, 96), 32800.0)
+    mset(R("dcn", 0, 264, 33, 32), 32800.0)
     mset(R("JT"), 256.0)
     cp(R("cols", 0, 1), R("ic", 2, 3))
-    mset(R("dif", KV, 99, 33, 128, 96), -15888.0)
+    mset(R("dcn", KV, 264, 33, 32), -15888.0)
+    mset(R("eight", 0, 128, 1, 32), 8.0)
     mset(R("c97"), 24832.0)
     ts(R("cols", 3, 4), R("cols", 0, 1), 15.0, A.is_equal, 15.0, A.mult)
-    mset(R("dif", 32, 99, 33, 128, 96), 16368.0)
+    mset(R("dcn", 32, 264, 33, 32), 16368.0)
     ts(R("cols", 1, 2), R("cols", 0, 1), 15.0, A.is_lt)
     ts(R("cols", 2, 3), R("cols", 0, 1), 0.0, A.is_equal)
     ts(R("cols", 6, 7), R("cols", 0, 1), 0.0, A.is_equal, -97.0, A.mult)
     ts(R("cols", 7, 8), R("cols", 0, 1), 0.0, A.is_equal, float(1 << 23), A.mult)
     ts(R("cols", 4, 5), R("cols", 3, 4), 1.0, A.add, float(UNIT), A.mult)
     ts(R("cols", 5, 6), R("cols", 3, 4), 1.0, A.add, float(UNIT // 2), A.mult)
-    ts(R("ib"), R("ia"), 15, A.bitwise_and)
     mset(R("rst", 0, 256, 16), 0.0)
     mset(R("Z", V, V + S), 0.0)
     mset(R("Y", V, V + S), 0.0)
-    ts(R("mask"), R("ib"), 0.0, A.is_equal)
+    mset(R("Q0"), -97.0)
+    ts(R("ib"), R("ia"), 15, A.bitwise_and)
     ts(R("nL"), R("nL"), R("cols", 0, 1), A.add)
     cp(R("I16"), R("I"))
+    ts(R("mask"), R("ib"), 0.0, A.is_equal)
     cp(R("trf"), R("trk"))
-    cp(R("SL", 8, 24), R("trk", 0, 16))
+    ts(R("ro"), R("trk", 8, 16), float(W), A.subtract)
+    cp(R("SL", 8, 16), R("trk", 0, 8))
     cp(R("SL", 40, 48), R("trk", 16, 24))
     grp = R("Bo", 0, 128, 16)
     act(R("Bq"), R("Bo"), F.Identity, scale=-1.0 / 256)
@@ -293,7 +294,7 @@ def rank_program(g, core, T, topo):
 
     def mirror(c):
         lo = 512 * c
-        bk = "B%d" % (4 + c % 3)
+        bk = "B%d" % (4 + (c + 1) % 3)
         mm(R(bk), R("I"), R("t256", lo, lo + 512), True, False)
         mm(R(bk), R("nI"), R("Y", lo, lo + 512), False, True)
         act(R("Z", lo, lo + 512), R(bk), F.Identity)
@@ -301,6 +302,16 @@ def rank_program(g, core, T, topo):
     def marks(j):
         lo, hi = CH[j]
         ts(R("t256", lo, hi), R("Y", lo, hi), 256.0, A.mult, 256.0, A.min)
+
+    def clash_rows(q0, q1):
+        for q in range(q0, q1):
+            ts(R("RB", TOFF[q], TOFF[q] + SEG[q]), R("ones16", 0, SEG[q]), R("ngr", q, q + 1), A.mult)
+
+    marks(0)
+    mirror(8)
+    act(R("zd"), IND(R("Z", W, V), R("ro")), F.Identity)
+    act(R("td"), R("zd"), F.Sign)
+    mm(R("B3", 0, 128), R("TopM"), R("td"))
 
     ts(R("jtmp", 0, 8), R("trf", 0, 8), float(W), A.is_ge)
     ts(R("jtmp", 8, 16), R("trf", 0, 8), float(W - S), A.subtract)
@@ -310,43 +321,51 @@ def rank_program(g, core, T, topo):
     tt(R("jtmp", 24, 32), R("jtmp", 16, 24), R("jtmp", 0, 8), A.mult)
     ts(R("jo", 24, 32), R("trf", 16, 24), float(W - S - 640), A.subtract)
     tt(R("jtmp", 8, 16), R("jtmp", 24, 32), R("nL"), A.add)
-    cp(R("m2", 0, 128), R("mask"))
+    mset(R("ones16"), 1.0)
     cp(R("jo", 0, 8), R("jtmp", 8, 16))
+    ts(R("ngr"), grp, -1.0, A.mult)
+    cp(IND(R("JT"), R("jo", 0, 16)), R("jv"))
+    cp(R("m2", 0, 128), R("mask"))
     cp(R("m2", 128, 256), R("mask"))
-    marks(0)
+    clash_rows(0, 4)
+    tt(R("fd"), R("B3", 0, 128), R("zd"), A.mult)
+    mm(R("B3", 128, 256), R("Bo"), R("fd"))
+    act(R("PW", 0, 128), R("B3", 128, 256), F.Identity)
+    send([(STEP[1], R("PW", 0, 128), R("Wn1", 128, 256), "me")])
+    marks(1)
     mirror(0)
     mirror(1)
-    cp(IND(R("JT"), R("jo", 0, 16)), R("jv"))
-    marks(1)
-    mirror(2)
-    mirror(3)
-    tt(R("jm"), IND(R("JT"), R("jo", 16, 32)), R("m2"), A.mult)
-    ts(R("n128", 0, 8), R("nL"), 128.0, A.add)
-    ts(R("n128", 8, 16), R("nL"), 128.0, A.add)
     marks(2)
-    mirror(4)
-    mirror(5)
-    mset(R("X16", 0, 1024, 1, 128, 96), 8.0)
-    mset(R("ones16"), 1.0)
-    mset(R("nil16"), 0.0)
+    mirror(2)
     marks(3)
-    mirror(6)
+    clash_rows(4, 8)
 
     Yw, Zw = R("Y", 0, V), R("Z", 0, V)
     ts(R("ra"), IND(Yw, src_list(0)), 256.0, A.mult, 256.0, A.min)
     mm(R("B7", 0, 128), R("TopM"), R("ra"))
+    mirror(3)
     tt(R("rb"), IND(Yw, src_list(0)), R("ra"), A.subtract)
     tt(R("rc"), R("B7", 0, 128), R("rb"), A.mult)
     mm(R("B7", 128, 256), R("Bq"), R("rc"))
-    marks(4)
+    mirror(4)
+    mirror(5)
+    cp(R("pm16"), R("turn"))
+    mset(R("B0", 32, 264, 33), float(3 << 22))
+    mset(R("c26"), 26880.0)
     cp(R("p0"), R("B7", 128, 256))
     send([(STEP[0], R("p0"), beta(0), "b0")])
+    marks(4)
+    mirror(6)
     mirror(7)
-    mirror(8)
+    sel(R("Q1"), R("Q0"), [[0, 32], [-16, 8]], A.is_ge, 0, 1)
+    sel(R("Q97"), R("Q1"), [[0, 32], [16, 8]], A.is_ge, 15, -1)
+    sel(R("nDn"), R("nBo"), [[-1, 128]], A.is_equal, 1, 1)
+    iota(R("rowj"), [[1, 128]], 128, 0, True)
+    sel(R("FstE"), R("nDn"), [[-1, 128]], A.not_equal, 0, 1, 1.0)
 
     def step1_a(t):
-        w = 256 if t < 2 else 128
-        act(R("zz", 0, w), IND(Zw, src_list(t, t < 2)), F.Identity)
+        w = 256 if t == 1 else 128
+        act(R("zz", 0, w), IND(Zw, src_list(t, t == 1)), F.Identity)
         act(R("tt", 0, w), R("zz", 0, w), F.Sign)
         mm(R("B5", 0, w), R("TopM"), R("tt", 0, w))
         if t < 2:
@@ -354,7 +373,7 @@ def rank_program(g, core, T, topo):
             mm(R("B5", 256, 384), R("Up2"), R("tt", 0, 128), False, True)
 
     def step1_b(t):
-        w = 256 if t < 2 else 128
+        w = 256 if t == 1 else 128
         tt(R("pr", 0, w), R("B5", 0, w), R("zz", 0, w), A.mult)
         mm(R("B7", 0, 128), R("I"), R("zz", 0, 128), True, False)
         mm(R("B7", 0, 128), R("nBo"), R("pr", 0, 128), False, True)
@@ -370,78 +389,62 @@ def rank_program(g, core, T, topo):
         if t < 2:
             mm(R("B6", 384, 512), R("nBo"), R("pr", 256, 384), True, False)
             mm(R("B6", 384, 512), R("nBo"), R("pr", 0, 128), False, True)
+        if t == 1:
             mm(R("B5", 0, 128), R("Bo"), R("pr", 128, 256))
 
     def step1_d(t):
         pa = R("PA", 256 * t, 256 * t + 256)
         act(pa, R("B7", 128, 384), F.Relu)
         send([(STEP[t], pa, R("RA", 256 * t, 256 * t + 256), "ma%d" % t)])
-        if t < 2:
+        if t == 1:
             act(R("PW", 256 * t, 256 * t + 128), R("B5", 0, 128), F.Identity)
 
     def step1_e(t):
         tt(R("PB", 256 * t, 256 * t + 128), R("B6", 384, 512), R("mask"), A.mult)
         tt(R("PB", 256 * t + 128, 256 * t + 256), R("B6", 384, 512), R("PA", 256 * t + 128, 256 * t + 256), A.mult)
-        send([(STEP[t], R("PB", 256 * t, 256 * t + 256), R(XD[t], 128, 384), "mb%d" % t),
-              (STEP[t + 1], R("PW", 256 * t, 256 * t + 256), R(Wn[t + 1], 128, 384), "mw%d" % t)])
+        second = (STEP[t], R("PB", 256 * t, 256 * t + 256), R(XD[t], 128, 384), "mb%d" % t)
+        if t == 0:
+            send([second])
+            send([(STEP[1], beta(0), R("Wn1", 256, 384), "mw0")])
+        else:
+            send([second, (STEP[2], R("PW", 256, 512), R("Wn2", 128, 384), "mw1")])
 
     def step1_ge():
         mm(R("B7", 384, 512), R("nUp"), R("tt", 0, 128))
         act(R("geN"), R("B7", 384, 512), F.Identity, bias=-1.0, scale=-1.0)
 
-    def key_steps(t, bank):
+    def key_turn(t, bank):
+        mm(R(bank, 0, 264), R("eight", 0, 128, 1, 32), R("dcn", 0, 264, 1, 32), True, False)
         for gg in range(8):
-            mm(R(bank, 33 * gg, 33 * gg + 33), R("X16", gg, 1024, 8), R("dif", 33 * t, 33 * t + 33))
+            mm(R(bank, 33 * gg, 33 * gg + 33), R("X16", gg, 1024, 8, 96), R("dif", 33 * t, 33 * t + 33, 1, 96),
+               False, gg == 7)
+
+    def key_keep(t, bank):
         act(R("kp", 264 * t, 264 * t + 264), R(bank, 0, 264), F.Identity)
 
-    cp(R("pm16"), R("turn"))
     ts(R("P16"), R("cnd"), 2048.0, A.subtract)
     for q in range(8):
         c0 = (q % 4) * 128
         mm(R("B%d" % (1 + q // 4), c0, c0 + 128, 1, 96), R("P16", q, 768, 8), R("pm16"))
-    step1_a(0)
     tt(R("dif", 0, 99, 1, 96), R("dfa", 0, 99, 1, 96), R("dfb", 0, 99, 1, 96), A.subtract)
+    ts(R("tri"), R("jv", 0, 16), R("cols", 0, 1), A.is_ge, 32768.0, A.mult)
+    mset(R("nil16"), 0.0)
     cp(R("ex"), R("idd"))
-    cp(R("dif", 32, 99, 33, 96), R("dfa", 32, 99, 33, 96))
-    cp(R("X16", 0, 512, 1, 96), R("B1", 0, 512, 1, 96))
-    cp(R("X16", 512, 1024, 1, 96), R("B2", 0, 512, 1, 96))
-    step1_b(0)
-    step1_c(0)
-    key_steps(0, "B1")
-    ts(R("ngr"), grp, -1.0, A.mult)
-    ts(R("tri"), R("rowj", 0, 16), R("cols", 0, 1), A.is_ge, 32768.0, A.mult)
-    cp(R("Q16", 0, 8), grp)
-    mset(R("B0", 32, 264, 33), float(3 << 22))
     mset(R("tri", 15, 16), 6144.0)
-    cp(R("Q16", 8, 16), grp)
-    mset(R("c26"), 26880.0)
-    mset(R("lrow", 128, 144), 0.0)
-    mset(R("PO"), 0)
-
-    def clash_constants():
-        for q in range(8):
-            ts(R("RB", TOFF[q], TOFF[q] + SEG[q]), R("ones16", 0, SEG[q]), R("ngr", q, q + 1), A.mult)
 
     def landing_constants():
-        cp(R("XD0", 0, 128), R("mask"))
         scan(R("js"), R("rst"), R("jm"), A.mult, A.add)
-        ts(R("n256"), R("nL"), 256.0, A.add)
+        ts(R("n128", 0, 8), R("nL"), 128.0, A.add)
+        ts(R("n128", 8, 16), R("nL"), 128.0, A.add)
+        cp(R("XD0", 0, 128), R("mask"))
         tt(R("base"), R("js", 15, 256, 16), R("n128"), A.min)
-
-    def list_constants():
-        cp(R("XD1", 0, 128), R("mask"))
-        ts(R("b16", 16, 24), R("nL"), float(V), A.add)
-        cp(R("b16", 24, 32), R("trf", 16, 24))
-        ts(R("b16", 32, 40), R("nL"), float(V), A.add)
-
-    def relink_constants():
-        tt(R("jg"), R("rowj", 128, 256), R("mask"), A.mult)
-        ts(R("jx1"), R("base", 8, 16), 128.0, A.min)
-        tt(R("md1"), R("jg"), R("jm", 128, 256), A.subtract)
 
     def relink():
         scan(R("js", 0, 128), R("rst", 0, 128), R("jm", 0, 128), A.mult, A.add)
+        cp(R("XD1", 0, 128), R("mask"))
+        ts(R("b16", 16, 24), R("nL"), float(V), A.add)
         tt(R("base", 8, 16), R("base", 8, 16), R("js", 15, 128, 16), A.add)
+        cp(R("b16", 24, 32), R("trf", 16, 24))
 
     def as_days(o, z, tmark, bank, lo):
         mm(R(bank, lo, lo + 128), R("I256"), tmark, True, False)
@@ -461,23 +464,20 @@ def rank_program(g, core, T, topo):
         if t > 0:
             act(bt, IND(R(Wn[t]), R(RO[t], 0, 8)), F.Identity)
             tt(R("uu"), R("RG", 128 * (t - 1), 128 * t), R("dl"), A.mult)
-        else:
-            step1_d(0)
-        mm(R("B6", 0, 128), bt, R("I"))
+        mm(R("B7", 0, 128), bt, R("I"))
+        tt(R("xm"), R("B7", 0, 128), R("mask"), A.mult)
         for j in range(4):
             mm(R("B4", 128 * j, 128 * j + 128), R("I15"), bt)
-        tt(R("xm"), R("B6", 0, 128), R("mask"), A.mult)
         mm(R("B3", 128, 384), R("xm"), R("Q97"), False, True)
         if t > 0:
             tt(IND(Zall, src_list(t - 1)), R("zp"), R("uu"), A.add)
         else:
-            step1_e(0)
+            cp(R("X16", 0, 512, 1, 96), R("B1", 0, 512, 1, 96))
         act(R("thr"), R("B4"), F.Identity)
         halves = [(0, 128), (128, 256)]
         for (lo, hi) in halves:
             tt(R("ci", lo, hi), R("B3", 128 + lo, 128 + hi), R("cnd", 256 * t + lo, 256 * t + hi), A.add)
-        if t > 0:
-            step1_a(t)
+        step1_a(t)
         for (lo, hi) in halves:
             ts(R("cj", lo, hi), R("ci", lo, hi), W - 1, A.bitwise_and)
         for (lo, hi) in halves:
@@ -505,47 +505,48 @@ def rank_program(g, core, T, topo):
             act(R("cmp", 128 * k0, 128 * k1), R("B%d" % (1 + j % 2), 0, 128 * (k1 - k0)), F.Sign, bias=-0.5)
 
         vchunk(0)
-        if t > 0:
-            step1_b(t)
-        sgather(0)
-        if t > 0:
-            step1_c(t)
-        score(VCH[0], "Wv")
-        vchunk(1)
+        step1_b(t)
         if t == 0:
-            sgather(1)
-        ssign(0)
-        if t > 0:
-            step1_d(t)
+            cp(R("X16", 512, 1024, 1, 96), R("B2", 0, 512, 1, 96))
+            cp(R("dif", 32, 99, 33, 96), R("dfa", 32, 99, 33, 96))
+        sgather(0)
+        step1_c(t)
+        score(VCH[0], "Wv")
+        if t == 0:
+            key_turn(0, "B4")
+        vchunk(1)
+        sgather(1)
+        step1_d(t)
         score(VCH[1], "Wv")
         vchunk(2)
-        if t > 0:
-            sgather(1)
-        score(SCH[0], "Ws")
-        if t == 1:
-            step1_e(1)
+        ssign(0)
+        if not last:
+            step1_e(t)
         score(VCH[2], "Wv")
-        vchunk(3)
+        score(SCH[0], "Ws")
         sgather(2)
+        vchunk(3)
         ssign(1)
         score(VCH[3], "Wv")
         vchunk(4)
-        mm(R("B3", 384, 392), R("I"), R("c26"), True, False)
-        mm(R("B3", 384, 392), bt, R("W97"), False, False)
-        mm(R("B3", 384, 392), R("RA", 256 * t, 256 * t + 128), R("W23"), False, True)
         score(SCH[1], "Ws")
+        if t == 0:
+            key_keep(0, "B4")
         ssign(2)
         score(VCH[4], "Wv")
         vchunk(5)
-        score(SCH[2], "Ws")
         score(VCH[5], "Wv")
+        score(SCH[2], "Ws")
+        mm(R("B3", 384, 392), R("I"), R("c26"), True, False)
+        mm(R("B3", 384, 392), bt, R("W97"), False, False)
+        mm(R("B3", 384, 392), R("RA", 256 * t, 256 * t + 128), R("W23"), False, True)
         if t == 0:
-            clash_constants()
+            tt(R("jm"), IND(R("JT"), R("jo", 16, 32)), R("m2"), A.mult)
         if t == 1:
             tt(R("jm", 0, 128), IND(R("lrow"), R("jx1")), R("md1"), A.mult)
+        scan(R("sc"), R("kp", 264 * t, 264 * t + 264), R("B0", 0, 264), A.add, A.min)
         if last:
             as_days(R("rd"), R("zz", 0, 128), R("tt", 0, 128), "B6", 256)
-        scan(R("sc"), R("kp", 264 * t, 264 * t + 264), R("B0", 0, 264), A.add, A.min)
         if t > 0:
             act(R("ra"), IND(Zw, src_list(t - 1)), F.Identity)
             act(R("rb"), R("ra"), F.Sign)
@@ -554,8 +555,14 @@ def rank_program(g, core, T, topo):
         for q in range(8):
             bk, c0 = SOFF[q]
             mm(R("B%d" % bk, c0 + SEG[q] - 16, c0 + SEG[q]), R("I16"), R("tri"), False, False)
+        if t == 0:
+            cp(R("Q16", 0, 8), grp)
         tt(R("ki"), R("B3", 384, 392), R("sc", 32, 264, 33), A.add)
+        if t == 0:
+            cp(R("Q16", 8, 16), grp)
         ts(R("km"), R("ki"), (3 << 22) | (W - 1), A.bitwise_and)
+        if t == 0:
+            ts(R("n256"), R("nL"), 256.0, A.add)
         ts(R("A16"), IND(R("km"), R("ex", 0, 8)), 8192.0, A.min, 2048.0, A.subtract)
         tt(R("B16"), R("A16"), R("mask"), A.mult)
         for q in range(8):
@@ -582,14 +589,18 @@ def rank_program(g, core, T, topo):
             bk, c0 = SOFF[q]
             o, i = R("mn", q, q + 1), R("B%d" % bk, c0, c0 + SEG[q])
             op("v", lambda: g.vector.tensor_reduce(o[0], i[0], AxisListType.X, A.min, apply_absolute_value=True), o, [i])
-        ts(R("dU"), R("B3", 392, 400), 2048.0, A.add, float(W - 1), A.min)
-        ts(R("land", 0, 8), R("mn"), 0.0, A.is_gt)
+            if q == 4:
+                ts(R("dU"), R("B3", 392, 400), 2048.0, A.add, float(W - 1), A.min)
         act(R("zd"), IND(Zc, R("dU")), F.Identity)
         act(R("ed"), R("zd"), F.Relu, bias=1.0, scale=-1.0)
         if last:
-            tt(R("Rm", 0, 128), IND(R("land", 0, 8), R("ex", 0, 8)), R("mask"), A.mult)
+            ts(R("b16", 32, 40), R("nL"), float(V), A.add)
+            tt(R("Rm", 0, 128), IND(R("mn"), R("ex", 0, 8)), R("mask"), A.min)
+            ts(R("land", 0, 8), R("mn"), 0.0, A.is_gt)
         else:
             tt(R("doff", 0, 8), R("n256"), R("base", 8 * t, 8 * t + 8), A.subtract)
+            ts(R("land", 0, 8), R("mn"), 0.0, A.is_gt)
+            ts(R("ta"), R("B3", 392, 408), 2048.0, A.add)
             tt(R("Rm"), IND(R("land", 0, 8), R("ex")), R(XD[t], 0, 256), A.mult)
             mm(R("B5", 0, 128), R("Bo"), R("Rm", 128, 256), False, True)
         mm(R("B4", 0, 128), R("Bo"), R("Rm", 0, 128), False, True)
@@ -597,7 +608,10 @@ def rank_program(g, core, T, topo):
         act(pg, R("B4", 0, 128), F.Identity)
         if not last:
             tt(R("oa"), R("land", 0, 8), R("doff", 0, 8), A.mult)
-            ts(R("ta"), R("B3", 392, 408), 2048.0, A.add)
+            if t == 0:
+                mset(R("PO"), 0)
+            else:
+                ts(R("land", 8, 16), R("mn"), 0.0, A.is_gt)
             tt(R("ob"), R("oa"), R("base", 8 * t, 8 * t + 8), A.add)
             pn = R("PN", 128 * t, 128 * t + 128)
             cp(pn, R("B5", 0, 128))
@@ -611,21 +625,24 @@ def rank_program(g, core, T, topo):
             as_days(R("yd"), R("zd"), R("td"), "B7", 0)
         if t == 0:
             mm(R("B7", 0, 128), R("Bo"), R("Rm", 0, 128))
-            act(R("lrow", 0, 128), R("B7", 0, 128), F.Identity)
             ts(R("b16", 0, 8), R("nL"), float(V), A.add)
             cp(R("b16", 8, 16), R("trf", 8, 16))
+            mset(R("lrow", 128, 144), 0.0)
+            act(R("lrow", 0, 128), R("B7", 0, 128), F.Identity)
+            ts(R("land", 8, 16), R("mn"), 0.0, A.is_gt)
         if not last:
-            key_steps(t + 1, "B1")
+            key_turn(t + 1, "B1")
+            key_keep(t + 1, "B1")
         w = 8 if last else 16
         bs = R("b16", 16 * t, 16 * t + w)
         if last:
             ts(R("ta", 0, w), R("B3", 392, 392 + w), 2048.0, A.add)
             put_days(2, "rd", 1)
-        else:
-            ts(R("land", 8, 16), R("mn"), 0.0, A.is_gt)
         tt(R("tb", 0, w), R("ta", 0, w), bs, A.subtract)
         if last:
             put_days(1, "rc", 0)
+        if t == 0:
+            ts(R("jx1"), R("base", 8, 16), 128.0, A.min)
         tt(R("tc", 0, w), R("tb", 0, w), R("land", 0, w), A.mult)
         if last:
             put_days(1, "rc", 1)
@@ -638,12 +655,12 @@ def rank_program(g, core, T, topo):
         cp(R("zp"), IND(Sw, src_list(t)))
         mm(R("B6", 128, 256), R("TopM"), R("zp"))
         if t == 0:
-            list_constants()
+            tt(R("jg"), R("rowj"), R("mask"), A.mult)
         if t == 1:
             put_days(0, "rc", 0)
         tt(R("dl"), R("B6", 128, 256), R("geN"), A.mult)
         if t == 0:
-            relink_constants()
+            tt(R("md1"), R("jg"), R("jm", 128, 256), A.subtract)
         if t == 1:
             put_days(0, "rc", 1)
 

@@ -1,59 +1,128 @@
 from concourse.bass import DstId, RemoteDMATransfer
-from concourse.mybir import AluOpType as A, AxisListType, ActivationFunctionType as F
+from concourse.mybir import AluOpType as A, ActivationFunctionType as F
 
 N, W, V, S, K = 8, 4096, 4608, 128, 32
 STEP = (1, 2, 3)
-KV = 20
-VCH = [(0, 2), (2, 6), (6, 10), (10, 14), (14, 18), (18, KV)]
-SCH = [(KV, KV + 4), (KV + 4, KV + 8), (KV + 8, K)]
+SCH = [[(4, 8), (8, 12), (12, 15)]] * 3
+VCH = [[(0, 2), (2, 4), (15, 19), (19, 23), (23, 27), (27, 31), (31, 32)]] * 3
 UNIT = 1 << 18
-SEG = [16 * (q + 1) for q in range(8)]
-SOFF = [(1, 0), (1, 16), (1, 48), (1, 96), (1, 160), (2, 0), (2, 96), (2, 208)]
-TOFF = [0, 16, 48, 96, 160, 240, 336, 448]
+BIG, OFF = float(1 << 24), float(1 << 19)
+NV = 6
+EOFF = [0, 112, 208, 288, 352, 400, 432]
 LOADS = [(4096, 4608), (0, 2048), (2048, 3072), (3072, 4096)]
-CH = [(4096, 4608), (0, 1024), (1024, 2048), (2048, 3072), (3072, 4096)]
+ZBANK = ("B0", "B5", "B6", "B2", "B5", "B6", "B4", "B1", "B4")
+ZADD = (6, 7)
+
+CYCLE, LINK, GATHER, SCATTER = 0.00093, 0.15, 1.56, 3.8
+ISSUE, FIRST, HOP, HOP2, DMA0, ROW, RATE = 0.3, 2.3, 1.6, 1.85, 1.6, 0.02, 20000.0
 
 bf, f32, i32, u16, f16 = "bfloat16", "float32", "int32", "uint16", "float16"
+SIZE = {bf: 2, f32: 4, i32: 4, u16: 2, f16: 2}
 SCRATCH = {}
 WHERE = {}
 for _n, _w, _d in [
     ("Y", V + S, bf), ("Z", V + S, bf), ("t256", V, bf), ("trk", 24, i32), ("cnd", 768, i32),
-    ("ones", 128, bf), ("I", 128, bf), ("nI", 128, bf), ("I256", 128, bf), ("I15", 128, bf), ("Bo0", 128, bf),
-    ("Bo", 128, bf), ("nBo", 128, bf), ("Bq", 128, bf), ("nUp", 128, bf), ("Up2", 128, bf), ("nDn", 128, bf),
-    ("TopM", 128, bf), ("FstE", 128, bf), ("E0", 128, bf), ("mask", 128, bf), ("rst", 256, bf), ("c26", 8, bf),
-    ("c97", 256, bf), ("Q0", 256, bf), ("Q1", 256, bf), ("Q97", 256, bf), ("turn", 128, bf), ("dfa", 99, bf),
-    ("dfb", 99, bf), ("I16", 128, f16), ("ones16", 128, f16), ("Q16", 16, f16), ("pm16", 128, f16),
-    ("RB", 576, f16), ("nil16", 336, f16), ("tri", 16, f16), ("dif", 99, f16), ("dcn", 264, f16), ("eight", 128, f16),
-    ("P16", 768, f16), ("X16", 1024, f16), ("Wv", 8, bf), ("Ws", 8, bf), ("W97", 8, bf), ("W23", 8, bf),
-    ("ia", 128, i32), ("ib", 128, i32), ("ic", 16, i32), ("idd", 16, i32), ("ex", 16, u16), ("rowj", 128, bf),
-    ("kp", 792, f32), ("JT", 1280, bf), ("jo", 32, u16), ("ro", 8, u16),
-    ("jg", 128, bf), ("jm", 256, bf), ("js", 256, bf), ("jv", 256, bf), ("m2", 256, bf),
-    ("md1", 128, bf), ("jx1", 8, u16), ("SL", 72, u16), ("dU", 8, u16),
-    ("PW", 768, bf), ("Wn1", 384, bf), ("Wn2", 384, bf), ("XD0", 384, bf), ("XD1", 384, bf), ("PA", 768, bf),
-    ("PB", 512, bf), ("RA", 768, bf), ("RG", 384, bf), ("PG", 384, bf), ("PN", 256, bf), ("PO", 256, u16),
-    ("RO1", 128, u16), ("RO2", 128, u16), ("p0", 128, bf), ("lrow", 144, bf),
-    ("xm", 128, bf), ("ci", 256, i32), ("cj", 256, i32), ("cu", 256, u16), ("thr", 512, bf), ("cmp", 4096, bf),
-    ("raw", 1536, bf), ("sc", 264, f32), ("ki", 8, i32), ("km", 8, i32), ("A16", 128, f16), ("B16", 128, f16),
-    ("Rm", 256, bf),
-    ("zz", 256, bf), ("tt", 256, bf), ("pr", 384, bf), ("rl", 128, bf), ("geN", 128, bf), ("ed", 128, bf),
-    ("zd", 128, bf), ("fd", 128, bf), ("zp", 128, bf), ("dl", 128, bf), ("uu", 128, bf), ("braw", 128, bf),
-    ("ra", 128, bf), ("rb", 128, bf), ("rc", 128, bf), ("rd", 128, bf), ("td", 128, bf), ("yd", 128, bf),
+    ("I16", 128, f16), ("Q16", 8, f16), ("pm16", 128, f16), ("RD", 144, f16), ("tri", 144, f16),
+    ("dif", 132, f16), ("P16", 768, f16), ("X", 768, f16),
+    ("ic", 16, i32), ("ex", 8, u16), ("kp", 792, f32), ("JT", V + 512, bf), ("jo", 32, u16),
+    ("jx1", 8, u16), ("SL", 72, u16), ("dU", 8, u16),
+    ("rc0", 128, bf), ("RC", 128, bf), ("zz", 512, bf), ("ZR", 384, bf), ("res1", 128, bf), ("RS1", 128, bf),
+    ("bt", 512, bf), ("BT1", 128, bf), ("RB2", 256, bf), ("pm1", 128, u16), ("PM1", 128, u16), ("pm2", 256, u16),
+    ("PM2", 256, u16), ("G", 384, bf), ("RG", 384, bf), ("NL", 288, bf), ("RN", 256, bf), ("wn", 256, bf),
+    ("WD", 512, bf), ("q", 256, bf), ("cu", 256, u16),
+    ("thr", 512, bf), ("cmp", 4096, bf), ("raw", 1536, bf), ("sc", 264, f32), ("ki", 8, i32), ("km", 8, i32),
+    ("A16", 128, f16), ("B16", 128, f16), ("E", 432, bf), ("sp", 144, bf), ("sm", 144, bf),
 ]:
     SCRATCH[_n] = ("sbuf", [128, _w], _d)
     WHERE[_n] = (_n, 0, _w)
-_c = 0
-for _n, _w in [("cols", 8), ("ngr", 8), ("nL", 8), ("trf", 24), ("jtmp", 32), ("n128", 16), ("n256", 8), ("base", 16),
-               ("doff", 16), ("b16", 48), ("mn", 8), ("land", 16), ("ta", 16), ("tb", 16), ("tc", 16), ("oa", 8),
-               ("ob", 8)]:
-    WHERE[_n] = ("small", _c, _w)
-    _c += _w
-SCRATCH["small"] = ("sbuf", [128, _c], f32)
+
+
+def _pack(buf, dt, items):
+    c = 0
+    for n, w in items:
+        WHERE[n] = (buf, c, w)
+        c += w
+    SCRATCH[buf] = ("sbuf", [128, c], dt)
+
+
+_pack("small", f32, [("c15", 8), ("nL", 8), ("trf", 24), ("n128", 16), ("base", 16), ("far", 16), ("mx", 8),
+                     ("dd", 8), ("ta", 8), ("tb", 8), ("row", 128), ("farm", 128), ("zl", 128), ("ll", 128)])
+_pack("konst", bf, [(_n, 128) for _n in (
+    "ones", "G16", "R16", "I", "nI", "I256", "I15", "m4k", "Bo", "nBo", "BoR", "BoC", "nE0", "bar0", "Up",
+    "nUp", "nUp2", "nDn", "TopM", "FstE", "mask", "turn", "cst", "B8k", "B4k", "nB4k", "off", "rsb")]
+      + [("Q97", 256), ("jv", 256), ("rst", 256), ("m2", 256), ("dcn", 272), ("dfa", 144), ("dfb", 144),
+         ("dfc", 144), ("cols", 16), ("Wv", 16), ("Ws", 16), ("W97", 16), ("W33", 16), ("c26", 16), ("c33", 16),
+         ("cS", 16)])
+_pack("work", bf, [(_n, 128) for _n in (
+    "s33", "sgz", "nask", "bar", "sec", "gg", "ed", "zd", "td", "yd", "fd", "braw", "ra", "rb", "rd", "re0",
+    "re1", "nj", "zj", "lj", "t2", "t3", "xm", "r1", "s1")]
+      + [("tt", 512), ("jm", 256), ("js", 256), ("zp", 384), ("uu", 384)])
 for _b in range(8):
     SCRATCH["B%d" % _b] = ("psum", [128, 512], f32)
     WHERE["B%d" % _b] = ("B%d" % _b, 0, 512)
 
-ARR = ["b0", "me", "ma0", "ma1", "ma2", "mb0", "mb1", "mw0", "mw1", "mo0", "mo1", "mg0", "mg1", "mg2", "mn0", "mn1"]
+ARR = ["b0", "me", "z0", "z1", "z2", "s0", "s1", "g0", "g1", "g2", "n0", "n1", "w0", "w1"]
 SEMAPHORES = ["ev", "es", "ep", "eg", "sent"] + ["d%d" % _i for _i in range(10)] + ARR
+
+
+def clashes(hist, e, reads, writes):
+    out = []
+    for regs, wr in ((reads, False), (writes, True)):
+        for (n, lo, hi) in regs:
+            ps = SCRATCH[n][0] == "psum"
+            for (l2, h2, w2, e2, tok) in hist.get(n, []):
+                if (ps and (e2 != e or e == "p")) or (lo < h2 and l2 < hi and (wr or w2)):
+                    out.append((e2, tok))
+    return out
+
+
+def plan(calls):
+    hist, before, sender, last = {}, [], {}, {}
+    for j, c in enumerate(calls):
+        for s in c["sems"]:
+            sender[s] = j
+    for j, c in enumerate(calls):
+        pre = {}
+        for (e2, i) in clashes(hist, c["e"], c["reads"], c["writes"]):
+            if e2 == "r":
+                pre[sender[i]] = max(pre.get(sender[i], 0.0), calls[sender[i]]["hop"])
+            elif not c["kind"] == calls[i]["kind"] == "sum":
+                pre[i] = max(pre.get(i, 0.0), 0.0 if e2 == c["e"] == "p" else LINK)
+        if c["kind"] == "send" and j > min(sender.values()):
+            pre.setdefault(min(sender.values()), 0.0)
+        if c["line"] in last:
+            pre.setdefault(last[c["line"]], 0.0)
+        if c["line"]:
+            last[c["line"]] = j
+        before.append(pre)
+        tok = c["lands"] if c["e"] == "r" else j
+        for regs, wr in ((c["reads"], False), (c["writes"], True)):
+            for (n, lo, hi) in regs:
+                hist.setdefault(n, []).append((lo, hi, wr, c["e"], tok))
+    after = [[] for _ in calls]
+    for j, pre in enumerate(before):
+        for i, lat in pre.items():
+            after[i].append((j, lat))
+    tail = {}
+    for j in reversed(range(len(calls))):
+        tail[j] = calls[j]["cost"] + calls[j]["soon"] + max([lat + calls[k]["lead"] + tail[k] for k, lat in after[j]]
+                                                            + [0.0])
+    start, ready, busy = {}, {}, {}
+    for j in sorted(range(len(calls)), key=lambda x: (-tail[x], x)):
+        c = calls[j]
+        if c["e"] == "r":
+            continue
+        t = c["lead"] + max([start[i] + calls[i]["cost"] + lat for i, lat in before[j].items()] + [0.0])
+        ready[j] = t - c["lead"]
+        lane = busy.setdefault("d" if c["lead"] else c["e"], [])
+        for (a, b) in lane:
+            if t + c["cost"] <= a + 1e-9:
+                break
+            t = max(t, b)
+        lane.append((t, t + c["cost"]))
+        lane.sort()
+        start[j] = t
+    return sorted(start, key=lambda x: (ready[x] if calls[x]["lead"] else start[x], start[x], x))
 
 
 def rank_program(g, core, T, topo):
@@ -62,21 +131,486 @@ def rank_program(g, core, T, topo):
         return
     Q = {"v": g.vector, "s": g.scalar, "p": g.tensor, "g": g, "y": g.sync}
     ESEM = {"v": "ev", "s": "es", "p": "ep", "g": "eg"}
-    cnt = {"ev": 0, "es": 0, "ep": 0, "eg": 0}
+    calls = []
+
+    def R(name, lo=0, hi=None, step=1, parts=128, p0=0):
+        buf, c0, w = WHERE[name]
+        lo, hi = c0 + lo, c0 + (w if hi is None else hi)
+        ap = T[buf][p0:parts, lo:hi] if step == 1 else T[buf][p0:parts, lo:hi:step]
+        return (ap, [(buf, lo, hi)], [], len(range(lo, hi, step)), SIZE[SCRATCH[buf][2]], SCRATCH[buf][0] == "psum")
+
+    def IND(win, off):
+        return (win[0].indirect(off[0]), win[1], off[1], 16 * off[3], win[4], False)
+
+    def call(e, issue, reads, writes, cost, lead=0.0, hop=0.0, sems=(), lands=None, kind="op"):
+        calls.append(dict(e=e, issue=issue, reads=reads, writes=writes, cost=cost, lead=lead, hop=hop, sems=sems,
+                          lands=lands, kind=kind, line=None, soon=0.0))
+
+    def soon(us):
+        calls[-1]["soon"] = us
+
+    def line(name):
+        calls[-1]["line"] = name
+
+    def op(e, issue, out, ins, rate):
+        ins = [x for x in ins if isinstance(x, tuple)]
+        cost = max(64.0, rate * out[3]) * CYCLE
+        if out[2]:
+            cost = 0.056 + SCATTER * out[3] * CYCLE
+        elif any(x[2] for x in ins):
+            cost = 0.06 + GATHER * out[3] * CYCLE
+        elif e == "p":
+            cost = max(min(64, ins[0][3]), out[3]) * CYCLE / 2
+        elif e == "g":
+            cost = 0.18 + 2 * out[3] * CYCLE
+        call(e, issue, out[2] + [r for x in ins for r in x[1] + x[2]], out[1], cost)
+
+    def ap(x):
+        return x[0] if isinstance(x, tuple) else x
+
+    def wide(*xs):
+        return 1.0 if any(x[4] == 4 for x in xs if isinstance(x, tuple)) else 0.5
+
+    def mset(o, c):
+        op("v", lambda: g.vector.memset(o[0], c), o, [], wide(o))
+
+    def cp(o, i):
+        op("v", lambda: g.vector.tensor_copy(o[0], i[0]), o, [i], wide(o, i))
+
+    def tt(o, a, b, f):
+        op("v", lambda: g.vector.tensor_tensor(o[0], a[0], b[0], f), o, [a, b], 1.0 if a[5] or b[5] else 2.0)
+
+    def ts(o, a, s1, f0, s2=None, f1=None):
+        if f1 is None:
+            op("v", lambda: g.vector.tensor_scalar(o[0], a[0], ap(s1), None, f0), o, [a, s1], wide(o, a, s1))
+        else:
+            op("v", lambda: g.vector.tensor_scalar(o[0], a[0], ap(s1), ap(s2), f0, f1), o, [a, s1, s2],
+               wide(o, a, s1, s2))
+
+    def scan(o, d0, d1, f0, f1):
+        op("v", lambda: g.vector.tensor_tensor_scan(o[0], d0[0], d1[0], 0.0, f0, f1), o, [d0, d1], wide(o, d0, d1))
+
+    def act(o, i, fn=F.Identity, bias=0.0, scale=1.0):
+        op("s", lambda: g.scalar.activation(o[0], i[0], fn, bias=bias, scale=ap(scale)), o, [i, scale], 1.0)
+
+    def mm(o, l, r, start=True, stop=True):
+        op("p", lambda: g.tensor.matmul(o[0], l[0], r[0], start, stop), o, [l, r], 1.0)
+
+    def mms(o, pairs):
+        for j, (l, r) in enumerate(pairs):
+            mm(o, l, r, j == 0, j == len(pairs) - 1)
+
+    def tier_sum(o, pairs):
+        def issue():
+            return [g.tensor.matmul(o[0], l[0], r[0], j == 0, j == len(pairs) - 1) for j, (l, r) in enumerate(pairs)][-1]
+
+        call("p", issue, [x for (l, r) in pairs for x in l[1] + r[1]], o[1], 32 * CYCLE * len(pairs), kind="sum")
+
+    def iota(o, pat, base, cm, fl=True):
+        if fl:
+            op("g", lambda: g.iota(o[0], pat, base, cm, allow_small_or_imprecise_dtypes=True), o, [], 2.0)
+        else:
+            op("g", lambda: g.iota(o[0], pat, base, cm), o, [], 2.0)
+
+    def sel(o, i, pat, cmpop, base, cm, fill=0.0):
+        op("g", lambda: g.affine_select(o[0], i[0], pat, cmpop, fill, base, cm), o, [i], 2.0)
+
+    def dma(e, o, i, x, store=False, behind=()):
+        call(e, lambda: Q[e].dma_start(o, i), (x[1] if store else []) + list(behind), [] if store else x[1],
+             8 * (ROW + x[3] * x[4] / RATE), lead=DMA0, kind="dma")
+
+    def lanes(d, part, of):
+        en = topo.engines(core, T.cores[(rank + d) % N])
+        n = len(en) // of
+        m = 0
+        for x in en[part * n:(part + 1) * n]:
+            m |= 1 << x
+        return m, n
+
+    sent, landed = [0], {}
+
+    def send(items, early=0.0):
+        trs = []
+        for j, (d, src, dst, s) in enumerate(items):
+            rid, pid, _ = topo.addr(T.cores[(rank + d) % N])
+            m, n = lanes(d, j, len(items))
+            trs.append((rid, pid, m, s, src[0], dst[0]))
+            sent[0] += n
+            landed[s] = landed.get(s, 0) + len(topo.engines(T.cores[(rank - d) % N], core)) // len(items)
+
+        def issue():
+            if len(trs) == 1:
+                rid, pid, m, s, src, dst = trs[0]
+                g.remote_dma(dst, src, T.sem[s], T.sem.sent, pid, rid, m)
+            else:
+                g.remote_dma_fused([RemoteDMATransfer(dst_ids=[DstId(rid=rid, pnc=pid)], dma_engine_mask=m,
+                                                      remote_sem=T.sem[s], src=src, dst=dst)
+                                    for (rid, pid, m, s, src, dst) in trs], local_sem=T.sem.sent)
+
+        first = not any(c["kind"] == "send" for c in calls)
+        call("g", issue, [r for it in items for r in it[1][1]], [], ISSUE + (FIRST if first else 0.0),
+             hop=(HOP if len(items) == 1 else HOP2) - ISSUE, sems=[it[3] for it in items], kind="send")
+        soon(early)
+
+    def arrive(dsts, s):
+        call("r", None, [], [r for x in dsts for r in x[1]], 0.0, lands=s, kind="land")
+
+    def part(name, t, w=128):
+        return R(name, w * t, w * t + 128)
+
+    arrive([R("RC")], "b0")
+    arrive([R("RS1")], "me")
+    arrive([R("BT1"), R("PM1")], "s0")
+    arrive([R("RB2"), R("PM2")], "s1")
+    for t in range(3):
+        arrive([part("ZR", t)], "z%d" % t)
+        arrive([part("RG", t)], "g%d" % t)
+    for t in range(2):
+        arrive([part("RN", t)], "n%d" % t)
+        arrive([part("WD", t, 256)], "w%d" % t)
+
+    def src_list(t):
+        return R("SL", 24 * t + 8, 24 * t + 16)
+
+    def fill(name, c, lo=0, hi=None, h=None):
+        pp = (128, 0) if h is None else (32 * h + 32, 32 * h)
+        o = R(name, lo, hi, 1, *pp)
+        act(o, R("ones", 0, o[3], 1, *pp), scale=c)
+
+    dma("s", T.trk[:], T.trucks[:], R("trk"))
+    for (lo, hi) in LOADS:
+        dma("y", T.Y[:, lo:hi], T.days[:, lo:hi], R("Y", lo, hi))
+    dma("y", T.cnd[:, 0:256], T.cand[:, 0:256], R("cnd", 0, 256))
+
+    tier, yard, bars = (R("cols", j, j + 1) for j in range(3))
+    c15, wcol, nm0, wc0 = (R("c15", j, j + 1) for j in range(4))
+    grp = R("Bo", 0, 128, 16)
+    one32, one64 = R("ones", 0, 128, 1, 32), R("ones", 0, 128, 1, 64)
+    diag = [[-1, 128]]
+    mset(R("ones"), 1.0)
+    iota(R("ic", 0, 1), [[0, 1]], 0, 1, False)
+    sel(R("I"), R("ones"), diag, A.is_equal, 0, 1)
+    iota(R("G16"), [[1, 8], [0, 16]], 0, 0)
+    iota(R("R16"), [[0, 8], [1, 16]], 0, 0)
+    iota(R("jv", 0, 128), [[1, 128]], 0, 0)
+    soon(12.0)
+    iota(R("ta"), [[16, 8]], 0, 0)
+    sel(R("turn"), R("ones"), [[-1, 16], [-16, 8]], A.is_equal, 0, 1)
+    ts(R("ic", 2, 3), R("ic", 0, 1), 15, A.bitwise_and)
+    ts(R("ic", 3, 4), R("ic", 0, 1), 4, A.arith_shift_right)
+    cp(R("cols", 0, 2), R("ic", 2, 4))
+    ts(R("Bo"), R("G16"), yard, A.is_equal)
+    ts(R("mask"), R("R16"), tier, A.is_equal)
+    ts(R("nL"), R("ta"), tier, A.add)
+    ts(c15, tier, 15.0, A.is_lt)
+    ts(wc0, tier, 15.0, A.is_equal, 15.0 * UNIT, A.mult)
+    ts(wcol, wc0, float(UNIT), A.add)
+    ts(nm0, tier, 0.0, A.is_equal, -1.0, A.mult)
+    ts(bars, c15, 38912.0, A.mult, 6144.0, A.subtract)
+    mset(R("rst"), 1.0)
+    mset(R("rst", 0, 256, 16), 0.0)
+    for name, src, scale in [("nI", "I", -1.0), ("m4k", "I", -4096.0), ("I256", "I", 256.0), ("I15", "I", c15),
+                             ("nBo", "Bo", -1.0), ("BoC", "Bo", 1.0), ("BoR", "Bo", c15), ("nE0", "Bo", nm0),
+                             ("B8k", "Bo", 8192.0), ("B4k", "Bo", 4096.0), ("nB4k", "Bo", -4096.0)]:
+        act(R(name), R(src), scale=scale)
+    mset(R("BoC", 15, 128, 16), 0.0)
+    sel(R("nUp"), R("nBo"), diag, A.is_equal, -1, 1)
+    sel(R("nUp2"), R("nBo"), diag, A.is_equal, -2, 1)
+    sel(R("nDn"), R("nBo"), diag, A.is_equal, 1, 1)
+    sel(R("TopM"), R("nUp"), diag, A.not_equal, 0, 1, 1.0)
+    sel(R("FstE"), R("nDn"), diag, A.not_equal, 0, 1, 1.0)
+    act(R("Up"), R("nUp"), scale=-1.0)
+    act(R("Q97", 0, 8), grp, scale=-97.0)
+    act(R("Q97", 8, 16), grp, scale=-97.0)
+    for w in (16, 32, 64, 128):
+        act(R("Q97", w, 2 * w), R("Q97", 0, w))
+    act(R("Wv", 0, 8), grp, scale=wcol)
+    act(R("Ws", 0, 8), R("Wv", 0, 8), scale=0.5)
+    act(R("W97", 0, 8), R("nE0", 0, 128, 16), scale=97.0)
+    act(R("W33", 0, 8), R("BoR", 0, 128, 16), scale=BIG / 2)
+    act(R("B3", 0, 128), R("mask"))
+    for h in range(2):
+        act(R("n128", 8 * h, 8 * h + 8), R("nL"), bias=128.0)
+        fill("cst", (16384.0, 968.0)[h], h=h)
+        fill("c26", (712.0, -65536.0)[h], 0, 8, h)
+        fill("WD", 0.0, 256 * h + 128, 256 * h + 256)
+    fill("cS", 31.0 * W, 0, 8, 0)
+    fill("c33", 15.0 * UNIT, 0, 8, 0)
+    fill("Z", 0.0, V, V + S)
+    fill("Y", 0.0, V, V + S)
+    fill("NL", 0.0, 128, 144)
+    act(R("jv", 128, 256), R("jv", 0, 128))
+    soon(12.0)
+    act(R("off"), R("mask"), scale=-OFF, bias=OFF)
+    act(R("bar0"), R("mask"), scale=-OFF, bias=OFF + W)
+    act(R("rsb"), R("rst", 0, 128), scale=-BIG, bias=BIG)
+    act(R("row"), R("jv", 0, 128), bias=float(V - 2048))
+    tt(R("farm"), R("row"), R("off"), A.add)
+    cp(R("I16"), R("I"))
+    cp(R("Q16"), grp)
+    cp(R("pm16"), R("turn"))
+    cp(R("ex"), R("jv", 0, 8))
+    ts(R("tri", 0, 128), R("R16"), tier, A.is_le, bars, A.mult)
+    mset(R("tri", 128, 144), 0.0)
+    ts(R("RD", 0, 128), R("Bo"), c15, A.mult, -1.0, A.mult)
+    ts(R("RD", 128, 144), R("ones", 0, 16), R("nBo", 16 * NV, 16 * NV + 1), A.mult)
+    fill("dfa", 1.0, 0, 128)
+    fill("dfa", 1.0, 128, 132)
+    sel(R("dfb", 0, 132), R("dfa", 0, 132), [[-32, 4], [-1, 33]], A.is_equal, 1, 1)
+    sel(R("dfc", 0, 132), R("dfb", 0, 132), [[-32, 4], [-1, 33]], A.not_equal, 0, 1, -1.0)
+    cp(R("dif"), R("dfc", 0, 132))
+    ts(R("dif", 32, 132, 33), R("dif", 32, 132, 33), 0.0, A.max)
+    mset(R("dcn", 0, 264, 1, 32), -128.0)
+    mset(R("dcn", 0, 264, 33, 32), float(UNIT))
+    mset(R("dcn", 32, 264, 33, 32), 69632.0)
+
+    cp(R("SL", 8, 16), R("trk", 0, 8))
+    cp(R("SL", 40, 48), R("trk", 16, 24))
+    cp(R("trf"), R("trk"))
+    act(R("far"), R("trf", 8, 24), bias=-2048.0)
+    cp(R("jo", 0, 8), R("trk", 0, 8))
+    ts(R("jo", 8, 16), R("trk", 8, 16), 512.0, A.add)
+    ts(R("jo", 16, 24), R("trk", 8, 16), float(W), A.subtract)
+    ts(R("jo", 24, 32), R("trk", 16, 24), float(W - 512), A.subtract)
+    for h in range(2):
+        mset(R("JT", W + 512 * h, V + 512 * h), 256.0)
+    for h in range(4):
+        cp(IND(R("JT"), R("jo", 4 * h, 4 * h + 4)), R("jv", 64 * h, 64 * h + 64))
+    for h in range(2):
+        jm, js = R("jm", 128 * h, 128 * h + 128), R("js", 128 * h, 128 * h + 128)
+        tt(jm, IND(R("JT", W, V + 512), R("jo", 16 + 8 * h, 24 + 8 * h)), R("mask"), A.mult)
+        scan(js, R("rst", 0, 128), jm, A.mult, A.add)
+        tt(R("base", 8 * h, 8 * h + 8), R("js", 128 * h + 15, 128 * h + 128, 16), R("n128", 0, 8), A.min)
+    mset(R("pm1"), 0)
+    mset(R("pm2"), 0)
+    cp(R("pm1", 0, 8), R("base", 0, 8))
+    ts(R("jx1"), R("base", 8, 16), 128.0, A.min)
+    tt(R("dd"), R("base", 8, 16), R("n128", 0, 8), A.subtract)
+
+    Yw, Zw, Zc, Yall, Zall = R("Y", 0, V), R("Z", 0, V), R("Z", 0, W), R("Y"), R("Z")
+
+    def tops(out, src, sign, rev, bank):
+        act(sign, src, F.Sign)
+        ts(rev, src, -1.0, A.mult, 256.0, A.add)
+        mms(bank, [(R("I"), sign), (R("nUp"), sign)])
+        tt(out, bank, rev, A.mult)
+
+    tops(R("res1"), IND(R("Y", W, V), R("jo", 16, 24)), R("s1"), R("r1"), R("B7", 0, 128))
+    send([(STEP[1], R("res1"), R("RS1"), "me")])
+    tops(R("rc0"), IND(Yw, src_list(0)), part("tt", 0), R("rb"), R("B7", 128, 256))
+    send([(STEP[0], R("rc0"), R("RC"), "b0")])
+    dma("y", T.cnd[:, 256:768], T.cand[:, 256:768], R("cnd", 256, 768), behind=R("RC")[1])
+    tt(part("zz", 0), R("rb"), part("tt", 0), A.mult)
+    send([(STEP[0], part("zz", 0), part("ZR", 0), "z0")])
+    for c in (8, 0, 1, 2, 3, 6, 7, 4, 5):
+        y, z, m, bank = (R("Y", 512 * c, 512 * c + 512), R("Z", 512 * c, 512 * c + 512),
+                         R("t256", 512 * c, 512 * c + 512), R(ZBANK[c]))
+        ts(m, y, 256.0, A.mult, 256.0, A.min)
+        if c in ZADD:
+            mm(bank, R("nI"), y)
+            tt(z, bank, m, A.add)
+        else:
+            mms(bank, [(R("I"), m), (R("nI"), y)])
+            act(z, bank)
+            line("mirror")
+
+    def narrow(t):
+        for lo in range(256 * t, 256 * t + 256, 128):
+            ts(R("P16", lo, lo + 128), R("cnd", lo, lo + 128), 2048.0, A.subtract)
+
+    def turn1(t, bank):
+        for q in range(8):
+            a, c0 = q // 2, 256 + (q % 2) * 128
+            mm(R(bank, c0, c0 + 128, 1, 32 * a + 32, 32 * a), R("P16", 256 * t + q, 256 * t + 256, 8), R("pm16"))
+        for lo in (0, 128):
+            cp(R("X", 256 * t + lo, 256 * t + lo + 128), R(bank, 256 + lo, 384 + lo))
+            soon(0.0 if t else 4.0)
+
+    def turn2(t, bank):
+        mm(R(bank, 0, 264), one32, R("dcn", 0, 264, 1, 32), True, False)
+        for a in range(4):
+            for gg in range(8):
+                mm(R(bank, 33 * gg, 33 * gg + 33, 1, 32 * a + 32, 32 * a), R("X", 256 * t + gg, 256 * t + 256, 8),
+                   R("dif", 33 * a, 33 * a + 33), False, gg == 7)
+        act(R("kp", 264 * t, 264 * t + 264), R(bank, 0, 264))
+
+    for t in range(3):
+        narrow(t)
+
+    def put_days(t, buf):
+        for h in range(2):
+            lo = 24 * t + 8 + 4 * h
+            cp(IND(Yall, R("SL", lo, lo + 4)), R(buf, 64 * h, 64 * h + 64))
+
+    LA = [R("B5", 0, 128), R("B5", 128, 256)]
+    LB = [R("B6", 0, 128), R("B0", 264, 392)]
+
+    for t in range(3):
+        last = t == 2
+        bt = R("bt", (0, 384, 128)[t], (0, 384, 128)[t] + 128)
+        zo, zr, so, zp, uu = part("zz", t), part("ZR", t), part("tt", t), part("zp", t), part("uu", t)
+        thr0 = R("thr", 0, 128)
+        mm(R("B5", 0, 256), R("I16"), R("P16", 256 * t, 256 * t + 256), True, False)
+        for h in range(2):
+            mm(LB[h], R("I16"), R("P16", 256 * t + 128 * h, 256 * t + 128 * h + 128), True, False)
+            mm(LB[h], one64, R("cst", 0, 128, 1, 64), False, False)
+        if t == 0:
+            terms = [R("RC")]
+            mm(R("B7", 0, 128), R("RC"), R("Bo"))
+            mm(R("B4", 0, 128), R("BoC"), R("RC"))
+        else:
+            res, btp = (R("RS1"), R("BT1")) if t == 1 else (R("RB2", 0, 128), R("RB2", 128, 256))
+            rn, zq, uq = part("RN", t - 1), part("zp", t - 1), part("uu", t - 1)
+            terms = [btp, R("t3"), R("t2")]
+            mms(R("B3", 128, 256), [(R("Bo"), res), (R("nI"), btp)])
+            tt(R("t3"), R("B3", 128, 256), rn, A.mult)
+            tt(R("t2"), IND(R("WD", 256 * (t - 1), 256 * t), R("PM%d" % t, 0, 8)), rn, A.mult)
+            mms(R("B7", 0, 128), [(x, R("I")) for x in terms])
+            mms(R("B4", 0, 128), [(R("I15"), x) for x in terms])
+        tt(R("xm"), R("B7", 0, 128), R("mask"), A.mult)
+        act(thr0, R("B4", 0, 128))
+        act(R("thr", 128, 256), thr0)
+        act(R("thr", 256, 512), R("thr", 0, 256))
+        mm(R("B5", 0, 256), R("xm"), R("Q97"), False, True)
+        for h in range(2):
+            q = R("q", 128 * h, 128 * h + 128)
+            mm(LB[h], R("xm"), R("Q97", 128 * h, 128 * h + 128), False, False)
+            act(q, LA[h], bias=135.0 + 513.0 / 8192, scale=1.0 / W)
+            mm(LB[h], R("m4k"), q, False, True)
+            cp(R("cu", 128 * h, 128 * h + 128), LB[h])
+        mms(R("B4", 128, 256), [(R("Bo") if t == 0 else R("I"), x) for x in terms])
+        act(bt, R("B4", 128, 256))
+        if t == 0:
+            send([(STEP[1], bt, R("BT1"), "s0"), (STEP[1], R("pm1"), R("PM1"), "s0")], 4.0)
+            turn1(0, "B4")
+            turn2(0, "B6")
+        else:
+            act(zo, IND(Zw, src_list(t)))
+            send([(STEP[t], zo, zr, "z%d" % t)], 2.5)
+            act(so, zo, F.Sign)
+            mms(R("B7", 0, 128), [(R("I"), zq), (R("I"), uq)])
+            act(R("ra"), R("B7", 0, 128), F.Sign)
+            mms(R("B7", 128, 256), [(R("I256"), R("ra")), (R("nI"), zq), (R("nI"), uq)])
+            act(R("re%d" % (t - 1)), R("B7", 128, 256))
+            put_days(t - 1, "re%d" % (t - 1))
+        if t == 1:
+            act(part("zz", 3), IND(Zw, R("SL", 40, 48)))
+            act(part("tt", 3), part("zz", 3), F.Sign)
+            mm(R("B4", 256, 384), R("TopM"), part("tt", 3))
+            tt(R("bt", 256, 384), R("B4", 256, 384), part("zz", 3), A.mult)
+            send([(STEP[2], R("bt", 256, 512), R("RB2"), "s1"), (STEP[2], R("pm2"), R("PM2"), "s1")], 2.0)
+        if last:
+            mms(R("B6", 384, 512), [(R("I256"), so), (R("nI"), zo)])
+            act(R("rd"), R("B6", 384, 512))
+            put_days(2, "rd")
+        mms(R("B6", 264, 272), [(one64, R("c26", 0, 8, 1, 64)), (thr0, R("W97", 0, 8))])
+        for (k0, k1) in VCH[t]:
+            tt(R("cmp", 128 * k0, 128 * k1), IND(Zc, R("cu", 8 * k0, 8 * k1)), R("thr", 0, 128 * (k1 - k0)), A.is_gt)
+            line("compare")
+            for k in range(k0, k1):
+                tier_sum(R("B0", k, 264, 33), [(part("cmp", k), R("Wv", 0, 8))])
+        for j, sign in ((0, False), (1, False), (0, True), (2, False), (1, True), (2, True)):
+            k0, k1 = SCH[t][j]
+            n = 128 * (k1 - k0)
+            raw, bank = R("raw", 512 * j, 512 * j + n), R(("B1", "B2", "B7")[j], 0, n)
+            if not sign:
+                act(raw, IND(Zc, R("cu", 8 * k0, 8 * k1)))
+                line("gather")
+                mms(bank, [(R("nI"), R("thr", 0, n)), (R("I"), raw)])
+                continue
+            act(R("cmp", 128 * k0, 128 * k1), bank, F.Sign, bias=-0.5)
+            line("gather")
+            for k in range(k0, k1):
+                tier_sum(R("B0", k, 264, 33), [(one32, R("cS", 0, 8, 1, 32)), (part("cmp", k), R("Ws", 0, 8))])
+        mms(R("B5", 0, 128), [(R("nI"), thr0), (R("I"), zr)])
+        act(R("s33"), R("B5", 0, 128), F.Sign, bias=-0.5)
+        tier_sum(R("B0", 32, 264, 33), [(one32, R("c33", 0, 8, 1, 32)), (R("s33"), R("W33", 0, 8))])
+        mm(R("B5", 128, 256), R("BoR"), R("s33"))
+        act(R("nask"), R("B5", 128, 256), F.Relu, bias=-14.0 * BIG, scale=-BIG)
+        mms(R("B1", 0, 128), [(R("I"), R("bar0")), (R("I"), R("nask"))])
+        act(R("bar"), R("B1", 0, 128))
+        if not last:
+            act(R("sgz"), zr, F.Sign)
+            mms(R("B7", 384, 512), [(R("Up"), R("sgz")), (R("nUp2"), R("sgz"))])
+            tt(R("sec"), R("B7", 384, 512), zr, A.mult)
+            turn1(t + 1, "B5")
+        scan(R("sc"), R("kp", 264 * t, 264 * t + 264), R("B0", 0, 264), A.add, A.min)
+        tt(R("ki"), R("B6", 264, 272), R("sc", 32, 264, 33), A.add)
+        ts(R("km"), R("ki"), (3 << 22) | (W - 1), A.bitwise_and)
+        ts(R("A16"), IND(R("km"), R("ex")), 8192.0, A.min, 2048.0, A.subtract)
+        mms(R("B3", 384, 512), [(R("Up"), so), (R("nE0"), so)])
+        tt(R("B16"), R("B3", 0, 128), R("A16"), A.mult)
+        if not last:
+            mms(R("B3", 256, 384), [(R("Bo"), R("sec")), (R("nI"), bt)])
+        aim, tail = R("B2", 128, 256), R("B2", 240, 256)
+        mm(R("B6", 0, 128), R("A16"), R("I16"))
+        mm(R("B6", 128, 136), R("B16"), R("Q16"))
+        mm(R("B4", 0, 144), R("I16"), R("tri"), True, False)
+        mm(R("B4", 0, 128), R("A16"), R("I16"), False, False)
+        mm(R("B4", 128, 144), R("A16"), R("I16", 112, 128), False, False)
+        mm(R("B4", 0, 144), R("B16"), R("RD"), False, True)
+        act(R("sp"), R("B4", 0, 144), F.Sign, bias=0.5)
+        act(R("sm"), R("B4", 0, 144), F.Sign, bias=-0.5)
+        mm(aim, R("I"), R("off"), True, False)
+        mm(aim, R("A16"), R("I16"), False, False)
+        for q in range(NV):
+            e = R("E", EOFF[q], EOFF[q + 1])
+            ts(e, R("B6", 16 * q + 16, 128), R("B6", 128 + q, 129 + q), A.is_equal)
+            line("equal")
+            if q in (3, NV - 1):
+                wts, src = (R("B4k"), "sp") if q == 3 else (R("nB4k"), "sm")
+                mm(aim, wts, R(src, 0, 128), False, False)
+                mm(tail, wts, R(src, 128, 144), False, False)
+            mm(R("B2", 128 + 16 * q + 16, 256), R("B8k"), e, False, q == NV - 1)
+        ts(R("dU"), R("B6", 128, 136), 2048.0, A.add, float(W - 1), A.min)
+        act(R("zd"), IND(Zc, R("dU")))
+        gone = part("G", t)
+        tt(gone, aim, R("bar"), A.is_lt)
+        if not last:
+            nl = part("NL", t, 144)
+            tt(nl, aim, R("bar0"), A.is_ge)
+            tt(part("wn", t), R("B3", 256, 384), gone, A.mult)
+            send([(STEP[t + 1], nl, part("RN", t), "n%d" % t),
+                  (STEP[t + 1] - STEP[t], part("wn", t), part("WD", t, 256), "w%d" % t)])
+        send([(-STEP[t], gone, part("RG", t), "g%d" % t)])
+        lo = 0 if last else 24 * (t + 1)
+        tt(R("zl"), aim, R("farm"), A.min)
+        scan(R("ll"), R("rsb"), R("zl"), A.add, A.min)
+        ts(R("SL", lo, lo + 8), R("ll", 15, 128, 16), 2048.0, A.add)
+        act(R("ed"), R("zd"), F.Relu, bias=1.0, scale=-1.0)
+        mm(R("B1", 384, 512), R("FstE"), R("ed"))
+        if last:
+            act(R("braw"), bt, bias=256.0, scale=-1.0)
+            act(R("td"), R("zd"), F.Sign)
+            mms(R("B5", 0, 128), [(R("I256"), R("td")), (R("nI"), R("zd"))])
+            act(R("yd"), R("B5", 0, 128))
+        tt(R("fd"), R("B1", 384, 512), R("braw") if last else bt, A.mult)
+        St, Sw = (Yall, Yw) if last else (Zall, Zw)
+        tt(IND(St, R("SL", lo, lo + 8)), R("yd") if last else R("zd"), R("fd"), A.add)
+        cp(zp, IND(Sw, src_list(t)))
+        mm(R("B2", 384, 512), R("TopM"), zp)
+        if not last:
+            tt(R("mx"), R("ll", 15, 128, 16), R("far", 8 * t, 8 * t + 8), A.min)
+            ts(R("SL", lo + 8, lo + 16), R("mx"), 2048.0, A.add)
+            turn2(t + 1, "B1")
+        if t == 0:
+            act(R("nj"), IND(R("NL", 0, 144), R("jx1")))
+            tt(R("zj"), R("B3", 0, 128), R("nj"), A.mult)
+            scan(R("lj"), R("rst", 0, 128), R("zj"), A.mult, A.add)
+            tt(R("ta"), R("lj", 15, 128, 16), R("dd"), A.mult)
+            tt(R("tb"), R("ta"), R("n128", 0, 8), A.add)
+            cp(R("pm2", 0, 8), R("tb"))
+        tt(R("gg"), R("B3", 384, 512), part("RG", t), A.mult)
+        tt(uu, R("B2", 384, 512), R("gg"), A.mult)
+        tt(IND(St, src_list(t)), zp, uu, A.add)
+
+    dma("y", T.y[:], T.Y[:, 0:V], Yw, store=True)
+
+    cnt = {s: 0 for s in ESEM.values()}
     known = {e: {} for e in Q}
     clock = {}
     hist = {}
-    sent = [0]
-    ndma = [0]
-
-    def R(name, lo=0, hi=None, step=1, parts=128):
-        buf, c0, w = WHERE[name]
-        lo, hi = c0 + lo, c0 + (w if hi is None else hi)
-        ap = T[buf][0:parts, lo:hi] if step == 1 else T[buf][0:parts, lo:hi:step]
-        return (ap, [(buf, lo, hi)])
-
-    def IND(win, off):
-        return (win[0].indirect(off[0]), win[1], off[1])
+    dmas = []
 
     def need(e, toks):
         kn = known[e]
@@ -94,578 +628,29 @@ def rank_program(g, core, T, topo):
                 if kn.get(s2, 0) < c2:
                     kn[s2] = c2
 
-    def order(e, reads, writes):
-        toks = []
-        for regs, wr in ((reads, False), (writes, True)):
+    def note(c, tok):
+        for regs, wr in ((c["reads"], False), (c["writes"], True)):
             for (n, lo, hi) in regs:
-                ps = SCRATCH[n][0] == "psum"
-                for (l2, h2, w2, e2, tok) in hist.get(n, []):
-                    if ps and e2 != e:
-                        toks.append(tok)
-                    elif ps and e == "p":
-                        continue
-                    elif lo < h2 and l2 < hi and (wr or w2):
-                        toks.append(tok)
-        need(e, toks)
+                hist.setdefault(n, []).append((lo, hi, wr, c["e"], tok))
 
-    def note(e, reads, writes, tok):
-        clock[tok] = dict(known[e]) if e in known else {}
-        for regs, wr in ((reads, False), (writes, True)):
-            for (n, lo, hi) in regs:
-                hist.setdefault(n, []).append((lo, hi, wr, e, tok))
-
-    def op(e, call, out, ins):
-        reads, writes = [], list(out[1])
-        if len(out) == 3:
-            reads += out[2]
-        for x in ins:
-            if isinstance(x, tuple):
-                reads += x[1]
-                if len(x) == 3:
-                    reads += x[2]
-        order(e, reads, writes)
-        s = ESEM[e]
-        cnt[s] += 1
-        call().then_inc(T.sem[s], 1)
-        note(e, reads, writes, (s, cnt[s]))
-
-    def ap(x):
-        return x[0] if isinstance(x, tuple) else x
-
-    def mset(o, c):
-        op("v", lambda: g.vector.memset(o[0], c), o, [])
-
-    def cp(o, i):
-        op("v", lambda: g.vector.tensor_copy(o[0], i[0]), o, [i])
-
-    def tt(o, a, b, f):
-        op("v", lambda: g.vector.tensor_tensor(o[0], a[0], b[0], f), o, [a, b])
-
-    def ts(o, a, s1, f0, s2=None, f1=None):
-        if f1 is None:
-            op("v", lambda: g.vector.tensor_scalar(o[0], a[0], ap(s1), None, f0), o, [a, s1])
+    for c in calls:
+        if c["kind"] == "land":
+            note(c, (c["lands"], landed[c["lands"]]))
+    for j in plan(calls):
+        c = calls[j]
+        e = c["e"]
+        need(e, [tok for (e2, tok) in clashes(hist, e, c["reads"], c["writes"]) if not e2 == e == "p"])
+        if c["kind"] == "send":
+            c["issue"]()
+            continue
+        if c["kind"] == "dma":
+            tok = ("d%d" % len(dmas), 16)
+            dmas.append(tok)
         else:
-            op("v", lambda: g.vector.tensor_scalar(o[0], a[0], ap(s1), ap(s2), f0, f1), o, [a, s1, s2])
-
-    def scan(o, d0, d1, f0, f1):
-        op("v", lambda: g.vector.tensor_tensor_scan(o[0], d0[0], d1[0], 0.0, f0, f1), o, [d0, d1])
-
-    def act(o, i, fn, bias=0.0, scale=1.0):
-        op("s", lambda: g.scalar.activation(o[0], i[0], fn, bias=bias, scale=ap(scale)), o, [i, scale])
-
-    def mm(o, l, r, start=True, stop=True):
-        op("p", lambda: g.tensor.matmul(o[0], l[0], r[0], start, stop), o, [l, r])
-
-    def iota(o, pat, base, cm, fl=False):
-        if fl:
-            op("g", lambda: g.iota(o[0], pat, base, cm, allow_small_or_imprecise_dtypes=True), o, [])
-        else:
-            op("g", lambda: g.iota(o[0], pat, base, cm), o, [])
-
-    def sel(o, i, pat, cmpop, base, cm, fill=0.0):
-        op("g", lambda: g.affine_select(o[0], i[0], pat, cmpop, fill, base, cm), o, [i])
-
-    def dma(e, o, i, reads, writes):
-        s = "d%d" % ndma[0]
-        ndma[0] += 1
-        order(e, reads, writes)
-        Q[e].dma_start(o, i).then_inc(T.sem[s], 16)
-        note(e, reads, writes, (s, 16))
-        return (s, 16)
-
-    def lanes(d, part, of):
-        en = topo.engines(core, T.cores[(rank + d) % N])
-        n = len(en) // of
-        m = 0
-        for x in en[part * n:(part + 1) * n]:
-            m |= 1 << x
-        return m, n
-
-    def send(items):
-        order("g", [r for it in items for r in it[1][1]], [])
-        if len(items) == 1:
-            d, src, dst, s = items[0]
-            rid, pid, _ = topo.addr(T.cores[(rank + d) % N])
-            m, n = lanes(d, 0, 1)
-            g.remote_dma(dst[0], src[0], T.sem[s], T.sem.sent, pid, rid, m)
-            sent[0] += n
-            return
-        trs = []
-        for j, (d, src, dst, s) in enumerate(items):
-            rid, pid, _ = topo.addr(T.cores[(rank + d) % N])
-            m, n = lanes(d, j, len(items))
-            trs.append(RemoteDMATransfer(dst_ids=[DstId(rid=rid, pnc=pid)], dma_engine_mask=m,
-                                         remote_sem=T.sem[s], src=src[0], dst=dst[0]))
-            sent[0] += n
-        g.remote_dma_fused(trs, local_sem=T.sem.sent)
-
-    arrivals = []
-
-    def arrive(dst, s, d, of):
-        src = T.cores[(rank - d) % N]
-        n = len(topo.engines(src, core)) // of
-        note("r" + s, [], dst[1], (s, n))
-        arrivals.append((s, n))
-
-    def beta(t):
-        return R("PW", 256 * t + 128, 256 * t + 256)
-
-    Wn = {1: "Wn1", 2: "Wn2"}
-    RO = {1: "RO1", 2: "RO2"}
-    XD = {0: "XD0", 1: "XD1"}
-    arrive(beta(0), "b0", STEP[0], 1)
-    for t in range(3):
-        arrive(R("RA", 256 * t, 256 * t + 256), "ma%d" % t, STEP[t], 1)
-        arrive(R("RG", 128 * t, 128 * t + 128), "mg%d" % t, -STEP[t], 1)
-    arrive(R("Wn1", 128, 256), "me", STEP[1], 1)
-    arrive(R("Wn1", 256, 384), "mw0", STEP[1], 1)
-    arrive(R("XD0", 128, 384), "mb0", STEP[0], 1)
-    arrive(R("Wn2", 128, 384), "mw1", STEP[2], 2)
-    arrive(R("XD1", 128, 384), "mb1", STEP[1], 2)
-    for t in range(2):
-        arrive(R(Wn[t + 1], 0, 128), "mn%d" % t, STEP[t + 1] - STEP[t], 2)
-        arrive(R(RO[t + 1]), "mo%d" % t, STEP[t + 1], 2)
-
-    def src_list(t, wide=False):
-        lo = 24 * t + 8
-        return R("SL", lo, lo + (16 if wide else 8))
-
-    dma("s", T.trk[:], T.trucks[:], [], [("trk", 0, 24)])
-    for (lo, hi) in LOADS:
-        dma("y", T.Y[:, lo:hi], T.days[:, lo:hi], [], [("Y", lo, hi)])
-    dma("y", T.cnd[:], T.cand[:], [], [("cnd", 0, 768)])
-
-    mset(R("ones"), 1.0)
-    iota(R("ic", 0, 1), [[0, 1]], 0, 1)
-    sel(R("I"), R("ones"), [[-1, 128]], A.is_equal, 0, 1)
-    sel(R("Bo0"), R("ones"), [[-16, 8], [0, 16]], A.is_ge, 0, 1)
-    iota(R("nL"), [[16, 8]], 0, 0, True)
-    sel(R("Bo"), R("Bo0"), [[16, 8], [0, 16]], A.is_ge, 15, -1)
-    iota(R("ia"), [[1, 128]], 128, -1)
-    act(R("nI"), R("I"), F.Identity, scale=-1.0)
-    act(R("nBo"), R("Bo"), F.Identity, scale=-1.0)
-    sel(R("nUp"), R("nBo"), [[-1, 128]], A.is_equal, -1, 1)
-    iota(R("idd"), [[0, 2], [1, 8]], 0, 0)
-    sel(R("TopM"), R("nUp"), [[-1, 128]], A.not_equal, 0, 1, 1.0)
-    iota(R("jv"), [[0, 2], [1, 128]], 0, 0, True)
-    sel(R("dfa"), R("ones", 0, 99), [[-32, 3], [-1, 33]], A.is_equal, 1, 1)
-    sel(R("dfb"), R("ones", 0, 99), [[-32, 3], [-1, 33]], A.is_equal, 0, 1)
-    sel(R("turn"), R("ones"), [[-1, 16], [-16, 8]], A.is_equal, 0, 1)
-    sel(R("Up2"), R("Bo"), [[-1, 128]], A.is_equal, -2, 1)
-
-    mset(R("dcn", 0, 264, 1, 32), -16.0)
-    mset(R("rst"), 1.0)
-    ts(R("ic", 2, 3), R("ic", 0, 1), 15, A.bitwise_and)
-    mset(R("dcn", 0, 264, 33, 32), 32800.0)
-    mset(R("JT"), 256.0)
-    cp(R("cols", 0, 1), R("ic", 2, 3))
-    mset(R("dcn", KV, 264, 33, 32), -15888.0)
-    mset(R("eight", 0, 128, 1, 32), 8.0)
-    mset(R("c97"), 24832.0)
-    ts(R("cols", 3, 4), R("cols", 0, 1), 15.0, A.is_equal, 15.0, A.mult)
-    mset(R("dcn", 32, 264, 33, 32), 16368.0)
-    ts(R("cols", 1, 2), R("cols", 0, 1), 15.0, A.is_lt)
-    ts(R("cols", 2, 3), R("cols", 0, 1), 0.0, A.is_equal)
-    ts(R("cols", 6, 7), R("cols", 0, 1), 0.0, A.is_equal, -97.0, A.mult)
-    ts(R("cols", 7, 8), R("cols", 0, 1), 0.0, A.is_equal, float(1 << 23), A.mult)
-    ts(R("cols", 4, 5), R("cols", 3, 4), 1.0, A.add, float(UNIT), A.mult)
-    ts(R("cols", 5, 6), R("cols", 3, 4), 1.0, A.add, float(UNIT // 2), A.mult)
-    mset(R("rst", 0, 256, 16), 0.0)
-    mset(R("Z", V, V + S), 0.0)
-    mset(R("Y", V, V + S), 0.0)
-    mset(R("Q0"), -97.0)
-    ts(R("ib"), R("ia"), 15, A.bitwise_and)
-    ts(R("nL"), R("nL"), R("cols", 0, 1), A.add)
-    cp(R("I16"), R("I"))
-    ts(R("mask"), R("ib"), 0.0, A.is_equal)
-    cp(R("trf"), R("trk"))
-    ts(R("ro"), R("trk", 8, 16), float(W), A.subtract)
-    cp(R("SL", 8, 16), R("trk", 0, 8))
-    cp(R("SL", 40, 48), R("trk", 16, 24))
-    grp = R("Bo", 0, 128, 16)
-    act(R("Bq"), R("Bo"), F.Identity, scale=-1.0 / 256)
-    act(R("I15"), R("I"), F.Identity, scale=R("cols", 1, 2))
-    act(R("I256"), R("I"), F.Identity, scale=256.0)
-    act(R("E0"), R("Bo"), F.Identity, scale=R("cols", 2, 3))
-    act(R("Wv"), grp, F.Identity, scale=R("cols", 4, 5))
-    act(R("Ws"), grp, F.Identity, scale=R("cols", 5, 6))
-    act(R("W97"), grp, F.Identity, scale=R("cols", 6, 7))
-    act(R("W23"), grp, F.Identity, scale=R("cols", 7, 8))
-
-    def mirror(c):
-        lo = 512 * c
-        bk = "B%d" % (4 + (c + 1) % 3)
-        mm(R(bk), R("I"), R("t256", lo, lo + 512), True, False)
-        mm(R(bk), R("nI"), R("Y", lo, lo + 512), False, True)
-        act(R("Z", lo, lo + 512), R(bk), F.Identity)
-
-    def marks(j):
-        lo, hi = CH[j]
-        ts(R("t256", lo, hi), R("Y", lo, hi), 256.0, A.mult, 256.0, A.min)
-
-    def clash_rows(q0, q1):
-        for q in range(q0, q1):
-            ts(R("RB", TOFF[q], TOFF[q] + SEG[q]), R("ones16", 0, SEG[q]), R("ngr", q, q + 1), A.mult)
-
-    marks(0)
-    mirror(8)
-    act(R("zd"), IND(R("Z", W, V), R("ro")), F.Identity)
-    act(R("td"), R("zd"), F.Sign)
-    mm(R("B3", 0, 128), R("TopM"), R("td"))
-
-    ts(R("jtmp", 0, 8), R("trf", 0, 8), float(W), A.is_ge)
-    ts(R("jtmp", 8, 16), R("trf", 0, 8), float(W - S), A.subtract)
-    ts(R("jo", 8, 16), R("trf", 8, 16), float(W - S - 640), A.subtract)
-    tt(R("jtmp", 16, 24), R("jtmp", 8, 16), R("nL"), A.subtract)
-    ts(R("jo", 16, 24), R("trf", 8, 16), float(W - S), A.subtract)
-    tt(R("jtmp", 24, 32), R("jtmp", 16, 24), R("jtmp", 0, 8), A.mult)
-    ts(R("jo", 24, 32), R("trf", 16, 24), float(W - S - 640), A.subtract)
-    tt(R("jtmp", 8, 16), R("jtmp", 24, 32), R("nL"), A.add)
-    mset(R("ones16"), 1.0)
-    cp(R("jo", 0, 8), R("jtmp", 8, 16))
-    ts(R("ngr"), grp, -1.0, A.mult)
-    cp(IND(R("JT"), R("jo", 0, 16)), R("jv"))
-    cp(R("m2", 0, 128), R("mask"))
-    cp(R("m2", 128, 256), R("mask"))
-    clash_rows(0, 4)
-    tt(R("fd"), R("B3", 0, 128), R("zd"), A.mult)
-    mm(R("B3", 128, 256), R("Bo"), R("fd"))
-    act(R("PW", 0, 128), R("B3", 128, 256), F.Identity)
-    send([(STEP[1], R("PW", 0, 128), R("Wn1", 128, 256), "me")])
-    marks(1)
-    mirror(0)
-    mirror(1)
-    marks(2)
-    mirror(2)
-    marks(3)
-    clash_rows(4, 8)
-
-    Yw, Zw = R("Y", 0, V), R("Z", 0, V)
-    ts(R("ra"), IND(Yw, src_list(0)), 256.0, A.mult, 256.0, A.min)
-    mm(R("B7", 0, 128), R("TopM"), R("ra"))
-    mirror(3)
-    tt(R("rb"), IND(Yw, src_list(0)), R("ra"), A.subtract)
-    tt(R("rc"), R("B7", 0, 128), R("rb"), A.mult)
-    mm(R("B7", 128, 256), R("Bq"), R("rc"))
-    mirror(4)
-    mirror(5)
-    cp(R("pm16"), R("turn"))
-    mset(R("B0", 32, 264, 33), float(3 << 22))
-    mset(R("c26"), 26880.0)
-    cp(R("p0"), R("B7", 128, 256))
-    send([(STEP[0], R("p0"), beta(0), "b0")])
-    marks(4)
-    mirror(6)
-    mirror(7)
-    sel(R("Q1"), R("Q0"), [[0, 32], [-16, 8]], A.is_ge, 0, 1)
-    sel(R("Q97"), R("Q1"), [[0, 32], [16, 8]], A.is_ge, 15, -1)
-    sel(R("nDn"), R("nBo"), [[-1, 128]], A.is_equal, 1, 1)
-    iota(R("rowj"), [[1, 128]], 128, 0, True)
-    sel(R("FstE"), R("nDn"), [[-1, 128]], A.not_equal, 0, 1, 1.0)
-
-    def step1_a(t):
-        w = 256 if t == 1 else 128
-        act(R("zz", 0, w), IND(Zw, src_list(t, t == 1)), F.Identity)
-        act(R("tt", 0, w), R("zz", 0, w), F.Sign)
-        mm(R("B5", 0, w), R("TopM"), R("tt", 0, w))
-        if t < 2:
-            mm(R("B5", 256, 384), R("nUp"), R("tt", 0, 128), True, False)
-            mm(R("B5", 256, 384), R("Up2"), R("tt", 0, 128), False, True)
-
-    def step1_b(t):
-        w = 256 if t == 1 else 128
-        tt(R("pr", 0, w), R("B5", 0, w), R("zz", 0, w), A.mult)
-        mm(R("B7", 0, 128), R("I"), R("zz", 0, 128), True, False)
-        mm(R("B7", 0, 128), R("nBo"), R("pr", 0, 128), False, True)
-        if t < 2:
-            tt(R("pr", 256, 384), R("B5", 256, 384), R("zz", 0, 128), A.mult)
-
-    def step1_c(t):
-        act(R("rl"), R("B7", 0, 128), F.Relu)
-        mm(R("B7", 128, 256), R("E0"), R("ones"), True, False)
-        mm(R("B7", 128, 256), R("nBo"), R("rl"), False, True)
-        mm(R("B7", 256, 384), R("E0"), R("tt", 0, 128), True, False)
-        mm(R("B7", 256, 384), R("nBo"), R("rl"), False, True)
-        if t < 2:
-            mm(R("B6", 384, 512), R("nBo"), R("pr", 256, 384), True, False)
-            mm(R("B6", 384, 512), R("nBo"), R("pr", 0, 128), False, True)
-        if t == 1:
-            mm(R("B5", 0, 128), R("Bo"), R("pr", 128, 256))
-
-    def step1_d(t):
-        pa = R("PA", 256 * t, 256 * t + 256)
-        act(pa, R("B7", 128, 384), F.Relu)
-        send([(STEP[t], pa, R("RA", 256 * t, 256 * t + 256), "ma%d" % t)])
-        if t == 1:
-            act(R("PW", 256 * t, 256 * t + 128), R("B5", 0, 128), F.Identity)
-
-    def step1_e(t):
-        tt(R("PB", 256 * t, 256 * t + 128), R("B6", 384, 512), R("mask"), A.mult)
-        tt(R("PB", 256 * t + 128, 256 * t + 256), R("B6", 384, 512), R("PA", 256 * t + 128, 256 * t + 256), A.mult)
-        second = (STEP[t], R("PB", 256 * t, 256 * t + 256), R(XD[t], 128, 384), "mb%d" % t)
-        if t == 0:
-            send([second])
-            send([(STEP[1], beta(0), R("Wn1", 256, 384), "mw0")])
-        else:
-            send([second, (STEP[2], R("PW", 256, 512), R("Wn2", 128, 384), "mw1")])
-
-    def step1_ge():
-        mm(R("B7", 384, 512), R("nUp"), R("tt", 0, 128))
-        act(R("geN"), R("B7", 384, 512), F.Identity, bias=-1.0, scale=-1.0)
-
-    def key_turn(t, bank):
-        mm(R(bank, 0, 264), R("eight", 0, 128, 1, 32), R("dcn", 0, 264, 1, 32), True, False)
-        for gg in range(8):
-            mm(R(bank, 33 * gg, 33 * gg + 33), R("X16", gg, 1024, 8, 96), R("dif", 33 * t, 33 * t + 33, 1, 96),
-               False, gg == 7)
-
-    def key_keep(t, bank):
-        act(R("kp", 264 * t, 264 * t + 264), R(bank, 0, 264), F.Identity)
-
-    ts(R("P16"), R("cnd"), 2048.0, A.subtract)
-    for q in range(8):
-        c0 = (q % 4) * 128
-        mm(R("B%d" % (1 + q // 4), c0, c0 + 128, 1, 96), R("P16", q, 768, 8), R("pm16"))
-    tt(R("dif", 0, 99, 1, 96), R("dfa", 0, 99, 1, 96), R("dfb", 0, 99, 1, 96), A.subtract)
-    ts(R("tri"), R("jv", 0, 16), R("cols", 0, 1), A.is_ge, 32768.0, A.mult)
-    mset(R("nil16"), 0.0)
-    cp(R("ex"), R("idd"))
-    mset(R("tri", 15, 16), 6144.0)
-
-    def landing_constants():
-        scan(R("js"), R("rst"), R("jm"), A.mult, A.add)
-        ts(R("n128", 0, 8), R("nL"), 128.0, A.add)
-        ts(R("n128", 8, 16), R("nL"), 128.0, A.add)
-        cp(R("XD0", 0, 128), R("mask"))
-        tt(R("base"), R("js", 15, 256, 16), R("n128"), A.min)
-
-    def relink():
-        scan(R("js", 0, 128), R("rst", 0, 128), R("jm", 0, 128), A.mult, A.add)
-        cp(R("XD1", 0, 128), R("mask"))
-        ts(R("b16", 16, 24), R("nL"), float(V), A.add)
-        tt(R("base", 8, 16), R("base", 8, 16), R("js", 15, 128, 16), A.add)
-        cp(R("b16", 24, 32), R("trf", 16, 24))
-
-    def as_days(o, z, tmark, bank, lo):
-        mm(R(bank, lo, lo + 128), R("I256"), tmark, True, False)
-        mm(R(bank, lo, lo + 128), R("nI"), z, False, True)
-        act(o, R(bank, lo, lo + 128), F.Identity)
-
-    Yall, Zall = R("Y"), R("Z")
-
-    def put_days(t, buf, half):
-        lo = 24 * t + 8 + 4 * half
-        cp(IND(Yall, R("SL", lo, lo + 4)), R(buf, 64 * half, 64 * half + 64))
-
-    for t in range(3):
-        last = t == 2
-        bt = beta(t)
-        mm(R("B3", 128, 384), R("I"), R("c97"), True, False)
-        if t > 0:
-            act(bt, IND(R(Wn[t]), R(RO[t], 0, 8)), F.Identity)
-            tt(R("uu"), R("RG", 128 * (t - 1), 128 * t), R("dl"), A.mult)
-        mm(R("B7", 0, 128), bt, R("I"))
-        tt(R("xm"), R("B7", 0, 128), R("mask"), A.mult)
-        for j in range(4):
-            mm(R("B4", 128 * j, 128 * j + 128), R("I15"), bt)
-        mm(R("B3", 128, 384), R("xm"), R("Q97"), False, True)
-        if t > 0:
-            tt(IND(Zall, src_list(t - 1)), R("zp"), R("uu"), A.add)
-        else:
-            cp(R("X16", 0, 512, 1, 96), R("B1", 0, 512, 1, 96))
-        act(R("thr"), R("B4"), F.Identity)
-        halves = [(0, 128), (128, 256)]
-        for (lo, hi) in halves:
-            tt(R("ci", lo, hi), R("B3", 128 + lo, 128 + hi), R("cnd", 256 * t + lo, 256 * t + hi), A.add)
-        step1_a(t)
-        for (lo, hi) in halves:
-            ts(R("cj", lo, hi), R("ci", lo, hi), W - 1, A.bitwise_and)
-        for (lo, hi) in halves:
-            cp(R("cu", lo, hi), R("cj", lo, hi))
-        Zc = R("Z", 0, W)
-
-        def vchunk(c):
-            k0, k1 = VCH[c]
-            tt(R("cmp", 128 * k0, 128 * k1), IND(Zc, R("cu", 8 * k0, 8 * k1)), R("thr", 0, 128 * (k1 - k0)), A.is_gt)
-
-        def score(ks, wts):
-            for k in range(ks[0], ks[1]):
-                mm(R("B0", k, 264, 33), R("cmp", 128 * k, 128 * k + 128), R(wts))
-
-        def sgather(j):
-            k0, k1 = SCH[j]
-            n = 128 * (k1 - k0)
-            bk = R("B%d" % (1 + j % 2), 0, n)
-            act(R("raw", 512 * j, 512 * j + n), IND(Zc, R("cu", 8 * k0, 8 * k1)), F.Identity)
-            mm(bk, R("nI"), R("thr", 0, n), True, False)
-            mm(bk, R("I"), R("raw", 512 * j, 512 * j + n), False, True)
-
-        def ssign(j):
-            k0, k1 = SCH[j]
-            act(R("cmp", 128 * k0, 128 * k1), R("B%d" % (1 + j % 2), 0, 128 * (k1 - k0)), F.Sign, bias=-0.5)
-
-        vchunk(0)
-        step1_b(t)
-        if t == 0:
-            cp(R("X16", 512, 1024, 1, 96), R("B2", 0, 512, 1, 96))
-            cp(R("dif", 32, 99, 33, 96), R("dfa", 32, 99, 33, 96))
-        sgather(0)
-        step1_c(t)
-        score(VCH[0], "Wv")
-        if t == 0:
-            key_turn(0, "B4")
-        vchunk(1)
-        sgather(1)
-        step1_d(t)
-        score(VCH[1], "Wv")
-        vchunk(2)
-        ssign(0)
-        if not last:
-            step1_e(t)
-        score(VCH[2], "Wv")
-        score(SCH[0], "Ws")
-        sgather(2)
-        vchunk(3)
-        ssign(1)
-        score(VCH[3], "Wv")
-        vchunk(4)
-        score(SCH[1], "Ws")
-        if t == 0:
-            key_keep(0, "B4")
-        ssign(2)
-        score(VCH[4], "Wv")
-        vchunk(5)
-        score(VCH[5], "Wv")
-        score(SCH[2], "Ws")
-        mm(R("B3", 384, 392), R("I"), R("c26"), True, False)
-        mm(R("B3", 384, 392), bt, R("W97"), False, False)
-        mm(R("B3", 384, 392), R("RA", 256 * t, 256 * t + 128), R("W23"), False, True)
-        if t == 0:
-            tt(R("jm"), IND(R("JT"), R("jo", 16, 32)), R("m2"), A.mult)
-        if t == 1:
-            tt(R("jm", 0, 128), IND(R("lrow"), R("jx1")), R("md1"), A.mult)
-        scan(R("sc"), R("kp", 264 * t, 264 * t + 264), R("B0", 0, 264), A.add, A.min)
-        if last:
-            as_days(R("rd"), R("zz", 0, 128), R("tt", 0, 128), "B6", 256)
-        if t > 0:
-            act(R("ra"), IND(Zw, src_list(t - 1)), F.Identity)
-            act(R("rb"), R("ra"), F.Sign)
-        mm(R("B1", 0, 240), R("I16"), R("nil16", 0, 240), True, False)
-        mm(R("B2", 0, 336), R("I16"), R("nil16", 0, 336), True, False)
-        for q in range(8):
-            bk, c0 = SOFF[q]
-            mm(R("B%d" % bk, c0 + SEG[q] - 16, c0 + SEG[q]), R("I16"), R("tri"), False, False)
-        if t == 0:
-            cp(R("Q16", 0, 8), grp)
-        tt(R("ki"), R("B3", 384, 392), R("sc", 32, 264, 33), A.add)
-        if t == 0:
-            cp(R("Q16", 8, 16), grp)
-        ts(R("km"), R("ki"), (3 << 22) | (W - 1), A.bitwise_and)
-        if t == 0:
-            ts(R("n256"), R("nL"), 256.0, A.add)
-        ts(R("A16"), IND(R("km"), R("ex", 0, 8)), 8192.0, A.min, 2048.0, A.subtract)
-        tt(R("B16"), R("A16"), R("mask"), A.mult)
-        for q in range(8):
-            bk, c0 = SOFF[q]
-            mm(R("B%d" % bk, c0, c0 + SEG[q] - 1), R("A16"), R("I16", 0, SEG[q] - 1), False, False)
-        mm(R("B1", 0, 240), R("B16"), R("RB", 0, 240), False, True)
-        mm(R("B2", 0, 336), R("B16"), R("RB", 240, 576), False, True)
-        mm(R("B3", 392, 408), R("B16"), R("Q16"))
-        mm(R("B4", 0, 128), R("I"), R("RA", 256 * t + 128, 256 * t + 256), True, False)
-        if not last:
-            mm(R("B5", 0, 128), R("I"), bt, True, False)
-            mm(R("B5", 0, 128), R("I"), R(XD[t], 256, 384), False, False)
-        if t > 0:
-            as_days(R("rc"), R("ra"), R("rb"), "B6", 128)
-        step1_ge()
-        if t == 0:
-            landing_constants()
-        if t == 1:
-            relink()
-        if last:
-            put_days(2, "rd", 0)
-            act(R("braw"), bt, F.Identity, bias=256.0, scale=-1.0)
-        for q in range(8):
-            bk, c0 = SOFF[q]
-            o, i = R("mn", q, q + 1), R("B%d" % bk, c0, c0 + SEG[q])
-            op("v", lambda: g.vector.tensor_reduce(o[0], i[0], AxisListType.X, A.min, apply_absolute_value=True), o, [i])
-            if q == 4:
-                ts(R("dU"), R("B3", 392, 400), 2048.0, A.add, float(W - 1), A.min)
-        act(R("zd"), IND(Zc, R("dU")), F.Identity)
-        act(R("ed"), R("zd"), F.Relu, bias=1.0, scale=-1.0)
-        if last:
-            ts(R("b16", 32, 40), R("nL"), float(V), A.add)
-            tt(R("Rm", 0, 128), IND(R("mn"), R("ex", 0, 8)), R("mask"), A.min)
-            ts(R("land", 0, 8), R("mn"), 0.0, A.is_gt)
-        else:
-            tt(R("doff", 0, 8), R("n256"), R("base", 8 * t, 8 * t + 8), A.subtract)
-            ts(R("land", 0, 8), R("mn"), 0.0, A.is_gt)
-            ts(R("ta"), R("B3", 392, 408), 2048.0, A.add)
-            tt(R("Rm"), IND(R("land", 0, 8), R("ex")), R(XD[t], 0, 256), A.mult)
-            mm(R("B5", 0, 128), R("Bo"), R("Rm", 128, 256), False, True)
-        mm(R("B4", 0, 128), R("Bo"), R("Rm", 0, 128), False, True)
-        pg = R("PG", 128 * t, 128 * t + 128)
-        act(pg, R("B4", 0, 128), F.Identity)
-        if not last:
-            tt(R("oa"), R("land", 0, 8), R("doff", 0, 8), A.mult)
-            if t == 0:
-                mset(R("PO"), 0)
-            else:
-                ts(R("land", 8, 16), R("mn"), 0.0, A.is_gt)
-            tt(R("ob"), R("oa"), R("base", 8 * t, 8 * t + 8), A.add)
-            pn = R("PN", 128 * t, 128 * t + 128)
-            cp(pn, R("B5", 0, 128))
-            cp(R("PO", 128 * t, 128 * t + 8), R("ob"))
-            send([(STEP[t + 1] - STEP[t], pn, R(Wn[t + 1], 0, 128), "mn%d" % t),
-                  (STEP[t + 1], R("PO", 128 * t, 128 * t + 128), R(RO[t + 1]), "mo%d" % t)])
-        send([(-STEP[t], pg, R("RG", 128 * t, 128 * t + 128), "mg%d" % t)])
-        mm(R("B6", 0, 128), R("FstE"), R("ed"))
-        if last:
-            act(R("td"), R("zd"), F.Sign)
-            as_days(R("yd"), R("zd"), R("td"), "B7", 0)
-        if t == 0:
-            mm(R("B7", 0, 128), R("Bo"), R("Rm", 0, 128))
-            ts(R("b16", 0, 8), R("nL"), float(V), A.add)
-            cp(R("b16", 8, 16), R("trf", 8, 16))
-            mset(R("lrow", 128, 144), 0.0)
-            act(R("lrow", 0, 128), R("B7", 0, 128), F.Identity)
-            ts(R("land", 8, 16), R("mn"), 0.0, A.is_gt)
-        if not last:
-            key_turn(t + 1, "B1")
-            key_keep(t + 1, "B1")
-        w = 8 if last else 16
-        bs = R("b16", 16 * t, 16 * t + w)
-        if last:
-            ts(R("ta", 0, w), R("B3", 392, 392 + w), 2048.0, A.add)
-            put_days(2, "rd", 1)
-        tt(R("tb", 0, w), R("ta", 0, w), bs, A.subtract)
-        if last:
-            put_days(1, "rc", 0)
-        if t == 0:
-            ts(R("jx1"), R("base", 8, 16), 128.0, A.min)
-        tt(R("tc", 0, w), R("tb", 0, w), R("land", 0, w), A.mult)
-        if last:
-            put_days(1, "rc", 1)
-        tt(R("ta", 0, w), R("tc", 0, w), bs, A.add)
-        tt(R("fd"), R("B6", 0, 128), R("braw") if last else bt, A.mult)
-        lo = 0 if last else 24 * (t + 1)
-        cp(R("SL", lo, lo + w), R("ta", 0, w))
-        St, Sw = (Yall, Yw) if last else (Zall, Zw)
-        tt(IND(St, R("SL", lo, lo + 8)), R("yd") if last else R("zd"), R("fd"), A.add)
-        cp(R("zp"), IND(Sw, src_list(t)))
-        mm(R("B6", 128, 256), R("TopM"), R("zp"))
-        if t == 0:
-            tt(R("jg"), R("rowj"), R("mask"), A.mult)
-        if t == 1:
-            put_days(0, "rc", 0)
-        tt(R("dl"), R("B6", 128, 256), R("geN"), A.mult)
-        if t == 0:
-            tt(R("md1"), R("jg"), R("jm", 128, 256), A.subtract)
-        if t == 1:
-            put_days(0, "rc", 1)
-
-    tt(R("uu"), R("RG", 256, 384), R("dl"), A.mult)
-    tt(IND(Yall, src_list(2)), R("zp"), R("uu"), A.add)
-    tok = dma("y", T.y[:], T.Y[:, 0:V], [("Y", 0, V)], [])
-    need("y", [tok])
-    need("g", arrivals + [(s, c) for s, c in cnt.items()] + [("d%d" % i, 16) for i in range(ndma[0] - 1)] + [("sent", sent[0])])
+            cnt[ESEM[e]] += 1
+            tok = (ESEM[e], cnt[ESEM[e]])
+        c["issue"]().then_inc(T.sem[tok[0]], 16 if c["kind"] == "dma" else 1)
+        clock[tok] = dict(known[e])
+        note(c, tok)
+    need("y", dmas[-1:])
+    need("g", list(landed.items()) + list(cnt.items()) + dmas[:-1] + [("sent", sent[0])])

@@ -3,18 +3,25 @@ from concourse.mybir import AluOpType as A, ActivationFunctionType as F
 
 N, W, V, S, K = 8, 4096, 4608, 128, 32
 STEP = (1, 2, 3)
-SCH = [[(4, 8), (8, 12), (12, 15)]] * 3
-VCH = [[(0, 2), (2, 4), (15, 19), (19, 23), (23, 27), (27, 31), (31, 32)]] * 3
+KS = (16, 15, 16)
+SCH = [[(4, 8), (8, 12), (12, _k)] for _k in KS]
+VCH = [[(0, 2), (2, 4), (_k, _k + 4), (_k + 4, _k + 8), (_k + 8, _k + 12), (_k + 12, 31), (31, 32)] for _k in KS]
 UNIT = 1 << 18
 BIG, OFF = float(1 << 24), float(1 << 19)
+CUT = 64
 NV = 6
 EOFF = [0, 112, 208, 288, 352, 400, 432]
-LOADS = [(4096, 4608), (0, 2048), (2048, 3072), (3072, 4096)]
-ZBANK = ("B0", "B5", "B6", "B2", "B5", "B6", "B4", "B1", "B4")
-ZADD = (6, 7)
+DSEG = [(0, 128, 0)]
+for _q in range(NV, 7):
+    DSEG.append((DSEG[-1][1], DSEG[-1][1] + 112 - 16 * _q, 16 * _q + 16))
+DW = DSEG[-1][1]
+LOADS = [(0, 2048), (2048, 4608)]
+ZBANK = ("B0", "B5", "B6", "B2", "B5", "B6", "B4", "B1", "B2")
+ZORDER = (0, 1, 2, 3, 6, 7, 4, 5, 8)
+ZADD = (7, 8)
 
-CYCLE, LINK, GATHER, SCATTER = 0.00093, 0.15, 1.56, 3.8
-ISSUE, FIRST, HOP, HOP2, DMA0, ROW, RATE = 0.3, 2.3, 1.6, 1.85, 1.6, 0.02, 20000.0
+CYCLE, LINK, GATHER, SCATTER, SCALAR = 0.00093, 0.15, 1.56, 3.8, 1.06
+ISSUE, FIRST, HOP, HOP2, DMA0, ROW, RATE = 0.6, 2.3, 1.65, 1.9, 1.75, 0.02, 20000.0
 
 bf, f32, i32, u16, f16 = "bfloat16", "float32", "int32", "uint16", "float16"
 SIZE = {bf: 2, f32: 4, i32: 4, u16: 2, f16: 2}
@@ -22,16 +29,15 @@ SCRATCH = {}
 WHERE = {}
 for _n, _w, _d in [
     ("Y", V + S, bf), ("Z", V + S, bf), ("t256", V, bf), ("trk", 24, i32), ("cnd", 768, i32),
-    ("I16", 128, f16), ("Q16", 8, f16), ("pm16", 128, f16), ("RD", 144, f16), ("tri", 144, f16),
-    ("dif", 132, f16), ("P16", 768, f16), ("X", 768, f16),
-    ("ic", 16, i32), ("ex", 8, u16), ("kp", 792, f32), ("JT", V + 512, bf), ("jo", 32, u16),
+    ("P16", 768, f16), ("X", 768, f16),
+    ("ic", 16, i32), ("ex", 8, u16), ("kp", 792, f32), ("JT", V + 512, bf), ("jo", 16, u16),
     ("jx1", 8, u16), ("SL", 72, u16), ("dU", 8, u16),
-    ("rc0", 128, bf), ("RC", 128, bf), ("zz", 512, bf), ("ZR", 384, bf), ("res1", 128, bf), ("RS1", 128, bf),
-    ("bt", 512, bf), ("BT1", 128, bf), ("RB2", 256, bf), ("pm1", 128, u16), ("PM1", 128, u16), ("pm2", 256, u16),
-    ("PM2", 256, u16), ("G", 384, bf), ("RG", 384, bf), ("NL", 288, bf), ("RN", 256, bf), ("wn", 256, bf),
-    ("WD", 512, bf), ("q", 256, bf), ("cu", 256, u16),
-    ("thr", 512, bf), ("cmp", 4096, bf), ("raw", 1536, bf), ("sc", 264, f32), ("ki", 8, i32), ("km", 8, i32),
-    ("A16", 128, f16), ("B16", 128, f16), ("E", 432, bf), ("sp", 144, bf), ("sm", 144, bf),
+    ("rc0", 128, bf), ("RC", 128, bf), ("zz", 512, bf), ("ZR", 384, bf), ("bt", 640, bf), ("RB", 512, bf),
+    ("pm1", 8, u16), ("PM1", 8, u16), ("pm2", 8, u16), ("PM2", 8, u16),
+    ("G", 384, bf), ("RG", 384, bf), ("NL", 288, bf), ("RN", 256, bf), ("wn", 256, bf),
+    ("WD", 288, bf), ("q", 256, bf), ("cu", 256, u16),
+    ("thr", 512, bf), ("cmp", 4096, bf), ("raw", 1536, bf), ("sc", 264, i32), ("km", 8, i32),
+    ("A16", 128, f16), ("B16", 128, f16), ("E", 432, bf), ("sp", DW, bf), ("sm", DW, bf),
 ]:
     SCRATCH[_n] = ("sbuf", [128, _w], _d)
     WHERE[_n] = (_n, 0, _w)
@@ -45,13 +51,12 @@ def _pack(buf, dt, items):
     SCRATCH[buf] = ("sbuf", [128, c], dt)
 
 
-_pack("small", f32, [("c15", 8), ("nL", 8), ("trf", 24), ("n128", 16), ("base", 16), ("far", 16), ("mx", 8),
-                     ("dd", 8), ("ta", 8), ("tb", 8), ("row", 128), ("farm", 128), ("zl", 128), ("ll", 128)])
+_pack("small", f32, [("c15", 8), ("nL", 8), ("far", 16), ("mx", 8), ("farm", 128), ("ll", 128)])
 _pack("konst", bf, [(_n, 128) for _n in (
     "ones", "G16", "R16", "I", "nI", "I256", "I15", "m4k", "Bo", "nBo", "BoR", "BoC", "nE0", "bar0", "Up",
-    "nUp", "nUp2", "nDn", "TopM", "FstE", "mask", "turn", "cst", "B8k", "B4k", "nB4k", "off", "rsb")]
-      + [("Q97", 256), ("jv", 256), ("rst", 256), ("m2", 256), ("dcn", 272), ("dfa", 144), ("dfb", 144),
-         ("dfc", 144), ("cols", 16), ("Wv", 16), ("Ws", 16), ("W97", 16), ("W33", 16), ("c26", 16), ("c33", 16),
+    "nUp", "nUp2", "nDn", "TopM", "FstE", "mask", "turn", "B4k", "off", "jn", "rst")]
+      + [("Q97", 256), ("cst", 192), ("dcn", 272), ("dfa", 144), ("dfb", 144), ("RD", DW), ("tri", DW),
+         ("dif", 144), ("cols", 16), ("Wv", 16), ("Ws", 16), ("W97", 16), ("W33", 16), ("c26", 16), ("c33", 16),
          ("cS", 16)])
 _pack("work", bf, [(_n, 128) for _n in (
     "s33", "sgz", "nask", "bar", "sec", "gg", "ed", "zd", "td", "yd", "fd", "braw", "ra", "rb", "rd", "re0",
@@ -61,7 +66,7 @@ for _b in range(8):
     SCRATCH["B%d" % _b] = ("psum", [128, 512], f32)
     WHERE["B%d" % _b] = ("B%d" % _b, 0, 512)
 
-ARR = ["b0", "me", "z0", "z1", "z2", "s0", "s1", "g0", "g1", "g2", "n0", "n1", "w0", "w1"]
+ARR = ["b0", "me", "p2", "z0", "z1", "z2", "s0", "s1", "g0", "g1", "g2", "n0", "n1", "w0", "w1"]
 SEMAPHORES = ["ev", "es", "ep", "eg", "sent"] + ["d%d" % _i for _i in range(10)] + ARR
 
 
@@ -72,7 +77,7 @@ def clashes(hist, e, reads, writes):
             ps = SCRATCH[n][0] == "psum"
             for (l2, h2, w2, e2, tok) in hist.get(n, []):
                 if (ps and (e2 != e or e == "p")) or (lo < h2 and l2 < hi and (wr or w2)):
-                    out.append((e2, tok))
+                    out.append((e2, tok, not e2 == e == "p"))
     return out
 
 
@@ -83,11 +88,11 @@ def plan(calls):
             sender[s] = j
     for j, c in enumerate(calls):
         pre = {}
-        for (e2, i) in clashes(hist, c["e"], c["reads"], c["writes"]):
+        for (e2, i, wait) in clashes(hist, c["e"], c["reads"], c["writes"]):
             if e2 == "r":
                 pre[sender[i]] = max(pre.get(sender[i], 0.0), calls[sender[i]]["hop"])
             elif not c["kind"] == calls[i]["kind"] == "sum":
-                pre[i] = max(pre.get(i, 0.0), 0.0 if e2 == c["e"] == "p" else LINK)
+                pre[i] = max(pre.get(i, 0.0), LINK if wait else 0.0)
         if c["kind"] == "send" and j > min(sender.values()):
             pre.setdefault(min(sender.values()), 0.0)
         if c["line"] in last:
@@ -123,6 +128,9 @@ def plan(calls):
         lane.sort()
         start[j] = t
     return sorted(start, key=lambda x: (ready[x] if calls[x]["lead"] else start[x], start[x], x))
+
+
+ORDER = []
 
 
 def rank_program(g, core, T, topo):
@@ -163,6 +171,8 @@ def rank_program(g, core, T, topo):
             cost = max(min(64, ins[0][3]), out[3]) * CYCLE / 2
         elif e == "g":
             cost = 0.18 + 2 * out[3] * CYCLE
+        if e == "s":
+            cost *= SCALAR
         call(e, issue, out[2] + [r for x in ins for r in x[1] + x[2]], out[1], cost)
 
     def ap(x):
@@ -191,7 +201,7 @@ def rank_program(g, core, T, topo):
         op("v", lambda: g.vector.tensor_tensor_scan(o[0], d0[0], d1[0], 0.0, f0, f1), o, [d0, d1], wide(o, d0, d1))
 
     def act(o, i, fn=F.Identity, bias=0.0, scale=1.0):
-        op("s", lambda: g.scalar.activation(o[0], i[0], fn, bias=bias, scale=ap(scale)), o, [i, scale], 1.0)
+        op("s", lambda: g.scalar.activation(o[0], i[0], fn, bias=ap(bias), scale=ap(scale)), o, [i, scale, bias], 1.0)
 
     def mm(o, l, r, start=True, stop=True):
         op("p", lambda: g.tensor.matmul(o[0], l[0], r[0], start, stop), o, [l, r], 1.0)
@@ -259,15 +269,15 @@ def rank_program(g, core, T, topo):
         return R(name, w * t, w * t + 128)
 
     arrive([R("RC")], "b0")
-    arrive([R("RS1")], "me")
-    arrive([R("BT1"), R("PM1")], "s0")
-    arrive([R("RB2"), R("PM2")], "s1")
+    arrive([R("PM1")], "me")
+    arrive([R("PM2")], "p2")
     for t in range(3):
         arrive([part("ZR", t)], "z%d" % t)
         arrive([part("RG", t)], "g%d" % t)
     for t in range(2):
+        arrive([R("RB", 256 * t, 256 * t + 256)], "s%d" % t)
         arrive([part("RN", t)], "n%d" % t)
-        arrive([part("WD", t, 256)], "w%d" % t)
+        arrive([part("WD", t, 144)], "w%d" % t)
 
     def src_list(t):
         return R("SL", 24 * t + 8, 24 * t + 16)
@@ -278,12 +288,13 @@ def rank_program(g, core, T, topo):
         act(o, R("ones", 0, o[3], 1, *pp), scale=c)
 
     dma("s", T.trk[:], T.trucks[:], R("trk"))
+    soon(2.0)
     for (lo, hi) in LOADS:
         dma("y", T.Y[:, lo:hi], T.days[:, lo:hi], R("Y", lo, hi))
-    dma("y", T.cnd[:, 0:256], T.cand[:, 0:256], R("cnd", 0, 256))
+    dma("y", T.cnd[:], T.cand[:], R("cnd"))
 
     tier, yard, bars = (R("cols", j, j + 1) for j in range(3))
-    c15, wcol, nm0, wc0 = (R("c15", j, j + 1) for j in range(4))
+    c15, wcol, nm0 = (R("c15", j, j + 1) for j in range(3))
     grp = R("Bo", 0, 128, 16)
     one32, one64 = R("ones", 0, 128, 1, 32), R("ones", 0, 128, 1, 64)
     diag = [[-1, 128]]
@@ -292,28 +303,25 @@ def rank_program(g, core, T, topo):
     sel(R("I"), R("ones"), diag, A.is_equal, 0, 1)
     iota(R("G16"), [[1, 8], [0, 16]], 0, 0)
     iota(R("R16"), [[0, 8], [1, 16]], 0, 0)
-    iota(R("jv", 0, 128), [[1, 128]], 0, 0)
+    iota(R("jn"), [[1, 128]], -128, 0)
     soon(12.0)
-    iota(R("ta"), [[16, 8]], 0, 0)
+    iota(R("nL"), [[16, 8]], V - 2048, 0)
     sel(R("turn"), R("ones"), [[-1, 16], [-16, 8]], A.is_equal, 0, 1)
     ts(R("ic", 2, 3), R("ic", 0, 1), 15, A.bitwise_and)
     ts(R("ic", 3, 4), R("ic", 0, 1), 4, A.arith_shift_right)
     cp(R("cols", 0, 2), R("ic", 2, 4))
     ts(R("Bo"), R("G16"), yard, A.is_equal)
     ts(R("mask"), R("R16"), tier, A.is_equal)
-    ts(R("nL"), R("ta"), tier, A.add)
     ts(c15, tier, 15.0, A.is_lt)
-    ts(wc0, tier, 15.0, A.is_equal, 15.0 * UNIT, A.mult)
-    ts(wcol, wc0, float(UNIT), A.add)
     ts(nm0, tier, 0.0, A.is_equal, -1.0, A.mult)
-    ts(bars, c15, 38912.0, A.mult, 6144.0, A.subtract)
-    mset(R("rst"), 1.0)
-    mset(R("rst", 0, 256, 16), 0.0)
+    act(wcol, c15, scale=-15.0 * UNIT, bias=16.0 * UNIT)
+    act(bars, c15, scale=38912.0, bias=-6144.0)
+    act(R("rst"), R("R16"), F.Sign)
     for name, src, scale in [("nI", "I", -1.0), ("m4k", "I", -4096.0), ("I256", "I", 256.0), ("I15", "I", c15),
                              ("nBo", "Bo", -1.0), ("BoC", "Bo", 1.0), ("BoR", "Bo", c15), ("nE0", "Bo", nm0),
-                             ("B8k", "Bo", 8192.0), ("B4k", "Bo", 4096.0), ("nB4k", "Bo", -4096.0)]:
+                             ("B4k", "Bo", 4096.0)]:
         act(R(name), R(src), scale=scale)
-    mset(R("BoC", 15, 128, 16), 0.0)
+    act(R("BoC", 15, 128, 16), grp, scale=0.0)
     sel(R("nUp"), R("nBo"), diag, A.is_equal, -1, 1)
     sel(R("nUp2"), R("nBo"), diag, A.is_equal, -2, 1)
     sel(R("nDn"), R("nBo"), diag, A.is_equal, 1, 1)
@@ -330,62 +338,50 @@ def rank_program(g, core, T, topo):
     act(R("W33", 0, 8), R("BoR", 0, 128, 16), scale=BIG / 2)
     act(R("B3", 0, 128), R("mask"))
     for h in range(2):
-        act(R("n128", 8 * h, 8 * h + 8), R("nL"), bias=128.0)
-        fill("cst", (16384.0, 968.0)[h], h=h)
+        fill("cst", (16384.0, 968.0)[h], 0, 128, h)
+        fill("cst", (16384.0, 968.0)[h], 128, 192, h)
         fill("c26", (712.0, -65536.0)[h], 0, 8, h)
-        fill("WD", 0.0, 256 * h + 128, 256 * h + 256)
+        fill("WD", 0.0, 144 * h + 128, 144 * h + 144)
     fill("cS", 31.0 * W, 0, 8, 0)
-    fill("c33", 15.0 * UNIT, 0, 8, 0)
+    fill("c33", 14.75 * UNIT, 0, 8, 0)
     fill("Z", 0.0, V, V + S)
     fill("Y", 0.0, V, V + S)
     fill("NL", 0.0, 128, 144)
-    act(R("jv", 128, 256), R("jv", 0, 128))
-    soon(12.0)
     act(R("off"), R("mask"), scale=-OFF, bias=OFF)
     act(R("bar0"), R("mask"), scale=-OFF, bias=OFF + W)
-    act(R("rsb"), R("rst", 0, 128), scale=-BIG, bias=BIG)
-    act(R("row"), R("jv", 0, 128), bias=float(V - 2048))
-    tt(R("farm"), R("row"), R("off"), A.add)
-    cp(R("I16"), R("I"))
-    cp(R("Q16"), grp)
-    cp(R("pm16"), R("turn"))
-    cp(R("ex"), R("jv", 0, 8))
+    fill("farm", -BIG)
+    act(R("farm", 0, 128, 16), R("nL"), bias=tier)
+    ts(R("ex"), R("jn", 0, 8), 128.0, A.add)
     ts(R("tri", 0, 128), R("R16"), tier, A.is_le, bars, A.mult)
-    mset(R("tri", 128, 144), 0.0)
-    ts(R("RD", 0, 128), R("Bo"), c15, A.mult, -1.0, A.mult)
-    ts(R("RD", 128, 144), R("ones", 0, 16), R("nBo", 16 * NV, 16 * NV + 1), A.mult)
+    fill("tri", 0.0, 128, DW)
+    act(R("RD", 0, 128), R("BoR"), scale=-1.0)
+    for (c0, c1, first) in DSEG[1:]:
+        act(R("RD", c0, c1), R("nBo", first - 16, first))
+        for c in range(c0 + 16, c1, 16):
+            act(R("RD", c, c + 16), R("nBo", first - 16, first))
     fill("dfa", 1.0, 0, 128)
     fill("dfa", 1.0, 128, 132)
     sel(R("dfb", 0, 132), R("dfa", 0, 132), [[-32, 4], [-1, 33]], A.is_equal, 1, 1)
-    sel(R("dfc", 0, 132), R("dfb", 0, 132), [[-32, 4], [-1, 33]], A.not_equal, 0, 1, -1.0)
-    cp(R("dif"), R("dfc", 0, 132))
-    ts(R("dif", 32, 132, 33), R("dif", 32, 132, 33), 0.0, A.max)
+    sel(R("dif", 0, 132), R("dfb", 0, 132), [[-32, 4], [-1, 33]], A.not_equal, 0, 1, -1.0)
+    act(R("dif", 32, 132, 33), R("dfb", 32, 132, 33))
     mset(R("dcn", 0, 264, 1, 32), -128.0)
-    mset(R("dcn", 0, 264, 33, 32), float(UNIT))
-    mset(R("dcn", 32, 264, 33, 32), 69632.0)
+    act(R("dcn", 0, 264, 33, 32), R("ones", 0, 8, 1, 32), scale=float(UNIT))
+    act(R("dcn", 32, 264, 33, 32), R("ones", 0, 8, 1, 32), scale=69632.0)
 
     cp(R("SL", 8, 16), R("trk", 0, 8))
-    cp(R("SL", 40, 48), R("trk", 16, 24))
-    cp(R("trf"), R("trk"))
-    act(R("far"), R("trf", 8, 24), bias=-2048.0)
-    cp(R("jo", 0, 8), R("trk", 0, 8))
-    ts(R("jo", 8, 16), R("trk", 8, 16), 512.0, A.add)
-    ts(R("jo", 16, 24), R("trk", 8, 16), float(W), A.subtract)
-    ts(R("jo", 24, 32), R("trk", 16, 24), float(W - 512), A.subtract)
+    ts(R("far"), R("trk", 8, 24), 2048.0, A.subtract)
+    ts(R("jo"), R("trk", 8, 24), float(W), A.subtract)
     for h in range(2):
-        mset(R("JT", W + 512 * h, V + 512 * h), 256.0)
-    for h in range(4):
-        cp(IND(R("JT"), R("jo", 4 * h, 4 * h + 4)), R("jv", 64 * h, 64 * h + 64))
-    for h in range(2):
-        jm, js = R("jm", 128 * h, 128 * h + 128), R("js", 128 * h, 128 * h + 128)
-        tt(jm, IND(R("JT", W, V + 512), R("jo", 16 + 8 * h, 24 + 8 * h)), R("mask"), A.mult)
-        scan(js, R("rst", 0, 128), jm, A.mult, A.add)
-        tt(R("base", 8 * h, 8 * h + 8), R("js", 128 * h + 15, 128 * h + 128, 16), R("n128", 0, 8), A.min)
-    mset(R("pm1"), 0)
-    mset(R("pm2"), 0)
-    cp(R("pm1", 0, 8), R("base", 0, 8))
-    ts(R("jx1"), R("base", 8, 16), 128.0, A.min)
-    tt(R("dd"), R("base", 8, 16), R("n128", 0, 8), A.subtract)
+        table = R("JT", W + 512 * h, V + 512 * h)
+        mset(table, 0.0)
+        if h == 0:
+            cp(IND(R("JT", 0, V), src_list(0)), R("jn"))
+        else:
+            for c in (0, 4):
+                cp(IND(table, R("jo", c, c + 4)), R("jn", 16 * c, 16 * c + 64))
+        tt(part("jm", h), IND(table, R("jo", 8 * h, 8 * h + 8)), R("mask"), A.mult)
+        scan(part("js", h), R("rst"), part("jm", h), A.mult, A.add)
+        ts(R(("pm1", "jx1")[h], 0, 8), R("js", 128 * h + 15, 128 * h + 128, 16), 128.0, A.add)
 
     Yw, Zw, Zc, Yall, Zall = R("Y", 0, V), R("Z", 0, V), R("Z", 0, W), R("Y"), R("Z")
 
@@ -395,14 +391,12 @@ def rank_program(g, core, T, topo):
         mms(bank, [(R("I"), sign), (R("nUp"), sign)])
         tt(out, bank, rev, A.mult)
 
-    tops(R("res1"), IND(R("Y", W, V), R("jo", 16, 24)), R("s1"), R("r1"), R("B7", 0, 128))
-    send([(STEP[1], R("res1"), R("RS1"), "me")])
+    send([(STEP[1], R("pm1"), R("PM1"), "me")])
     tops(R("rc0"), IND(Yw, src_list(0)), part("tt", 0), R("rb"), R("B7", 128, 256))
     send([(STEP[0], R("rc0"), R("RC"), "b0")])
-    dma("y", T.cnd[:, 256:768], T.cand[:, 256:768], R("cnd", 256, 768), behind=R("RC")[1])
     tt(part("zz", 0), R("rb"), part("tt", 0), A.mult)
     send([(STEP[0], part("zz", 0), part("ZR", 0), "z0")])
-    for c in (8, 0, 1, 2, 3, 6, 7, 4, 5):
+    def mirror(c):
         y, z, m, bank = (R("Y", 512 * c, 512 * c + 512), R("Z", 512 * c, 512 * c + 512),
                          R("t256", 512 * c, 512 * c + 512), R(ZBANK[c]))
         ts(m, y, 256.0, A.mult, 256.0, A.min)
@@ -414,6 +408,9 @@ def rank_program(g, core, T, topo):
             act(z, bank)
             line("mirror")
 
+    for c in ZORDER:
+        mirror(c)
+
     def narrow(t):
         for lo in range(256 * t, 256 * t + 256, 128):
             ts(R("P16", lo, lo + 128), R("cnd", lo, lo + 128), 2048.0, A.subtract)
@@ -421,10 +418,10 @@ def rank_program(g, core, T, topo):
     def turn1(t, bank):
         for q in range(8):
             a, c0 = q // 2, 256 + (q % 2) * 128
-            mm(R(bank, c0, c0 + 128, 1, 32 * a + 32, 32 * a), R("P16", 256 * t + q, 256 * t + 256, 8), R("pm16"))
+            mm(R(bank, c0, c0 + 128, 1, 32 * a + 32, 32 * a), R("P16", 256 * t + q, 256 * t + 256, 8), R("turn"))
         for lo in (0, 128):
             cp(R("X", 256 * t + lo, 256 * t + lo + 128), R(bank, 256 + lo, 384 + lo))
-            soon(0.0 if t else 4.0)
+            soon(0.0 if t else 1.0)
 
     def turn2(t, bank):
         mm(R(bank, 0, 264), one32, R("dcn", 0, 264, 1, 32), True, False)
@@ -437,76 +434,77 @@ def rank_program(g, core, T, topo):
     for t in range(3):
         narrow(t)
 
-    def put_days(t, buf):
+    def put_days(lo, z, dz, bank, buf):
+        mms(R(bank, 0, 128), [(R("I"), z), (R("I"), dz)])
+        act(R("ra"), R(bank, 0, 128), F.Sign)
+        mms(R(bank, 128, 256), [(R("I256"), R("ra")), (R("nI"), z), (R("nI"), dz)])
+        act(R(buf), R(bank, 128, 256))
         for h in range(2):
-            lo = 24 * t + 8 + 4 * h
-            cp(IND(Yall, R("SL", lo, lo + 4)), R(buf, 64 * h, 64 * h + 64))
+            cp(IND(Yall, R("SL", lo + 4 * h, lo + 4 * h + 4)), R(buf, 64 * h, 64 * h + 64))
 
-    LA = [R("B5", 0, 128), R("B5", 128, 256)]
-    LB = [R("B6", 0, 128), R("B0", 264, 392)]
+    LISTS = [(0, CUT, R("B5", 0, CUT), R("B6", 0, CUT)),
+             (CUT, 256, R("B1", 0, 256 - CUT), R("B0", 264, 520 - CUT))]
 
     for t in range(3):
         last = t == 2
-        bt = R("bt", (0, 384, 128)[t], (0, 384, 128)[t] + 128)
+        bt = part("bt", (1, 3, 4)[t])
         zo, zr, so, zp, uu = part("zz", t), part("ZR", t), part("tt", t), part("zp", t), part("uu", t)
         thr0 = R("thr", 0, 128)
-        mm(R("B5", 0, 256), R("I16"), R("P16", 256 * t, 256 * t + 256), True, False)
-        for h in range(2):
-            mm(LB[h], R("I16"), R("P16", 256 * t + 128 * h, 256 * t + 128 * h + 128), True, False)
-            mm(LB[h], one64, R("cst", 0, 128, 1, 64), False, False)
+        for (lo, hi, la, lb) in LISTS:
+            p16 = R("P16", 256 * t + lo, 256 * t + hi)
+            mm(la, R("I"), p16, True, False)
+            mm(lb, R("I"), p16, True, False)
+            mm(lb, one64, R("cst", 0, hi - lo, 1, 64), False, False)
         if t == 0:
             terms = [R("RC")]
             mm(R("B7", 0, 128), R("RC"), R("Bo"))
             mm(R("B4", 0, 128), R("BoC"), R("RC"))
         else:
-            res, btp = (R("RS1"), R("BT1")) if t == 1 else (R("RB2", 0, 128), R("RB2", 128, 256))
             rn, zq, uq = part("RN", t - 1), part("zp", t - 1), part("uu", t - 1)
-            terms = [btp, R("t3"), R("t2")]
-            mms(R("B3", 128, 256), [(R("Bo"), res), (R("nI"), btp)])
+            terms = [btp, R("t2"), R("t3")]
+            tt(R("t2"), IND(R("WD", 144 * (t - 1), 144 * t), R("PM%d" % t, 0, 8)), rn, A.mult)
+            line("start")
             tt(R("t3"), R("B3", 128, 256), rn, A.mult)
-            tt(R("t2"), IND(R("WD", 256 * (t - 1), 256 * t), R("PM%d" % t, 0, 8)), rn, A.mult)
+            line("start")
+            tt(R("gg"), R("B3", 384, 512), part("RG", t - 1), A.mult)
+            line("start")
+            tt(uq, R("B2", 384, 512), R("gg"), A.mult)
+            line("start")
             mms(R("B7", 0, 128), [(x, R("I")) for x in terms])
             mms(R("B4", 0, 128), [(R("I15"), x) for x in terms])
         tt(R("xm"), R("B7", 0, 128), R("mask"), A.mult)
+        line("start")
+        if t > 0:
+            tt(IND(Zall, src_list(t - 1)), zq, uq, A.add)
+            line("start")
         act(thr0, R("B4", 0, 128))
         act(R("thr", 128, 256), thr0)
-        act(R("thr", 256, 512), R("thr", 0, 256))
-        mm(R("B5", 0, 256), R("xm"), R("Q97"), False, True)
-        for h in range(2):
-            q = R("q", 128 * h, 128 * h + 128)
-            mm(LB[h], R("xm"), R("Q97", 128 * h, 128 * h + 128), False, False)
-            act(q, LA[h], bias=135.0 + 513.0 / 8192, scale=1.0 / W)
-            mm(LB[h], R("m4k"), q, False, True)
-            cp(R("cu", 128 * h, 128 * h + 128), LB[h])
+        sel(R("thr", 256, 512), R("thr", 0, 256), [[0, 256]], A.is_ge, 0, 0)
+        line("copy")
+        for (lo, hi, la, lb) in LISTS:
+            q = R("q", lo, hi)
+            mm(la, R("xm"), R("Q97", lo, hi), False, True)
+            mm(lb, R("xm"), R("Q97", lo, hi), False, False)
+            act(q, la, bias=135.0 + 513.0 / 8192, scale=1.0 / W)
+            mm(lb, R("m4k"), q, False, True)
+        cp(R("cu", 0, CUT), LISTS[0][3])
         mms(R("B4", 128, 256), [(R("Bo") if t == 0 else R("I"), x) for x in terms])
         act(bt, R("B4", 128, 256))
         if t == 0:
-            send([(STEP[1], bt, R("BT1"), "s0"), (STEP[1], R("pm1"), R("PM1"), "s0")], 4.0)
             turn1(0, "B4")
             turn2(0, "B6")
         else:
             act(zo, IND(Zw, src_list(t)))
             send([(STEP[t], zo, zr, "z%d" % t)], 2.5)
+            line("copy")
             act(so, zo, F.Sign)
-            mms(R("B7", 0, 128), [(R("I"), zq), (R("I"), uq)])
-            act(R("ra"), R("B7", 0, 128), F.Sign)
-            mms(R("B7", 128, 256), [(R("I256"), R("ra")), (R("nI"), zq), (R("nI"), uq)])
-            act(R("re%d" % (t - 1)), R("B7", 128, 256))
-            put_days(t - 1, "re%d" % (t - 1))
-        if t == 1:
-            act(part("zz", 3), IND(Zw, R("SL", 40, 48)))
-            act(part("tt", 3), part("zz", 3), F.Sign)
-            mm(R("B4", 256, 384), R("TopM"), part("tt", 3))
-            tt(R("bt", 256, 384), R("B4", 256, 384), part("zz", 3), A.mult)
-            send([(STEP[2], R("bt", 256, 512), R("RB2"), "s1"), (STEP[2], R("pm2"), R("PM2"), "s1")], 2.0)
-        if last:
-            mms(R("B6", 384, 512), [(R("I256"), so), (R("nI"), zo)])
-            act(R("rd"), R("B6", 384, 512))
-            put_days(2, "rd")
         mms(R("B6", 264, 272), [(one64, R("c26", 0, 8, 1, 64)), (thr0, R("W97", 0, 8))])
         for (k0, k1) in VCH[t]:
             tt(R("cmp", 128 * k0, 128 * k1), IND(Zc, R("cu", 8 * k0, 8 * k1)), R("thr", 0, 128 * (k1 - k0)), A.is_gt)
             line("compare")
+            if k0 == 0:
+                cp(R("cu", CUT, 256), LISTS[1][3])
+                line("compare")
             for k in range(k0, k1):
                 tier_sum(R("B0", k, 264, 33), [(part("cmp", k), R("Wv", 0, 8))])
         for j, sign in ((0, False), (1, False), (0, True), (2, False), (1, True), (2, True)):
@@ -524,46 +522,61 @@ def rank_program(g, core, T, topo):
                 tier_sum(R("B0", k, 264, 33), [(one32, R("cS", 0, 8, 1, 32)), (part("cmp", k), R("Ws", 0, 8))])
         mms(R("B5", 0, 128), [(R("nI"), thr0), (R("I"), zr)])
         act(R("s33"), R("B5", 0, 128), F.Sign, bias=-0.5)
+        soon(0.6)
         tier_sum(R("B0", 32, 264, 33), [(one32, R("c33", 0, 8, 1, 32)), (R("s33"), R("W33", 0, 8))])
         mm(R("B5", 128, 256), R("BoR"), R("s33"))
         act(R("nask"), R("B5", 128, 256), F.Relu, bias=-14.0 * BIG, scale=-BIG)
         mms(R("B1", 0, 128), [(R("I"), R("bar0")), (R("I"), R("nask"))])
         act(R("bar"), R("B1", 0, 128))
+        if last:
+            mms(R("B1", 256, 384), [(R("Up"), so), (R("nE0"), so)])
+            act(R("gg"), R("B1", 256, 384))
         if not last:
             act(R("sgz"), zr, F.Sign)
             mms(R("B7", 384, 512), [(R("Up"), R("sgz")), (R("nUp2"), R("sgz"))])
             tt(R("sec"), R("B7", 384, 512), zr, A.mult)
             turn1(t + 1, "B5")
+        if not last:
+            act(part("zz", 3), IND(R("Z", W, V), R("jo", 8 * t, 8 * t + 8)))
+            act(part("tt", 3), part("zz", 3), F.Sign)
+            mm(R("B1", 128, 256), R("TopM"), part("tt", 3))
+            tt(part("bt", 2 * t), R("B1", 128, 256), part("zz", 3), A.mult)
+            send([(STEP[t + 1], R("bt", 256 * t, 256 * t + 256), R("RB", 256 * t, 256 * t + 256), "s%d" % t)], 1.5)
+        if t == 1:
+            send([(STEP[2], R("pm2"), R("PM2"), "p2")], 3.0)
+        if t > 0:
+            put_days(24 * t - 16, zq, uq, "B2", "re%d" % (t - 1))
+        ends = R("kp", 264 * t + 32, 264 * t + 264, 33)
+        tt(ends, R("B6", 264, 272), ends, A.add)
+        soon(0.5)
         scan(R("sc"), R("kp", 264 * t, 264 * t + 264), R("B0", 0, 264), A.add, A.min)
-        tt(R("ki"), R("B6", 264, 272), R("sc", 32, 264, 33), A.add)
-        ts(R("km"), R("ki"), (3 << 22) | (W - 1), A.bitwise_and)
+        ts(R("km"), R("sc", 32, 264, 33), (3 << 22) | (W - 1), A.bitwise_and)
         ts(R("A16"), IND(R("km"), R("ex")), 8192.0, A.min, 2048.0, A.subtract)
-        mms(R("B3", 384, 512), [(R("Up"), so), (R("nE0"), so)])
+        if not last:
+            mms(R("B3", 384, 512), [(R("Up"), so), (R("nE0"), so)])
         tt(R("B16"), R("B3", 0, 128), R("A16"), A.mult)
         if not last:
             mms(R("B3", 256, 384), [(R("Bo"), R("sec")), (R("nI"), bt)])
-        aim, tail = R("B2", 128, 256), R("B2", 240, 256)
-        mm(R("B6", 0, 128), R("A16"), R("I16"))
-        mm(R("B6", 128, 136), R("B16"), R("Q16"))
-        mm(R("B4", 0, 144), R("I16"), R("tri"), True, False)
-        mm(R("B4", 0, 128), R("A16"), R("I16"), False, False)
-        mm(R("B4", 128, 144), R("A16"), R("I16", 112, 128), False, False)
-        mm(R("B4", 0, 144), R("B16"), R("RD"), False, True)
-        act(R("sp"), R("B4", 0, 144), F.Sign, bias=0.5)
-        act(R("sm"), R("B4", 0, 144), F.Sign, bias=-0.5)
+        aim = R("B2", 128, 256)
+        mm(R("B6", 0, 128), R("A16"), R("I"))
+        mm(R("B6", 128, 136), R("B16"), grp)
+        mm(R("B4", 0, DW), R("I"), R("tri"), True, False)
+        for (c0, c1, first) in DSEG:
+            mm(R("B4", c0, c1), R("A16"), R("I", first, 128), False, False)
+        mm(R("B4", 0, DW), R("B16"), R("RD"), False, True)
+        act(R("sp"), R("B4", 0, DW), F.Sign, bias=0.5)
+        act(R("sm"), R("B4", 0, DW), F.Sign, bias=0.5, scale=-1.0)
         mm(aim, R("I"), R("off"), True, False)
-        mm(aim, R("A16"), R("I16"), False, False)
+        mm(aim, R("A16"), R("I"), False, False)
         for q in range(NV):
             e = R("E", EOFF[q], EOFF[q + 1])
-            ts(e, R("B6", 16 * q + 16, 128), R("B6", 128 + q, 129 + q), A.is_equal)
+            ts(e, R("B6", 16 * q + 16, 128), R("B6", 128 + q, 129 + q), A.is_equal, 2.0, A.mult)
             line("equal")
-            if q in (3, NV - 1):
-                wts, src = (R("B4k"), "sp") if q == 3 else (R("nB4k"), "sm")
-                mm(aim, wts, R(src, 0, 128), False, False)
-                mm(tail, wts, R(src, 128, 144), False, False)
-            mm(R("B2", 128 + 16 * q + 16, 256), R("B8k"), e, False, q == NV - 1)
+            if q in (NV - 3, NV - 1):
+                for (c0, c1, first) in DSEG:
+                    mm(R("B2", 128 + first, 256), R("B4k"), R("sm" if q == NV - 1 else "sp", c0, c1), False, False)
+            mm(R("B2", 128 + 16 * q + 16, 256), R("B4k"), e, False, q == NV - 1)
         ts(R("dU"), R("B6", 128, 136), 2048.0, A.add, float(W - 1), A.min)
-        act(R("zd"), IND(Zc, R("dU")))
         gone = part("G", t)
         tt(gone, aim, R("bar"), A.is_lt)
         if not last:
@@ -571,38 +584,39 @@ def rank_program(g, core, T, topo):
             tt(nl, aim, R("bar0"), A.is_ge)
             tt(part("wn", t), R("B3", 256, 384), gone, A.mult)
             send([(STEP[t + 1], nl, part("RN", t), "n%d" % t),
-                  (STEP[t + 1] - STEP[t], part("wn", t), part("WD", t, 256), "w%d" % t)])
+                  (STEP[t + 1] - STEP[t], part("wn", t), part("WD", t, 144), "w%d" % t)])
         send([(-STEP[t], gone, part("RG", t), "g%d" % t)])
         lo = 0 if last else 24 * (t + 1)
-        tt(R("zl"), aim, R("farm"), A.min)
-        scan(R("ll"), R("rsb"), R("zl"), A.add, A.min)
+        scan(R("ll"), R("farm"), aim, A.max, A.min)
         ts(R("SL", lo, lo + 8), R("ll", 15, 128, 16), 2048.0, A.add)
-        act(R("ed"), R("zd"), F.Relu, bias=1.0, scale=-1.0)
-        mm(R("B1", 384, 512), R("FstE"), R("ed"))
+        St, Sw = (Yall, Yw) if last else (Zall, Zw)
+        act(R("ed"), IND(Zc, R("dU")), F.Relu, bias=1.0, scale=-1.0)
+        act(R("zd"), IND(Sw, R("dU")))
+        mm(R("B5", 0, 128), R("FstE"), R("ed"))
         if last:
             act(R("braw"), bt, bias=256.0, scale=-1.0)
-            act(R("td"), R("zd"), F.Sign)
-            mms(R("B5", 0, 128), [(R("I256"), R("td")), (R("nI"), R("zd"))])
-            act(R("yd"), R("B5", 0, 128))
-        tt(R("fd"), R("B1", 384, 512), R("braw") if last else bt, A.mult)
-        St, Sw = (Yall, Yw) if last else (Zall, Zw)
-        tt(IND(St, R("SL", lo, lo + 8)), R("yd") if last else R("zd"), R("fd"), A.add)
-        cp(zp, IND(Sw, src_list(t)))
+        tt(R("fd"), R("B5", 0, 128), R("braw") if last else bt, A.mult)
+        tt(IND(St, R("SL", lo, lo + 8)), R("zd"), R("fd"), A.add)
+        (cp if last else act)(zp, IND(Sw, src_list(t)))
         mm(R("B2", 384, 512), R("TopM"), zp)
+        if t == 1:
+            put_days(lo, R("zd"), R("fd"), "B4", "rd")
         if not last:
             tt(R("mx"), R("ll", 15, 128, 16), R("far", 8 * t, 8 * t + 8), A.min)
             ts(R("SL", lo + 8, lo + 16), R("mx"), 2048.0, A.add)
             turn2(t + 1, "B1")
         if t == 0:
             act(R("nj"), IND(R("NL", 0, 144), R("jx1")))
-            tt(R("zj"), R("B3", 0, 128), R("nj"), A.mult)
-            scan(R("lj"), R("rst", 0, 128), R("zj"), A.mult, A.add)
-            tt(R("ta"), R("lj", 15, 128, 16), R("dd"), A.mult)
-            tt(R("tb"), R("ta"), R("n128", 0, 8), A.add)
-            cp(R("pm2", 0, 8), R("tb"))
-        tt(R("gg"), R("B3", 384, 512), part("RG", t), A.mult)
-        tt(uu, R("B2", 384, 512), R("gg"), A.mult)
-        tt(IND(St, src_list(t)), zp, uu, A.add)
+            tt(R("zj"), part("jm", 1), R("nj"), A.mult)
+            scan(R("lj"), R("rst"), R("zj"), A.mult, A.add)
+            ts(R("pm2", 0, 8), R("lj", 15, 128, 16), 128.0, A.add)
+        if not last:
+            res, btp = part("RB", 2 * t), part("RB", 2 * t + 1)
+            mms(R("B3", 128, 256), [(R("Bo"), res), (R("nI"), btp)])
+
+    tt(R("B3", 384, 512), R("B2", 384, 512), R("gg"), A.mult)
+    tt(uu, R("B3", 384, 512), part("RG", 2), A.mult)
+    tt(IND(Yall, src_list(2)), zp, uu, A.add)
 
     dma("y", T.y[:], T.Y[:, 0:V], Yw, store=True)
 
@@ -636,10 +650,12 @@ def rank_program(g, core, T, topo):
     for c in calls:
         if c["kind"] == "land":
             note(c, (c["lands"], landed[c["lands"]]))
-    for j in plan(calls):
+    if not ORDER:
+        ORDER.extend(plan(calls))
+    for j in ORDER:
         c = calls[j]
         e = c["e"]
-        need(e, [tok for (e2, tok) in clashes(hist, e, c["reads"], c["writes"]) if not e2 == e == "p"])
+        need(e, [tok for (e2, tok, wait) in clashes(hist, e, c["reads"], c["writes"]) if wait])
         if c["kind"] == "send":
             c["issue"]()
             continue

@@ -3,11 +3,12 @@ from concourse.mybir import AluOpType as A, ActivationFunctionType as F
 
 N, W, V, S, K = 8, 4096, 4608, 128, 32
 STEP = (1, 2, 3)
-KS = (16, 15, 16)
+KS = (16, 16, 16)
 SCH = [[(4, 8), (8, 12), (12, _k)] for _k in KS]
 VCH = [[(0, 2), (2, 4), (_k, _k + 4), (_k + 4, _k + 8), (_k + 8, _k + 12), (_k + 12, 31), (31, 32)] for _k in KS]
 UNIT = 1 << 18
-BIG, OFF = float(1 << 24), float(1 << 19)
+BIG, OFF = float(1 << 24), 8192.0
+HIT = 8192.0
 CUT = 64
 NV = 6
 EOFF = [0, 112, 208, 288, 352, 400, 432]
@@ -15,26 +16,28 @@ DSEG = [(0, 128, 0)]
 for _q in range(NV, 7):
     DSEG.append((DSEG[-1][1], DSEG[-1][1] + 112 - 16 * _q, 16 * _q + 16))
 DW = DSEG[-1][1]
-LOADS = [(0, 2048), (2048, 4608)]
-ZBANK = ("B0", "B5", "B6", "B2", "B5", "B6", "B4", "B1", "B2")
-ZORDER = (0, 1, 2, 3, 6, 7, 4, 5, 8)
+KEY, BP, BQ, BR, BU, BD, BE, BF = ("B%d" % _b for _b in range(8))
+LOADS = [(0, 1536), (1536, 3072), (3072, 4608)]
+MID = 6
+ZBANK = (BP, BQ, BU, BR, BF, BD, BR, BE, BU)
 ZADD = (7, 8)
 
-CYCLE, LINK, GATHER, SCATTER, SCALAR = 0.00093, 0.15, 1.56, 3.8, 1.06
-ISSUE, FIRST, HOP, HOP2, DMA0, ROW, RATE = 0.6, 2.3, 1.65, 1.9, 1.75, 0.02, 20000.0
+CYCLE, LINK, GATHER, SCATTER, SCALAR = 0.001, 0.11, 1.56, 3.8, 1.0
+ISSUE, FIRST, HOP, HOP2, DMA0, ROW, RATE = 0.4, 2.3, 1.22, 1.45, 1.75, 0.015, 20000.0
+AFTER, DIRECT = False, False
+TRIES = 100
 
 bf, f32, i32, u16, f16 = "bfloat16", "float32", "int32", "uint16", "float16"
 SIZE = {bf: 2, f32: 4, i32: 4, u16: 2, f16: 2}
 SCRATCH = {}
 WHERE = {}
 for _n, _w, _d in [
-    ("Y", V + S, bf), ("Z", V + S, bf), ("t256", V, bf), ("trk", 24, i32), ("cnd", 768, i32),
+    ("Y", V + 240, bf), ("Z", V + 240, bf), ("t256", V, bf), ("trk", 24, i32), ("cnd", 768, i32),
     ("P16", 768, f16), ("X", 768, f16),
-    ("ic", 16, i32), ("ex", 8, u16), ("kp", 792, f32), ("JT", V + 512, bf), ("jo", 16, u16),
-    ("jx1", 8, u16), ("SL", 72, u16), ("dU", 8, u16),
-    ("rc0", 128, bf), ("RC", 128, bf), ("zz", 512, bf), ("ZR", 384, bf), ("bt", 640, bf), ("RB", 512, bf),
-    ("pm1", 8, u16), ("PM1", 8, u16), ("pm2", 8, u16), ("PM2", 8, u16),
-    ("G", 384, bf), ("RG", 384, bf), ("NL", 288, bf), ("RN", 256, bf), ("wn", 256, bf),
+    ("ic", 16, i32), ("ex", 8, u16), ("JT", V + 512, bf), ("jo", 16, u16), ("SL", 72, u16), ("dU", 8, u16),
+    ("rc0", 128, bf), ("RC", 128, bf), ("zz", 512, bf), ("ZR", 384, bf), ("res", 256, bf), ("RB", 256, bf),
+    ("RT", 16, i32), ("rl", 16, u16), ("PM1", 8, u16), ("pm2", 8, u16), ("PM2", 8, u16),
+    ("RG", 384, bf), ("NL", 256, bf), ("RN", 256, bf), ("wn", 256, bf), ("G", 384, bf),
     ("WD", 288, bf), ("q", 256, bf), ("cu", 256, u16),
     ("thr", 512, bf), ("cmp", 4096, bf), ("raw", 1536, bf), ("sc", 264, i32), ("km", 8, i32),
     ("A16", 128, f16), ("B16", 128, f16), ("E", 432, bf), ("sp", DW, bf), ("sm", DW, bf),
@@ -51,17 +54,16 @@ def _pack(buf, dt, items):
     SCRATCH[buf] = ("sbuf", [128, c], dt)
 
 
-_pack("small", f32, [("c15", 8), ("nL", 8), ("far", 16), ("mx", 8), ("farm", 128), ("ll", 128)])
+_pack("small", f32, [("fc", 8), ("LT", 16), ("nL", 8), ("far", 16), ("mx", 8), ("farm", 128), ("ll", 128), ("T2", 128)]
+      + [("st%d" % _k, 264) for _k in sorted(set(KS))])
 _pack("konst", bf, [(_n, 128) for _n in (
-    "ones", "G16", "R16", "I", "nI", "I256", "I15", "m4k", "Bo", "nBo", "BoR", "BoC", "nE0", "bar0", "Up",
-    "nUp", "nUp2", "nDn", "TopM", "FstE", "mask", "turn", "B4k", "off", "jn", "rst")]
-      + [("Q97", 256), ("cst", 192), ("dcn", 272), ("dfa", 144), ("dfb", 144), ("RD", DW), ("tri", DW),
-         ("dif", 144), ("cols", 16), ("Wv", 16), ("Ws", 16), ("W97", 16), ("W33", 16), ("c26", 16), ("c33", 16),
-         ("cS", 16)])
+    "ones", "G16", "R16", "I", "nI", "nI256", "m4k", "Bo", "nBo", "nE0", "E0", "bar0", "Up", "IUp", "nU1",
+    "nU2", "D1", "mask", "turn", "B4k", "off", "jn", "rst", "Wall", "Row4", "Ma", "Mb", "C2", "nC1")]
+      + [("Q97", 256), ("RD", DW), ("tri", DW), ("cols", 16), ("GE", 16), ("Wv", 16), ("Ws", 16), ("W33", 16),
+         ("c33", 16), ("W97", 272)])
 _pack("work", bf, [(_n, 128) for _n in (
-    "s33", "sgz", "nask", "bar", "sec", "gg", "ed", "zd", "td", "yd", "fd", "braw", "ra", "rb", "rd", "re0",
-    "re1", "nj", "zj", "lj", "t2", "t3", "xm", "r1", "s1")]
-      + [("tt", 512), ("jm", 256), ("js", 256), ("zp", 384), ("uu", 384)])
+    "s33", "nask", "bar", "gg", "ed", "zd", "fd", "ra", "rd", "re", "rf", "t2", "xm", "rc", "so", "ld", "jm", "js")]
+      + [("s12", 256), ("zp", 384), ("uu", 384)])
 for _b in range(8):
     SCRATCH["B%d" % _b] = ("psum", [128, 512], f32)
     WHERE["B%d" % _b] = ("B%d" % _b, 0, 512)
@@ -93,8 +95,6 @@ def plan(calls):
                 pre[sender[i]] = max(pre.get(sender[i], 0.0), calls[sender[i]]["hop"])
             elif not c["kind"] == calls[i]["kind"] == "sum":
                 pre[i] = max(pre.get(i, 0.0), LINK if wait else 0.0)
-        if c["kind"] == "send" and j > min(sender.values()):
-            pre.setdefault(min(sender.values()), 0.0)
         if c["line"] in last:
             pre.setdefault(last[c["line"]], 0.0)
         if c["line"]:
@@ -108,26 +108,49 @@ def plan(calls):
     for j, pre in enumerate(before):
         for i, lat in pre.items():
             after[i].append((j, lat))
-    tail = {}
-    for j in reversed(range(len(calls))):
-        tail[j] = calls[j]["cost"] + calls[j]["soon"] + max([lat + calls[k]["lead"] + tail[k] for k, lat in after[j]]
-                                                            + [0.0])
-    start, ready, busy = {}, {}, {}
-    for j in sorted(range(len(calls)), key=lambda x: (-tail[x], x)):
-        c = calls[j]
-        if c["e"] == "r":
-            continue
-        t = c["lead"] + max([start[i] + calls[i]["cost"] + lat for i, lat in before[j].items()] + [0.0])
-        ready[j] = t - c["lead"]
-        lane = busy.setdefault("d" if c["lead"] else c["e"], [])
-        for (a, b) in lane:
-            if t + c["cost"] <= a + 1e-9:
-                break
-            t = max(t, b)
-        lane.append((t, t + c["cost"]))
-        lane.sort()
-        start[j] = t
-    return sorted(start, key=lambda x: (ready[x] if calls[x]["lead"] else start[x], start[x], x))
+    real = [j for j, c in enumerate(calls) if c["e"] != "r"]
+
+    def place(more):
+        tail, end, held, busy = {}, {}, {}, {}
+        for j in reversed(real):
+            tail[j] = calls[j]["cost"] + calls[j]["soon"] + more.get(j, 0.0) + max(
+                [lat + calls[k]["lead"] + tail[k] for k, lat in after[j]] + [0.0])
+        for j in sorted(real, key=lambda x: (-tail[x], x)):
+            c = calls[j]
+            t, held[j] = max([(end[i] + lat, (i, False)) for i, lat in before[j].items()] + [(0.0, None)],
+                             key=lambda x: x[0])
+            t += c["lead"]
+            lane = busy.setdefault("d" if c["lead"] else c["e"], [])
+            at = len(lane)
+            while at > 0 and lane[at - 1][1] > t + 1e-9:
+                at -= 1
+            while at < len(lane) and t + c["cost"] > lane[at][0] + 1e-9:
+                t, held[j] = lane[at][1], (lane[at][2], True)
+                at += 1
+            lane.insert(at, (t, t + c["cost"], j))
+            end[j] = t + c["cost"]
+        return max(end.values()), end, held, tail
+
+    more, tried = {}, set()
+    best = place(more)
+    for _ in range(TRIES):
+        total, end, held, tail = best
+        j, pick = max(end, key=end.get), None
+        while held[j] and pick is None:
+            i, queued = held[j]
+            if queued and (i, j) not in tried:
+                pick = (i, j)
+            j = i
+        if pick is None:
+            break
+        tried.add(pick)
+        other = dict(more)
+        other[pick[1]] = more.get(pick[1], 0.0) + tail[pick[0]] - tail[pick[1]] + 0.01
+        got = place(other)
+        if got[0] < total - 1e-6:
+            more, best = other, got
+    end = best[1]
+    return sorted(real, key=lambda x: (end[x] - calls[x]["cost"] - calls[x]["lead"], end[x], x))
 
 
 ORDER = []
@@ -152,13 +175,10 @@ def rank_program(g, core, T, topo):
 
     def call(e, issue, reads, writes, cost, lead=0.0, hop=0.0, sems=(), lands=None, kind="op"):
         calls.append(dict(e=e, issue=issue, reads=reads, writes=writes, cost=cost, lead=lead, hop=hop, sems=sems,
-                          lands=lands, kind=kind, line=None, soon=0.0))
+                          lands=lands, kind=kind, line=e if e in "vsg" and kind != "dma" else None, soon=0.0))
 
     def soon(us):
         calls[-1]["soon"] = us
-
-    def line(name):
-        calls[-1]["line"] = name
 
     def op(e, issue, out, ins, rate):
         ins = [x for x in ins if isinstance(x, tuple)]
@@ -203,18 +223,14 @@ def rank_program(g, core, T, topo):
     def act(o, i, fn=F.Identity, bias=0.0, scale=1.0):
         op("s", lambda: g.scalar.activation(o[0], i[0], fn, bias=ap(bias), scale=ap(scale)), o, [i, scale, bias], 1.0)
 
-    def mm(o, l, r, start=True, stop=True):
-        op("p", lambda: g.tensor.matmul(o[0], l[0], r[0], start, stop), o, [l, r], 1.0)
+    def mm(o, l, r, start=False, kind="op"):
+        stop = []
+        op("p", lambda: g.tensor.matmul(o[0], l[0], r[0], start, bool(stop)), o, [l, r], 1.0)
+        calls[-1].update(kind=kind, start=start, stop=stop)
 
     def mms(o, pairs):
         for j, (l, r) in enumerate(pairs):
-            mm(o, l, r, j == 0, j == len(pairs) - 1)
-
-    def tier_sum(o, pairs):
-        def issue():
-            return [g.tensor.matmul(o[0], l[0], r[0], j == 0, j == len(pairs) - 1) for j, (l, r) in enumerate(pairs)][-1]
-
-        call("p", issue, [x for (l, r) in pairs for x in l[1] + r[1]], o[1], 32 * CYCLE * len(pairs), kind="sum")
+            mm(o, l, r, j == 0)
 
     def iota(o, pat, base, cm, fl=True):
         if fl:
@@ -239,7 +255,7 @@ def rank_program(g, core, T, topo):
 
     sent, landed = [0], {}
 
-    def send(items, early=0.0):
+    def send(items, late=0.0):
         trs = []
         for j, (d, src, dst, s) in enumerate(items):
             rid, pid, _ = topo.addr(T.cores[(rank + d) % N])
@@ -259,8 +275,7 @@ def rank_program(g, core, T, topo):
 
         first = not any(c["kind"] == "send" for c in calls)
         call("g", issue, [r for it in items for r in it[1][1]], [], ISSUE + (FIRST if first else 0.0),
-             hop=(HOP if len(items) == 1 else HOP2) - ISSUE, sems=[it[3] for it in items], kind="send")
-        soon(early)
+             hop=(HOP if len(items) == 1 else HOP2) - ISSUE + late, sems=[it[3] for it in items], kind="send")
 
     def arrive(dsts, s):
         call("r", None, [], [r for x in dsts for r in x[1]], 0.0, lands=s, kind="land")
@@ -269,355 +284,419 @@ def rank_program(g, core, T, topo):
         return R(name, w * t, w * t + 128)
 
     arrive([R("RC")], "b0")
-    arrive([R("PM1")], "me")
+    arrive([R("RT")], "me")
     arrive([R("PM2")], "p2")
     for t in range(3):
         arrive([part("ZR", t)], "z%d" % t)
         arrive([part("RG", t)], "g%d" % t)
     for t in range(2):
-        arrive([R("RB", 256 * t, 256 * t + 256)], "s%d" % t)
+        arrive([part("RB", t)], "s%d" % t)
         arrive([part("RN", t)], "n%d" % t)
         arrive([part("WD", t, 144)], "w%d" % t)
 
     def src_list(t):
         return R("SL", 24 * t + 8, 24 * t + 16)
 
-    def fill(name, c, lo=0, hi=None, h=None):
-        pp = (128, 0) if h is None else (32 * h + 32, 32 * h)
-        o = R(name, lo, hi, 1, *pp)
-        act(o, R("ones", 0, o[3], 1, *pp), scale=c)
+    def rows(name, h, lo=0, hi=None, step=1):
+        return R(name, lo, hi, step, 32 * h + 32, 32 * h)
 
     dma("s", T.trk[:], T.trucks[:], R("trk"))
-    soon(2.0)
+    soon(9.0)
     for (lo, hi) in LOADS:
         dma("y", T.Y[:, lo:hi], T.days[:, lo:hi], R("Y", lo, hi))
-    dma("y", T.cnd[:], T.cand[:], R("cnd"))
+    dma("y", T.cnd[:, 0:256], T.cand[:, 0:256], R("cnd", 0, 256))
 
-    tier, yard, bars = (R("cols", j, j + 1) for j in range(3))
-    c15, wcol, nm0 = (R("c15", j, j + 1) for j in range(3))
-    grp = R("Bo", 0, 128, 16)
-    one32, one64 = R("ones", 0, 128, 1, 32), R("ones", 0, 128, 1, 64)
-    diag = [[-1, 128]]
-    mset(R("ones"), 1.0)
-    iota(R("ic", 0, 1), [[0, 1]], 0, 1, False)
-    sel(R("I"), R("ones"), diag, A.is_equal, 0, 1)
-    iota(R("G16"), [[1, 8], [0, 16]], 0, 0)
-    iota(R("R16"), [[0, 8], [1, 16]], 0, 0)
-    iota(R("jn"), [[1, 128]], -128, 0)
-    soon(12.0)
-    iota(R("nL"), [[16, 8]], V - 2048, 0)
-    sel(R("turn"), R("ones"), [[-1, 16], [-16, 8]], A.is_equal, 0, 1)
-    ts(R("ic", 2, 3), R("ic", 0, 1), 15, A.bitwise_and)
-    ts(R("ic", 3, 4), R("ic", 0, 1), 4, A.arith_shift_right)
-    cp(R("cols", 0, 2), R("ic", 2, 4))
-    ts(R("Bo"), R("G16"), yard, A.is_equal)
-    ts(R("mask"), R("R16"), tier, A.is_equal)
-    ts(c15, tier, 15.0, A.is_lt)
-    ts(nm0, tier, 0.0, A.is_equal, -1.0, A.mult)
-    act(wcol, c15, scale=-15.0 * UNIT, bias=16.0 * UNIT)
-    act(bars, c15, scale=38912.0, bias=-6144.0)
-    act(R("rst"), R("R16"), F.Sign)
-    for name, src, scale in [("nI", "I", -1.0), ("m4k", "I", -4096.0), ("I256", "I", 256.0), ("I15", "I", c15),
-                             ("nBo", "Bo", -1.0), ("BoC", "Bo", 1.0), ("BoR", "Bo", c15), ("nE0", "Bo", nm0),
-                             ("B4k", "Bo", 4096.0)]:
-        act(R(name), R(src), scale=scale)
-    act(R("BoC", 15, 128, 16), grp, scale=0.0)
-    sel(R("nUp"), R("nBo"), diag, A.is_equal, -1, 1)
-    sel(R("nUp2"), R("nBo"), diag, A.is_equal, -2, 1)
-    sel(R("nDn"), R("nBo"), diag, A.is_equal, 1, 1)
-    sel(R("TopM"), R("nUp"), diag, A.not_equal, 0, 1, 1.0)
-    sel(R("FstE"), R("nDn"), diag, A.not_equal, 0, 1, 1.0)
-    act(R("Up"), R("nUp"), scale=-1.0)
-    act(R("Q97", 0, 8), grp, scale=-97.0)
-    act(R("Q97", 8, 16), grp, scale=-97.0)
-    for w in (16, 32, 64, 128):
-        act(R("Q97", w, 2 * w), R("Q97", 0, w))
-    act(R("Wv", 0, 8), grp, scale=wcol)
-    act(R("Ws", 0, 8), R("Wv", 0, 8), scale=0.5)
-    act(R("W97", 0, 8), R("nE0", 0, 128, 16), scale=97.0)
-    act(R("W33", 0, 8), R("BoR", 0, 128, 16), scale=BIG / 2)
-    act(R("B3", 0, 128), R("mask"))
-    for h in range(2):
-        fill("cst", (16384.0, 968.0)[h], 0, 128, h)
-        fill("cst", (16384.0, 968.0)[h], 128, 192, h)
-        fill("c26", (712.0, -65536.0)[h], 0, 8, h)
-        fill("WD", 0.0, 144 * h + 128, 144 * h + 144)
-    fill("cS", 31.0 * W, 0, 8, 0)
-    fill("c33", 14.75 * UNIT, 0, 8, 0)
-    fill("Z", 0.0, V, V + S)
-    fill("Y", 0.0, V, V + S)
-    fill("NL", 0.0, 128, 144)
-    act(R("off"), R("mask"), scale=-OFF, bias=OFF)
-    act(R("bar0"), R("mask"), scale=-OFF, bias=OFF + W)
-    fill("farm", -BIG)
-    act(R("farm", 0, 128, 16), R("nL"), bias=tier)
-    ts(R("ex"), R("jn", 0, 8), 128.0, A.add)
-    ts(R("tri", 0, 128), R("R16"), tier, A.is_le, bars, A.mult)
-    fill("tri", 0.0, 128, DW)
-    act(R("RD", 0, 128), R("BoR"), scale=-1.0)
-    for (c0, c1, first) in DSEG[1:]:
-        act(R("RD", c0, c1), R("nBo", first - 16, first))
-        for c in range(c0 + 16, c1, 16):
-            act(R("RD", c, c + 16), R("nBo", first - 16, first))
-    fill("dfa", 1.0, 0, 128)
-    fill("dfa", 1.0, 128, 132)
-    sel(R("dfb", 0, 132), R("dfa", 0, 132), [[-32, 4], [-1, 33]], A.is_equal, 1, 1)
-    sel(R("dif", 0, 132), R("dfb", 0, 132), [[-32, 4], [-1, 33]], A.not_equal, 0, 1, -1.0)
-    act(R("dif", 32, 132, 33), R("dfb", 32, 132, 33))
-    mset(R("dcn", 0, 264, 1, 32), -128.0)
-    act(R("dcn", 0, 264, 33, 32), R("ones", 0, 8, 1, 32), scale=float(UNIT))
-    act(R("dcn", 32, 264, 33, 32), R("ones", 0, 8, 1, 32), scale=69632.0)
-
-    cp(R("SL", 8, 16), R("trk", 0, 8))
-    ts(R("far"), R("trk", 8, 24), 2048.0, A.subtract)
-    ts(R("jo"), R("trk", 8, 24), float(W), A.subtract)
-    for h in range(2):
-        table = R("JT", W + 512 * h, V + 512 * h)
-        mset(table, 0.0)
-        if h == 0:
-            cp(IND(R("JT", 0, V), src_list(0)), R("jn"))
-        else:
-            for c in (0, 4):
-                cp(IND(table, R("jo", c, c + 4)), R("jn", 16 * c, 16 * c + 64))
-        tt(part("jm", h), IND(table, R("jo", 8 * h, 8 * h + 8)), R("mask"), A.mult)
-        scan(part("js", h), R("rst"), part("jm", h), A.mult, A.add)
-        ts(R(("pm1", "jx1")[h], 0, 8), R("js", 128 * h + 15, 128 * h + 128, 16), 128.0, A.add)
-
+    pm127, pm128, pm129, pm130, tier, yard, bars, c256, b256, sq = (R("cols", j, j + 1) for j in range(10))
+    c15, lt4, wcol, wrow = R("LT", 15, 16), R("LT", 4, 5), R("fc", 0, 1), R("fc", 1, 2)
+    grp, ones, cap, nBoR = R("Bo", 0, 128, 16), R("ones"), R(KEY, 384, 512), R("RD", 0, 128)
     Yw, Zw, Zc, Yall, Zall = R("Y", 0, V), R("Z", 0, V), R("Z", 0, W), R("Y"), R("Z")
 
-    def tops(out, src, sign, rev, bank):
-        act(sign, src, F.Sign)
-        ts(rev, src, -1.0, A.mult, 256.0, A.add)
-        mms(bank, [(R("I"), sign), (R("nUp"), sign)])
-        tt(out, bank, rev, A.mult)
+    def const(o, c, parts=128):
+        act(o, R("ones", 0, o[3], 1, parts), scale=c)
 
-    send([(STEP[1], R("pm1"), R("PM1"), "me")])
-    tops(R("rc0"), IND(Yw, src_list(0)), part("tt", 0), R("rb"), R("B7", 128, 256))
-    send([(STEP[0], R("rc0"), R("RC"), "b0")])
-    tt(part("zz", 0), R("rb"), part("tt", 0), A.mult)
-    send([(STEP[0], part("zz", 0), part("ZR", 0), "z0")])
+    def times(pairs):
+        for name, src, by in pairs:
+            ts(R(name), R(src), by, A.mult)
+
+    def table(h):
+        return R("JT", W + 512 * h, V + 512 * h)
+
+    def note_slots(c):
+        cp(IND(R("JT", 0, V), R("rl", c, c + 4)), R("jn", 16 * c, 16 * c + 64))
+
+    def read_slots(h):
+        tt(R("jm"), IND(table(h), R(("rl", "jo")[h], 8, 16)), R("mask"), A.mult)
+
+    def list_slots(h):
+        ts(R(("PM1", "pm2")[h]), R("js", 15, 128, 16), 128.0, A.add)
+
+    def mark(c):
+        ts(R("t256", 512 * c, 512 * c + 512), R("Y", 512 * c, 512 * c + 512), 256.0, A.mult, 256.0, A.min)
+
     def mirror(c):
         y, z, m, bank = (R("Y", 512 * c, 512 * c + 512), R("Z", 512 * c, 512 * c + 512),
                          R("t256", 512 * c, 512 * c + 512), R(ZBANK[c]))
-        ts(m, y, 256.0, A.mult, 256.0, A.min)
         if c in ZADD:
-            mm(bank, R("nI"), y)
+            mm(bank, R("nI"), y, True)
             tt(z, bank, m, A.add)
         else:
-            mms(bank, [(R("I"), m), (R("nI"), y)])
+            mms(bank, [(R("nI"), y), (R("I"), m)])
             act(z, bank)
-            line("mirror")
 
-    for c in ZORDER:
+    mset(ones, 1.0)
+    mset(table(0), 0.0)
+    iota(R("ic", 0, 1), [[0, 1]], 0, 1, False)
+    iota(R("jn"), [[1, 128]], -128, 0)
+    iota(R("cols", 0, 4), [[-1, 4]], -127, 1)
+    iota(R("R16"), [[0, 8], [1, 16]], 0, 0)
+    iota(R("G16"), [[1, 8], [0, 16]], 0, 0)
+    iota(R("Q97"), [[0, 32], [1, 8]], 0, 0)
+    send([(STEP[1], R("trk", 0, 16), R("RT"), "me")], 3.0)
+    mset(table(1), 0.0)
+    ts(R("ic", 2, 3), R("ic", 0, 1), 15, A.bitwise_and)
+    ts(R("ic", 3, 4), R("ic", 0, 1), 4, A.arith_shift_right)
+    cp(R("cols", 4, 6), R("ic", 2, 4))
+    ts(R("I"), R("jn"), pm128, A.is_equal)
+    for k in sorted(set(KS)):
+        for lo in (0, 128, 256):
+            const(R("st%d" % k, lo, min(lo + 128, 264)), -float(W))
+    const(R("c33", 0, 8, 1, 32), 14.75 * UNIT, 32)
+    for k in sorted(set(KS)):
+        for at, c in ((0, BIG), (4, -W - 15.5 * UNIT), (k, -W + 15.5 * UNIT), (32, 31.0 * W + 2048 + 97 * 256)):
+            const(R("st%d" % k, at, 264, 33), c)
+    act(R("rst"), R("R16"), F.Sign)
+    times([("nI", "I", -1.0), ("nI256", "I", -256.0), ("m4k", "I", -4096.0)])
+    ts(R("LT"), R("R16", 0, 16), tier, A.is_gt)
+    ts(R("mask"), R("R16"), tier, A.is_equal)
+    ts(R("GE"), R("R16", 0, 16), tier, A.is_le, -256.0, A.mult)
+    act(b256, c15, scale=256.0)
+    act(bars, c15, scale=38912.0, bias=-6144.0)
+    act(wcol, c15, scale=-15.0 * UNIT, bias=16.0 * UNIT)
+    ts(R("Bo"), R("G16"), yard, A.is_equal)
+    ts(R("nBo"), R("G16"), yard, A.is_equal, -1.0, A.mult)
+    ts(R("nU1"), R("jn"), pm129, A.is_equal, R("GE", 1, 2), A.mult)
+    act(R("off"), R("mask"), scale=-OFF, bias=OFF)
+    act(nBoR, R("nBo"), scale=c15)
+    act(R("Wv", 0, 8), grp, scale=wcol)
+    act(R("Ws", 0, 8), R("Wv", 0, 8), scale=0.5)
+    act(R("W33", 0, 8), R("RD", 0, 128, 16), scale=-BIG / 2)
+    for (c0, c1, first) in DSEG[1:]:
+        for c in range(c0, c1, 16):
+            act(R("RD", c, c + 16), R("nBo", first - 16, first))
+    act(cap, R("mask"), scale=W + OFF, bias=-OFF)
+    act(sq, tier, F.Square, bias=-2.0)
+    const(R("tri", 128, DW), 0.0)
+    cp(R("SL", 8, 16), R("trk", 0, 8))
+    ts(R("jo"), R("trk", 8, 24), float(W), A.subtract)
+
+    for c in range(MID):
+        if c == 3:
+            cp(IND(table(1), R("jo", 0, 8)), R("jn"))
+        mark(c)
+    read_slots(1)
+    for c in range(MID):
         mirror(c)
+    cp(R("rc0"), IND(Yw, src_list(0)))
+    send([(STEP[0], R("rc0"), R("RC"), "b0")])
+    sel(R("turn"), ones, [[-1, 16], [-16, 8]], A.is_equal, 0, 1)
+    iota(R("W97", 0, 264), [[0, 264]], -97, 0)
+    act(R("so"), R("rc0"), F.Sign)
+    for c in range(MID, 9):
+        mark(c)
+    mirror(MID)
+    mms(R(BP, 0, 128), [(R("I"), R("rc0")), (R("nI256"), R("so"))])
+    act(part("zz", 0), R(BP, 0, 128), scale=-1.0)
+    send([(STEP[0], part("zz", 0), part("ZR", 0), "z0")])
+    sel(R("W97", 0, 264), R("W97", 0, 264), [[-16, 8], [0, 33]], A.is_equal, 0, 1)
+    dma("y", T.cnd[:, 256:768], T.cand[:, 256:768], R("cnd", 256, 768), behind=part("ZR", 0)[1])
 
-    def narrow(t):
-        for lo in range(256 * t, 256 * t + 256, 128):
-            ts(R("P16", lo, lo + 128), R("cnd", lo, lo + 128), 2048.0, A.subtract)
+    def narrow(t, h=None):
+        lo, hi = (256 * t, 256 * t + 256) if h is None else (256 * t + 128 * h, 256 * t + 128 * h + 128)
+        ts(R("P16", lo, hi), R("cnd", lo, hi), 2048.0, A.subtract)
 
-    def turn1(t, bank):
+    def turn1(t):
+        bank = BD if t else KEY
         for q in range(8):
-            a, c0 = q // 2, 256 + (q % 2) * 128
-            mm(R(bank, c0, c0 + 128, 1, 32 * a + 32, 32 * a), R("P16", 256 * t + q, 256 * t + 256, 8), R("turn"))
-        for lo in (0, 128):
-            cp(R("X", 256 * t + lo, 256 * t + lo + 128), R(bank, 256 + lo, 384 + lo))
-            soon(0.0 if t else 1.0)
+            a, c0 = q // 2, (q % 2) * 128
+            mm(rows(bank, a, c0, c0 + 128), R("P16", 256 * t + q, 256 * t + 256, 8), R("turn"), True)
+        return lambda: cp(R("X", 256 * t, 256 * t + 256), R(bank, 0, 256))
 
-    def turn2(t, bank):
-        mm(R(bank, 0, 264), one32, R("dcn", 0, 264, 1, 32), True, False)
+    def turn2(t):
         for a in range(4):
             for gg in range(8):
-                mm(R(bank, 33 * gg, 33 * gg + 33, 1, 32 * a + 32, 32 * a), R("X", 256 * t + gg, 256 * t + 256, 8),
-                   R("dif", 33 * a, 33 * a + 33), False, gg == 7)
-        act(R("kp", 264 * t, 264 * t + 264), R(bank, 0, 264))
+                mm(rows(KEY, a, 33 * gg, 33 * gg + 32), R("X", 256 * t + gg, 256 * t + 256, 8),
+                   R("I", 32 * a, 32 * a + 32), kind="sum")
 
-    for t in range(3):
-        narrow(t)
+    def tier_sum(k, x, w):
+        mm(R(KEY, k, 264, 33), x, R(w, 0, 8), kind="sum")
 
-    def put_days(lo, z, dz, bank, buf):
-        mms(R(bank, 0, 128), [(R("I"), z), (R("I"), dz)])
-        act(R("ra"), R(bank, 0, 128), F.Sign)
-        mms(R(bank, 128, 256), [(R("I256"), R("ra")), (R("nI"), z), (R("nI"), dz)])
-        act(R(buf), R(bank, 128, 256))
-        for h in range(2):
-            cp(IND(Yall, R("SL", lo + 4 * h, lo + 4 * h + 4)), R(buf, 64 * h, 64 * h + 64))
+    def tops(o, x, two=False):
+        mm(o, R("I"), x, not two)
+        mm(o, R("nU2" if two else "nU1"), x)
 
-    LISTS = [(0, CUT, R("B5", 0, CUT), R("B6", 0, CUT)),
-             (CUT, 256, R("B1", 0, 256 - CUT), R("B0", 264, 520 - CUT))]
+    narrow(0)
+    ts(R("Q97"), R("Q97"), yard, A.is_equal, -97.0, A.mult)
+    scan(R("js"), R("rst"), R("jm"), A.mult, A.add)
+    for name, at, by in [("nU2", pm130, R("GE", 2, 3)), ("D1", pm127, b256)]:
+        ts(R(name), R("jn"), at, A.is_equal, by, A.mult)
+    list_slots(1)
+    ts(R("tri", 0, 128), R("R16"), tier, A.is_le, bars, A.mult)
+    ts(R("ex"), R("jn", 0, 8), 128.0, A.add)
+    ts(c256, sq, 1.0, A.is_equal, 256.0, A.mult)
+    for c in range(MID + 1, 9):
+        mirror(c)
+    turn1(0)()
+
+    def to_days(z, dz, buf):
+        mms(R(BF, 0, 128), [(R("I"), z), (R("I"), dz)])
+        act(R("ra"), R(BF, 0, 128), F.Sign)
+        mms(R(BF, 128, 256), [(R("I"), z), (R("I"), dz), (R("nI256"), R("ra"))])
+        return lambda: act(R(buf), R(BF, 128, 256), scale=-1.0)
+
+    def put_days(lo, h, a, b=None):
+        out, x = IND(Yall, R("SL", lo + 4 * h, lo + 4 * h + 4)), R(a, 64 * h, 64 * h + 64)
+        if b:
+            tt(out, x, R(b, 64 * h, 64 * h + 64), A.add)
+        else:
+            cp(out, x)
+
+    def take_tops(t, window):
+        if t == 2 or DIRECT:
+            tt(R("gg"), R(KEY, 0, 128), part("RG", t), A.mult)
+            tt(part("uu", t), shift, R("gg"), A.mult)
+        else:
+            tt(R(KEY, 128, 256), shift, R("gg"), A.mult)
+            tt(part("uu", t), R(KEY, 128, 256), part("RG", t), A.mult)
+        tt(IND(window, src_list(t)), part("zp", t), part("uu", t), A.add)
+
+    LISTS = [(0, CUT, R(BR, 0, CUT), R(BD, 0, CUT)),
+             (CUT, 256, R(BE, 0, 256 - CUT), R(BU, 0, 256 - CUT))]
+    spread, twice, shift = R(BP, 0, 128), [R(BQ, 0, 128), R(BQ, 128, 256)], R(BF, 0, 128)
+    LIFT = 135.0 * W + 2304
 
     for t in range(3):
         last = t == 2
-        bt = part("bt", (1, 3, 4)[t])
-        zo, zr, so, zp, uu = part("zz", t), part("ZR", t), part("tt", t), part("zp", t), part("uu", t)
+        zo, zr, zp = part("zz", t), part("ZR", t), part("zp", t)
         thr0 = R("thr", 0, 128)
-        for (lo, hi, la, lb) in LISTS:
+        if t:
+            tt(R("t2"), IND(R("WD", 144 * (t - 1), 144 * t), R("PM%d" % t, 0, 8)), part("RN", t - 1), A.max)
+            if AFTER:
+                turned()
+                ts(src_list(t), R("mx", 0, 8), 2048.0, A.add)
+        for j, (lo, hi, la, lb) in enumerate(LISTS):
             p16 = R("P16", 256 * t + lo, 256 * t + hi)
-            mm(la, R("I"), p16, True, False)
-            mm(lb, R("I"), p16, True, False)
-            mm(lb, one64, R("cst", 0, hi - lo, 1, 64), False, False)
+            mm(la, R("I"), p16, True)
+            mm(lb, R("I"), p16, True)
         if t == 0:
-            terms = [R("RC")]
-            mm(R("B7", 0, 128), R("RC"), R("Bo"))
-            mm(R("B4", 0, 128), R("BoC"), R("RC"))
+            tops(R(BF, 0, 128), R("RC"))
+            act(R("rc"), R(BF, 0, 128), F.Relu)
+            mms(spread, [(R("I"), R("off")), (R("rc"), R("Bo"))])
+            act(R("xm"), spread, F.Relu, scale=-1.0, bias=256.0)
+            for x in twice:
+                mm(x, R("nBo"), R("rc"), x is twice[0])
+            act(R("thr", 0, 256), R(BQ, 0, 256), scale=c15, bias=b256)
         else:
-            rn, zq, uq = part("RN", t - 1), part("zp", t - 1), part("uu", t - 1)
-            terms = [btp, R("t2"), R("t3")]
-            tt(R("t2"), IND(R("WD", 144 * (t - 1), 144 * t), R("PM%d" % t, 0, 8)), rn, A.mult)
-            line("start")
-            tt(R("t3"), R("B3", 128, 256), rn, A.mult)
-            line("start")
-            tt(R("gg"), R("B3", 384, 512), part("RG", t - 1), A.mult)
-            line("start")
-            tt(uq, R("B2", 384, 512), R("gg"), A.mult)
-            line("start")
-            mms(R("B7", 0, 128), [(x, R("I")) for x in terms])
-            mms(R("B4", 0, 128), [(R("I15"), x) for x in terms])
-        tt(R("xm"), R("B7", 0, 128), R("mask"), A.mult)
-        line("start")
-        if t > 0:
-            tt(IND(Zall, src_list(t - 1)), zq, uq, A.add)
-            line("start")
-        act(thr0, R("B4", 0, 128))
-        act(R("thr", 128, 256), thr0)
+            rb, zq, uq = part("RB", t - 1), part("zp", t - 1), part("uu", t - 1)
+            mms(spread, [(R("nI"), R("off")), (rb, R("Bo"))])
+            for x in twice:
+                mm(x, R("Bo"), rb, x is twice[0])
+            mm(spread, R("t2"), R("Wall"))
+            for x in twice:
+                mm(x, R("Wall"), R("t2"))
+            act(R("xm"), spread, F.Relu)
+            take_tops(t - 1, Zall)
+            act(R("thr", 0, 256), R(BQ, 0, 256), scale=c15)
         sel(R("thr", 256, 512), R("thr", 0, 256), [[0, 256]], A.is_ge, 0, 0)
-        line("copy")
         for (lo, hi, la, lb) in LISTS:
             q = R("q", lo, hi)
-            mm(la, R("xm"), R("Q97", lo, hi), False, True)
-            mm(lb, R("xm"), R("Q97", lo, hi), False, False)
+            mm(la, R("xm"), R("Q97", lo, hi))
+            mm(lb, R("xm"), R("Q97", lo, hi))
             act(q, la, bias=135.0 + 513.0 / 8192, scale=1.0 / W)
-            mm(lb, R("m4k"), q, False, True)
-        cp(R("cu", 0, CUT), LISTS[0][3])
-        mms(R("B4", 128, 256), [(R("Bo") if t == 0 else R("I"), x) for x in terms])
-        act(bt, R("B4", 128, 256))
-        if t == 0:
-            turn1(0, "B4")
-            turn2(0, "B6")
-        else:
+            mm(lb, R("m4k"), q)
+        ts(R("cu", 0, CUT), LISTS[0][3], LIFT, A.add)
+        if last and AFTER:
+            put_days(48, 0, "rd", "rf")
+        if t == 1:
+            act(R("ld"), part("RN", 0), F.Relu)
+        if t:
             act(zo, IND(Zw, src_list(t)))
-            send([(STEP[t], zo, zr, "z%d" % t)], 2.5)
-            line("copy")
-            act(so, zo, F.Sign)
-        mms(R("B6", 264, 272), [(one64, R("c26", 0, 8, 1, 64)), (thr0, R("W97", 0, 8))])
+            send([(STEP[t], zo, zr, "z%d" % t)])
+        else:
+            cp(R("rl", 0, 8), R("RT", 0, 8))
+            ts(R("rl", 8, 16), R("RT", 8, 16), float(W), A.subtract)
+            iota(R("Mb"), [[0, 8], [-1, 16]], 2, 0)
+            sel(R("nC1"), R("nBo"), [[0, 8], [1, 16]], A.is_equal, -1, 0)
+            sel(R("Mb"), R("Mb"), [[0, 8], [-1, 16]], A.is_ge, 3, 0)
+            sel(R("C2"), R("Bo"), [[0, 8], [1, 16]], A.is_equal, -2, 0)
+            sel(R("Mb"), R("Mb"), [[-16, 8], [0, 16]], A.is_ge, 0, 1)
+            sel(R("IUp"), R("nBo"), [[-1, 128]], A.is_equal, -1, 1)
+            sel(R("Mb"), R("Mb"), [[16, 8], [0, 16]], A.is_ge, 15, -1)
+            sel(R("Ma"), R("Mb"), [[0, 8], [1, 16]], A.is_ge, -1, 0)
+            sel(R("IUp"), R("IUp"), [[-1, 128]], A.not_equal, 0, 1, 1.0)
+            iota(R("nL"), [[16, 8]], V - 2048, 1)
+        mm(R(KEY, 0, 264), thr0, R("W97", 0, 264), True)
+        mm(R(KEY, 32, 264, 33), rows("ones", 0), rows("c33", 0, 0, 8), kind="sum")
+        turn2(t)
         for (k0, k1) in VCH[t]:
             tt(R("cmp", 128 * k0, 128 * k1), IND(Zc, R("cu", 8 * k0, 8 * k1)), R("thr", 0, 128 * (k1 - k0)), A.is_gt)
-            line("compare")
             if k0 == 0:
-                cp(R("cu", CUT, 256), LISTS[1][3])
-                line("compare")
+                ts(R("cu", CUT, 256), LISTS[1][3], LIFT, A.add)
             for k in range(k0, k1):
-                tier_sum(R("B0", k, 264, 33), [(part("cmp", k), R("Wv", 0, 8))])
+                tier_sum(k, part("cmp", k), "Wv")
         for j, sign in ((0, False), (1, False), (0, True), (2, False), (1, True), (2, True)):
             k0, k1 = SCH[t][j]
             n = 128 * (k1 - k0)
-            raw, bank = R("raw", 512 * j, 512 * j + n), R(("B1", "B2", "B7")[j], 0, n)
+            raw, bank = R("raw", 512 * j, 512 * j + n), R((BR, BQ, BP)[j], 0, n)
             if not sign:
                 act(raw, IND(Zc, R("cu", 8 * k0, 8 * k1)))
-                line("gather")
                 mms(bank, [(R("nI"), R("thr", 0, n)), (R("I"), raw)])
                 continue
+            if j == 2:
+                mms(R(BD, 0, 128), [(R("nI"), thr0), (R("I"), zr)])
+                act(R("s33"), R(BD, 0, 128), F.Sign, bias=-0.5)
+                tier_sum(32, R("s33"), "W33")
             act(R("cmp", 128 * k0, 128 * k1), bank, F.Sign, bias=-0.5)
-            line("gather")
             for k in range(k0, k1):
-                tier_sum(R("B0", k, 264, 33), [(one32, R("cS", 0, 8, 1, 32)), (part("cmp", k), R("Ws", 0, 8))])
-        mms(R("B5", 0, 128), [(R("nI"), thr0), (R("I"), zr)])
-        act(R("s33"), R("B5", 0, 128), F.Sign, bias=-0.5)
-        soon(0.6)
-        tier_sum(R("B0", 32, 264, 33), [(one32, R("c33", 0, 8, 1, 32)), (R("s33"), R("W33", 0, 8))])
-        mm(R("B5", 128, 256), R("BoR"), R("s33"))
-        act(R("nask"), R("B5", 128, 256), F.Relu, bias=-14.0 * BIG, scale=-BIG)
-        mms(R("B1", 0, 128), [(R("I"), R("bar0")), (R("I"), R("nask"))])
-        act(R("bar"), R("B1", 0, 128))
-        if last:
-            mms(R("B1", 256, 384), [(R("Up"), so), (R("nE0"), so)])
-            act(R("gg"), R("B1", 256, 384))
+                tier_sum(k, part("cmp", k), "Ws")
+        aim, vs = R(BU, 0, 128), R(BF, 0, 128)
+        res, s1, s2 = part("res", t % 2), part("s12", 0), part("s12", 1)
+        if t:
+            done = to_days(zq, uq, "re")
         if not last:
-            act(R("sgz"), zr, F.Sign)
-            mms(R("B7", 384, 512), [(R("Up"), R("sgz")), (R("nUp2"), R("sgz"))])
-            tt(R("sec"), R("B7", 384, 512), zr, A.mult)
-            turn1(t + 1, "B5")
-        if not last:
+            tops(R(BR, 0, 128), zr)
+            tops(R(BR, 128, 256), zr, True)
+            act(R("s12"), R(BR, 0, 256), F.Relu)
             act(part("zz", 3), IND(R("Z", W, V), R("jo", 8 * t, 8 * t + 8)))
-            act(part("tt", 3), part("zz", 3), F.Sign)
-            mm(R("B1", 128, 256), R("TopM"), part("tt", 3))
-            tt(part("bt", 2 * t), R("B1", 128, 256), part("zz", 3), A.mult)
-            send([(STEP[t + 1], R("bt", 256 * t, 256 * t + 256), R("RB", 256 * t, 256 * t + 256), "s%d" % t)], 1.5)
-        if t == 1:
-            send([(STEP[2], R("pm2"), R("PM2"), "p2")], 3.0)
-        if t > 0:
-            put_days(24 * t - 16, zq, uq, "B2", "re%d" % (t - 1))
-        ends = R("kp", 264 * t + 32, 264 * t + 264, 33)
-        tt(ends, R("B6", 264, 272), ends, A.add)
-        soon(0.5)
-        scan(R("sc"), R("kp", 264 * t, 264 * t + 264), R("B0", 0, 264), A.add, A.min)
+            tops(R(BQ, 0, 128), part("zz", 3))
+        if t:
+            done()
+        mm(R(BD, 128, 256), nBoR, R("s33"), True)
+        act(R("nask"), R(BD, 128, 256), F.Relu, bias=-14.0 * HIT, scale=HIT)
+        if last:
+            mms(R(BR, 0, 128), [(R("I"), R("bar0")), (R("I"), R("nask")), (R("I"), R("nask"))])
+            act(R("bar"), R(BR, 0, 128))
+        else:
+            act(res, R(BQ, 0, 128), F.Relu)
+            send([(STEP[t + 1], res, part("RB", t), "s%d" % t)])
+            both = [(R("I"), R("ld"))] * t + [(R("nC1"), s2), (R("nI"), R("nask"))]
+            mms(R(BP, 0, 128), [(R("Mb"), s1)] + both + [(R("C2"), res)])
+            mms(vs, [(R("Ma"), s1)] + both)
+        if t:
+            act(R("so"), zo, F.Sign)
+        else:
+            act(R("B4k"), R("Bo"), scale=4096.0)
+            act(R("nE0"), R("nBo"), scale=R("LT", 1, 2))
+            const(R("farm"), -BIG)
+            act(wrow, tier, F.Square, bias=-1.5)
+            act(R("farm", 0, 128, 16), R("nL"))
+            act(wrow, wrow, bias=-1.25)
+            act(R("WD", 128, 144), R("ones", 0, 16), scale=0.0, bias=c256)
+            act(wrow, R("mask", 0, 1), scale=-0.5, bias=wrow)
+        if t == 0:
+            note_slots(0)
+        if last:
+            put_days(48, 1, "rd", "rf")
+        scan(R("sc"), R("st%d" % KS[t], 0, 264), R(KEY, 0, 264), A.add, A.min)
+        if not last:
+            narrow(t + 1, 0)
         ts(R("km"), R("sc", 32, 264, 33), (3 << 22) | (W - 1), A.bitwise_and)
+        if not last:
+            narrow(t + 1, 1)
         ts(R("A16"), IND(R("km"), R("ex")), 8192.0, A.min, 2048.0, A.subtract)
-        if not last:
-            mms(R("B3", 384, 512), [(R("Up"), so), (R("nE0"), so)])
-        tt(R("B16"), R("B3", 0, 128), R("A16"), A.mult)
-        if not last:
-            mms(R("B3", 256, 384), [(R("Bo"), R("sec")), (R("nI"), bt)])
-        aim = R("B2", 128, 256)
-        mm(R("B6", 0, 128), R("A16"), R("I"))
-        mm(R("B6", 128, 136), R("B16"), grp)
-        mm(R("B4", 0, DW), R("I"), R("tri"), True, False)
+        if t == 0:
+            times([("Row4", "nBo", R("mask", 4, 5)), ("Up", "nU1", -1.0 / 256)])
+        if t == 1:
+            ts(R("bar0"), R("off"), float(W), A.add)
+        tt(R("B16"), cap, R("A16"), A.min)
+        if t:
+            put_days(24 * t - 16, 0, "re")
+        else:
+            note_slots(4)
+        mm(R(BD, 128, 136), R("off"), grp, True)
+        mm(R(BD, 0, 128), R("A16"), R("I"))
+        mm(R(BD, 128, 136), R("B16"), grp)
+        mms(R(BE, 0, DW), [(R("off"), R("RD")), (R("I"), R("tri"))])
         for (c0, c1, first) in DSEG:
-            mm(R("B4", c0, c1), R("A16"), R("I", first, 128), False, False)
-        mm(R("B4", 0, DW), R("B16"), R("RD"), False, True)
-        act(R("sp"), R("B4", 0, DW), F.Sign, bias=0.5)
-        act(R("sm"), R("B4", 0, DW), F.Sign, bias=0.5, scale=-1.0)
-        mm(aim, R("I"), R("off"), True, False)
-        mm(aim, R("A16"), R("I"), False, False)
-        for q in range(NV):
-            e = R("E", EOFF[q], EOFF[q + 1])
-            ts(e, R("B6", 16 * q + 16, 128), R("B6", 128 + q, 129 + q), A.is_equal, 2.0, A.mult)
-            line("equal")
-            if q in (NV - 3, NV - 1):
-                for (c0, c1, first) in DSEG:
-                    mm(R("B2", 128 + first, 256), R("B4k"), R("sm" if q == NV - 1 else "sp", c0, c1), False, False)
-            mm(R("B2", 128 + 16 * q + 16, 256), R("B4k"), e, False, q == NV - 1)
-        ts(R("dU"), R("B6", 128, 136), 2048.0, A.add, float(W - 1), A.min)
-        gone = part("G", t)
-        tt(gone, aim, R("bar"), A.is_lt)
+            mm(R(BE, c0, c1), R("A16"), R("I", first, 128))
+        mm(R(BE, 0, DW), R("B16"), R("RD"))
+        act(R("sp"), R(BE, 0, DW), F.Sign, bias=0.5)
+        act(R("sm"), R(BE, 0, DW), F.Sign, bias=0.5, scale=-1.0)
         if not last:
-            nl = part("NL", t, 144)
-            tt(nl, aim, R("bar0"), A.is_ge)
-            tt(part("wn", t), R("B3", 256, 384), gone, A.mult)
+            act(R("T2"), R(BP, 0, 128), bias=c256)
+        mms(aim, [(R("I"), R("off")), (R("A16"), R("I"))])
+        sums = BU if last else BF
+        for q in range(-1, NV + 1):
+            if q == (-1 if last else NV):
+                ts(R("dU"), R(BD, 128, 136), 2048.0, A.add, float(W - 1), A.min)
+            if 0 <= q < NV:
+                e = R("E", EOFF[q], EOFF[q + 1])
+                ts(e, R(BD, 16 * q + 16, 128), R(BD, 128 + q, 129 + q), A.is_equal, 2.0, A.mult)
+                mm(R(sums, 16 * q + 16, 128), R("B4k"), e, kind="sum")
+        for x in ("sp", "sm"):
+            for (c0, c1, first) in DSEG:
+                mm(R(sums, first, 128), R("B4k"), R(x, c0, c1), kind="sum")
+        if t:
+            put_days(24 * t - 16, 1, "re")
+        else:
+            read_slots(0)
+        gone = part("G", t)
+        if last:
+            tt(gone, aim, R("bar"), A.is_lt)
+        else:
+            nl = part("NL", t)
+            tt(nl, R("T2"), vs, A.subtract)
+            ts(part("wn", t), vs, 0.0, A.min, c256, A.add)
+            ts(gone, vs, 1024.0, A.is_le)
             send([(STEP[t + 1], nl, part("RN", t), "n%d" % t),
                   (STEP[t + 1] - STEP[t], part("wn", t), part("WD", t, 144), "w%d" % t)])
+            mm(aim, R("Row4"), nl)
+        if t == 0:
+            scan(R("js"), R("rst"), R("jm"), A.mult, A.add)
+            ts(R("far"), R("trk", 8, 24), 2048.0, A.subtract)
         send([(-STEP[t], gone, part("RG", t), "g%d" % t)])
+        if t == 0:
+            send([(STEP[2], R("pm2"), R("PM2"), "p2")])
         lo = 0 if last else 24 * (t + 1)
         scan(R("ll"), R("farm"), aim, A.max, A.min)
-        ts(R("SL", lo, lo + 8), R("ll", 15, 128, 16), 2048.0, A.add)
-        St, Sw = (Yall, Yw) if last else (Zall, Zw)
-        act(R("ed"), IND(Zc, R("dU")), F.Relu, bias=1.0, scale=-1.0)
-        act(R("zd"), IND(Sw, R("dU")))
-        mm(R("B5", 0, 128), R("FstE"), R("ed"))
-        if last:
-            act(R("braw"), bt, bias=256.0, scale=-1.0)
-        tt(R("fd"), R("B5", 0, 128), R("braw") if last else bt, A.mult)
-        tt(IND(St, R("SL", lo, lo + 8)), R("zd"), R("fd"), A.add)
-        (cp if last else act)(zp, IND(Sw, src_list(t)))
-        mm(R("B2", 384, 512), R("TopM"), zp)
-        if t == 1:
-            put_days(lo, R("zd"), R("fd"), "B4", "rd")
-        if not last:
-            tt(R("mx"), R("ll", 15, 128, 16), R("far", 8 * t, 8 * t + 8), A.min)
-            ts(R("SL", lo + 8, lo + 16), R("mx"), 2048.0, A.add)
-            turn2(t + 1, "B1")
         if t == 0:
-            act(R("nj"), IND(R("NL", 0, 144), R("jx1")))
-            tt(R("zj"), part("jm", 1), R("nj"), A.mult)
-            scan(R("lj"), R("rst"), R("zj"), A.mult, A.add)
-            ts(R("pm2", 0, 8), R("lj", 15, 128, 16), 128.0, A.add)
+            list_slots(0)
+        ts(R("SL", lo, lo + 8), R("ll", 15, 128, 16), 2048.0, A.add)
         if not last:
-            res, btp = part("RB", 2 * t), part("RB", 2 * t + 1)
-            mms(R("B3", 128, 256), [(R("Bo"), res), (R("nI"), btp)])
+            tt(R("mx", 0, 8), R("ll", 15, 128, 16), R("far", 8 * t, 8 * t + 8), A.min)
+        St, Sw = (Yall, Yw) if last else (Zall, Zw)
+        first = [(R("nI256"), R("ed")), (R("D1"), R("ed"))]
+        act(R("ed"), IND(Zc, R("dU")), F.Relu, bias=1.0, scale=-1.0)
+        if not last:
+            act(R("zd"), IND(Sw, R("dU")))
+        mms(R(BR, 0, 128), [(R("E0" if last else "nE0"), thr0)] + first)
+        act(R("fd"), R(BR, 0, 128), F.Relu, scale=-1.0, bias=0.0 if last else -256.0)
+        if last:
+            act(R("zd"), IND(Sw, R("dU")))
+        tt(IND(St, R("SL", lo, lo + 8)), R("zd"), R("fd"), A.add)
+        if not last and not AFTER:
+            ts(R("SL", lo + 8, lo + 16), R("mx", 0, 8), 2048.0, A.add)
+        if t == 0:
+            ts(R("Wall"), R("Bo"), wrow, A.mult, lt4, A.mult)
+            act(R("E0"), R("nE0"), scale=-1.0)
+            act(R("WD", 272, 288), R("ones", 0, 16), scale=0.0, bias=c256)
+        mms(R(KEY, 0, 128), [(R("Up"), R("so")), (R("nE0"), R("so"))])
+        if not last:
+            if not DIRECT:
+                act(R("gg"), R(KEY, 0, 128))
+            turned = turn1(t + 1)
+            if not AFTER:
+                turned()
+        if t == 1:
+            mms(R(BR, 128, 256), [(R("nI256"), R("ed")), (R("nI"), R("zd"))])
+            mms(R(BR, 256, 384), [(R("E0"), thr0)] + first)
+            act(R("rd"), R(BR, 128, 256), bias=256.0)
+            act(R("rf"), R(BR, 256, 384), F.Relu, scale=-1.0)
+            if not AFTER:
+                put_days(lo, 0, "rd", "rf")
+        act(zp, IND(Sw, src_list(t)))
+        mm(shift, R("IUp"), zp, True)
 
-    tt(R("B3", 384, 512), R("B2", 384, 512), R("gg"), A.mult)
-    tt(uu, R("B3", 384, 512), part("RG", 2), A.mult)
-    tt(IND(Yall, src_list(2)), zp, uu, A.add)
-
+    take_tops(2, Yall)
     dma("y", T.y[:], T.Y[:, 0:V], Yw, store=True)
 
     cnt = {s: 0 for s in ESEM.values()}
@@ -652,6 +731,16 @@ def rank_program(g, core, T, topo):
             note(c, (c["lands"], landed[c["lands"]]))
     if not ORDER:
         ORDER.extend(plan(calls))
+    closing = set(SCRATCH)
+    for j in reversed(ORDER):
+        c = calls[j]
+        if c["e"] == "p":
+            bank = c["writes"][0][0]
+            if bank in closing:
+                c["stop"].append(True)
+                closing.remove(bank)
+            if c["start"]:
+                closing.add(bank)
     for j in ORDER:
         c = calls[j]
         e = c["e"]

from concourse.bass import DstId, RemoteDMATransfer
from concourse.mybir import AluOpType as A, ActivationFunctionType as F

N, W, V, S, K = 8, 4096, 4608, 128, 32
STEP = (1, 2, 3)
KS = (16, 16, 16)
SCH = [[(4, 8), (8, 12), (12, _k)] for _k in KS]
VCH = [[(0, 2), (2, 4), (_k, _k + 4), (_k + 4, _k + 8), (_k + 8, _k + 12), (_k + 12, 31), (31, 32)] for _k in KS]
UNIT = 1 << 18
BIG, OFF = float(1 << 24), 8192.0
HIT = 8192.0
CUT = 64
NV = 6
EOFF = [0, 112, 208, 288, 352, 400, 432]
DSEG = [(0, 128, 0)]
for _q in range(NV, 7):
    DSEG.append((DSEG[-1][1], DSEG[-1][1] + 112 - 16 * _q, 16 * _q + 16))
DW = DSEG[-1][1]
KEY, BP, BQ, BR, BU, BD, BE, BF = ("B%d" % _b for _b in range(8))
LOADS = [(0, 1536), (1536, 3072), (3072, 4608)]
MID = 6
ZBANK = (BP, BQ, BU, BR, BF, BD, BR, BE, BU)
ZADD = (7, 8)

CYCLE, LINK, GATHER, SCATTER, SCALAR = 0.001, 0.11, 1.56, 3.8, 1.0
ISSUE, FIRST, HOP, HOP2, DMA0, ROW, RATE = 0.4, 2.3, 1.22, 1.45, 1.75, 0.015, 20000.0
AFTER, DIRECT = False, False
TRIES = 100

bf, f32, i32, u16, f16 = "bfloat16", "float32", "int32", "uint16", "float16"
SIZE = {bf: 2, f32: 4, i32: 4, u16: 2, f16: 2}
SCRATCH = {}
WHERE = {}
for _n, _w, _d in [
    ("Y", V + 240, bf), ("Z", V + 240, bf), ("t256", V, bf), ("trk", 24, i32), ("cnd", 768, i32),
    ("P16", 768, f16), ("X", 768, f16),
    ("ic", 16, i32), ("ex", 8, u16), ("JT", V + 512, bf), ("jo", 16, u16), ("SL", 72, u16), ("dU", 8, u16),
    ("rc0", 128, bf), ("RC", 128, bf), ("zz", 512, bf), ("ZR", 384, bf), ("res", 256, bf), ("RB", 256, bf),
    ("RT", 16, i32), ("rl", 16, u16), ("PM1", 8, u16), ("pm2", 8, u16), ("PM2", 8, u16),
    ("RG", 384, bf), ("NL", 256, bf), ("RN", 256, bf), ("wn", 256, bf), ("G", 384, bf),
    ("WD", 288, bf), ("q", 256, bf), ("cu", 256, u16),
    ("thr", 512, bf), ("cmp", 4096, bf), ("raw", 1536, bf), ("sc", 264, i32), ("km", 8, i32),
    ("A16", 128, f16), ("B16", 128, f16), ("E", 432, bf), ("sp", DW, bf), ("sm", DW, bf),
]:
    SCRATCH[_n] = ("sbuf", [128, _w], _d)
    WHERE[_n] = (_n, 0, _w)


def _pack(buf, dt, items):
    c = 0
    for n, w in items:
        WHERE[n] = (buf, c, w)
        c += w
    SCRATCH[buf] = ("sbuf", [128, c], dt)


_pack("small", f32, [("fc", 8), ("LT", 16), ("nL", 8), ("far", 16), ("mx", 8), ("farm", 128), ("ll", 128), ("T2", 128)]
      + [("st%d" % _k, 264) for _k in sorted(set(KS))])
_pack("konst", bf, [(_n, 128) for _n in (
    "ones", "G16", "R16", "I", "nI", "nI256", "m4k", "Bo", "nBo", "nE0", "E0", "bar0", "Up", "IUp", "nU1",
    "nU2", "D1", "mask", "turn", "B4k", "off", "jn", "rst", "Wall", "Row4", "Ma", "Mb", "C2", "nC1")]
      + [("Q97", 256), ("RD", DW), ("tri", DW), ("cols", 16), ("GE", 16), ("Wv", 16), ("Ws", 16), ("W33", 16),
         ("c33", 16), ("W97", 272)])
_pack("work", bf, [(_n, 128) for _n in (
    "s33", "nask", "bar", "gg", "ed", "zd", "fd", "ra", "rd", "re", "rf", "t2", "xm", "rc", "so", "ld", "jm", "js")]
      + [("s12", 256), ("zp", 384), ("uu", 384)])
for _b in range(8):
    SCRATCH["B%d" % _b] = ("psum", [128, 512], f32)
    WHERE["B%d" % _b] = ("B%d" % _b, 0, 512)

ARR = ["b0", "me", "p2", "z0", "z1", "z2", "s0", "s1", "g0", "g1", "g2", "n0", "n1", "w0", "w1"]
SEMAPHORES = ["ev", "es", "ep", "eg", "sent"] + ["d%d" % _i for _i in range(10)] + ARR


def clashes(hist, e, reads, writes):
    out = []
    for regs, wr in ((reads, False), (writes, True)):
        for (n, lo, hi) in regs:
            ps = SCRATCH[n][0] == "psum"
            for (l2, h2, w2, e2, tok) in hist.get(n, []):
                if (ps and (e2 != e or e == "p")) or (lo < h2 and l2 < hi and (wr or w2)):
                    out.append((e2, tok, not e2 == e == "p"))
    return out


def plan(calls):
    hist, before, sender, last = {}, [], {}, {}
    for j, c in enumerate(calls):
        for s in c["sems"]:
            sender[s] = j
    for j, c in enumerate(calls):
        pre = {}
        for (e2, i, wait) in clashes(hist, c["e"], c["reads"], c["writes"]):
            if e2 == "r":
                pre[sender[i]] = max(pre.get(sender[i], 0.0), calls[sender[i]]["hop"])
            elif not c["kind"] == calls[i]["kind"] == "sum":
                pre[i] = max(pre.get(i, 0.0), LINK if wait else 0.0)
        if c["line"] in last:
            pre.setdefault(last[c["line"]], 0.0)
        if c["line"]:
            last[c["line"]] = j
        before.append(pre)
        tok = c["lands"] if c["e"] == "r" else j
        for regs, wr in ((c["reads"], False), (c["writes"], True)):
            for (n, lo, hi) in regs:
                hist.setdefault(n, []).append((lo, hi, wr, c["e"], tok))
    after = [[] for _ in calls]
    for j, pre in enumerate(before):
        for i, lat in pre.items():
            after[i].append((j, lat))
    real = [j for j, c in enumerate(calls) if c["e"] != "r"]

    def place(more):
        tail, end, held, busy = {}, {}, {}, {}
        for j in reversed(real):
            tail[j] = calls[j]["cost"] + calls[j]["soon"] + more.get(j, 0.0) + max(
                [lat + calls[k]["lead"] + tail[k] for k, lat in after[j]] + [0.0])
        for j in sorted(real, key=lambda x: (-tail[x], x)):
            c = calls[j]
            t, held[j] = max([(end[i] + lat, (i, False)) for i, lat in before[j].items()] + [(0.0, None)],
                             key=lambda x: x[0])
            t += c["lead"]
            lane = busy.setdefault("d" if c["lead"] else c["e"], [])
            at = len(lane)
            while at > 0 and lane[at - 1][1] > t + 1e-9:
                at -= 1
            while at < len(lane) and t + c["cost"] > lane[at][0] + 1e-9:
                t, held[j] = lane[at][1], (lane[at][2], True)
                at += 1
            lane.insert(at, (t, t + c["cost"], j))
            end[j] = t + c["cost"]
        return max(end.values()), end, held, tail

    more, tried = {}, set()
    best = place(more)
    for _ in range(TRIES):
        total, end, held, tail = best
        j, pick = max(end, key=end.get), None
        while held[j] and pick is None:
            i, queued = held[j]
            if queued and (i, j) not in tried:
                pick = (i, j)
            j = i
        if pick is None:
            break
        tried.add(pick)
        other = dict(more)
        other[pick[1]] = more.get(pick[1], 0.0) + tail[pick[0]] - tail[pick[1]] + 0.01
        got = place(other)
        if got[0] < total - 1e-6:
            more, best = other, got
    end = best[1]
    return sorted(real, key=lambda x: (end[x] - calls[x]["cost"] - calls[x]["lead"], end[x], x))


ORDER = []


def rank_program(g, core, T, topo):
    rank = T.rank_of(core)
    if rank is None:
        return
    Q = {"v": g.vector, "s": g.scalar, "p": g.tensor, "g": g, "y": g.sync}
    ESEM = {"v": "ev", "s": "es", "p": "ep", "g": "eg"}
    calls = []

    def R(name, lo=0, hi=None, step=1, parts=128, p0=0):
        buf, c0, w = WHERE[name]
        lo, hi = c0 + lo, c0 + (w if hi is None else hi)
        ap = T[buf][p0:parts, lo:hi] if step == 1 else T[buf][p0:parts, lo:hi:step]
        return (ap, [(buf, lo, hi)], [], len(range(lo, hi, step)), SIZE[SCRATCH[buf][2]], SCRATCH[buf][0] == "psum")

    def IND(win, off):
        return (win[0].indirect(off[0]), win[1], off[1], 16 * off[3], win[4], False)

    def call(e, issue, reads, writes, cost, lead=0.0, hop=0.0, sems=(), lands=None, kind="op"):
        calls.append(dict(e=e, issue=issue, reads=reads, writes=writes, cost=cost, lead=lead, hop=hop, sems=sems,
                          lands=lands, kind=kind, line=e if e in "vsg" and kind != "dma" else None, soon=0.0))

    def soon(us):
        calls[-1]["soon"] = us

    def op(e, issue, out, ins, rate):
        ins = [x for x in ins if isinstance(x, tuple)]
        cost = max(64.0, rate * out[3]) * CYCLE
        if out[2]:
            cost = 0.056 + SCATTER * out[3] * CYCLE
        elif any(x[2] for x in ins):
            cost = 0.06 + GATHER * out[3] * CYCLE
        elif e == "p":
            cost = max(min(64, ins[0][3]), out[3]) * CYCLE / 2
        elif e == "g":
            cost = 0.18 + 2 * out[3] * CYCLE
        if e == "s":
            cost *= SCALAR
        call(e, issue, out[2] + [r for x in ins for r in x[1] + x[2]], out[1], cost)

    def ap(x):
        return x[0] if isinstance(x, tuple) else x

    def wide(*xs):
        return 1.0 if any(x[4] == 4 for x in xs if isinstance(x, tuple)) else 0.5

    def mset(o, c):
        op("v", lambda: g.vector.memset(o[0], c), o, [], wide(o))

    def cp(o, i):
        op("v", lambda: g.vector.tensor_copy(o[0], i[0]), o, [i], wide(o, i))

    def tt(o, a, b, f):
        op("v", lambda: g.vector.tensor_tensor(o[0], a[0], b[0], f), o, [a, b], 1.0 if a[5] or b[5] else 2.0)

    def ts(o, a, s1, f0, s2=None, f1=None):
        if f1 is None:
            op("v", lambda: g.vector.tensor_scalar(o[0], a[0], ap(s1), None, f0), o, [a, s1], wide(o, a, s1))
        else:
            op("v", lambda: g.vector.tensor_scalar(o[0], a[0], ap(s1), ap(s2), f0, f1), o, [a, s1, s2],
               wide(o, a, s1, s2))

    def scan(o, d0, d1, f0, f1):
        op("v", lambda: g.vector.tensor_tensor_scan(o[0], d0[0], d1[0], 0.0, f0, f1), o, [d0, d1], wide(o, d0, d1))

    def act(o, i, fn=F.Identity, bias=0.0, scale=1.0):
        op("s", lambda: g.scalar.activation(o[0], i[0], fn, bias=ap(bias), scale=ap(scale)), o, [i, scale, bias], 1.0)

    def mm(o, l, r, start=False, kind="op"):
        stop = []
        op("p", lambda: g.tensor.matmul(o[0], l[0], r[0], start, bool(stop)), o, [l, r], 1.0)
        calls[-1].update(kind=kind, start=start, stop=stop)

    def mms(o, pairs):
        for j, (l, r) in enumerate(pairs):
            mm(o, l, r, j == 0)

    def iota(o, pat, base, cm, fl=True):
        if fl:
            op("g", lambda: g.iota(o[0], pat, base, cm, allow_small_or_imprecise_dtypes=True), o, [], 2.0)
        else:
            op("g", lambda: g.iota(o[0], pat, base, cm), o, [], 2.0)

    def sel(o, i, pat, cmpop, base, cm, fill=0.0):
        op("g", lambda: g.affine_select(o[0], i[0], pat, cmpop, fill, base, cm), o, [i], 2.0)

    def dma(e, o, i, x, store=False, behind=()):
        call(e, lambda: Q[e].dma_start(o, i), (x[1] if store else []) + list(behind), [] if store else x[1],
             8 * (ROW + x[3] * x[4] / RATE), lead=DMA0, kind="dma")

    def lanes(d, part, of):
        en = topo.engines(core, T.cores[(rank + d) % N])
        n = len(en) // of
        m = 0
        for x in en[part * n:(part + 1) * n]:
            m |= 1 << x
        return m, n

    sent, landed = [0], {}

    def send(items, late=0.0):
        trs = []
        for j, (d, src, dst, s) in enumerate(items):
            rid, pid, _ = topo.addr(T.cores[(rank + d) % N])
            m, n = lanes(d, j, len(items))
            trs.append((rid, pid, m, s, src[0], dst[0]))
            sent[0] += n
            landed[s] = landed.get(s, 0) + len(topo.engines(T.cores[(rank - d) % N], core)) // len(items)

        def issue():
            if len(trs) == 1:
                rid, pid, m, s, src, dst = trs[0]
                g.remote_dma(dst, src, T.sem[s], T.sem.sent, pid, rid, m)
            else:
                g.remote_dma_fused([RemoteDMATransfer(dst_ids=[DstId(rid=rid, pnc=pid)], dma_engine_mask=m,
                                                      remote_sem=T.sem[s], src=src, dst=dst)
                                    for (rid, pid, m, s, src, dst) in trs], local_sem=T.sem.sent)

        first = not any(c["kind"] == "send" for c in calls)
        call("g", issue, [r for it in items for r in it[1][1]], [], ISSUE + (FIRST if first else 0.0),
             hop=(HOP if len(items) == 1 else HOP2) - ISSUE + late, sems=[it[3] for it in items], kind="send")

    def arrive(dsts, s):
        call("r", None, [], [r for x in dsts for r in x[1]], 0.0, lands=s, kind="land")

    def part(name, t, w=128):
        return R(name, w * t, w * t + 128)

    arrive([R("RC")], "b0")
    arrive([R("RT")], "me")
    arrive([R("PM2")], "p2")
    for t in range(3):
        arrive([part("ZR", t)], "z%d" % t)
        arrive([part("RG", t)], "g%d" % t)
    for t in range(2):
        arrive([part("RB", t)], "s%d" % t)
        arrive([part("RN", t)], "n%d" % t)
        arrive([part("WD", t, 144)], "w%d" % t)

    def src_list(t):
        return R("SL", 24 * t + 8, 24 * t + 16)

    def rows(name, h, lo=0, hi=None, step=1):
        return R(name, lo, hi, step, 32 * h + 32, 32 * h)

    dma("s", T.trk[:], T.trucks[:], R("trk"))
    soon(9.0)
    for (lo, hi) in LOADS:
        dma("y", T.Y[:, lo:hi], T.days[:, lo:hi], R("Y", lo, hi))
    dma("y", T.cnd[:, 0:256], T.cand[:, 0:256], R("cnd", 0, 256))

    pm127, pm128, pm129, pm130, tier, yard, bars, c256, b256, sq = (R("cols", j, j + 1) for j in range(10))
    c15, lt4, wcol, wrow = R("LT", 15, 16), R("LT", 4, 5), R("fc", 0, 1), R("fc", 1, 2)
    grp, ones, cap, nBoR = R("Bo", 0, 128, 16), R("ones"), R(KEY, 384, 512), R("RD", 0, 128)
    Yw, Zw, Zc, Yall, Zall = R("Y", 0, V), R("Z", 0, V), R("Z", 0, W), R("Y"), R("Z")

    def const(o, c, parts=128):
        act(o, R("ones", 0, o[3], 1, parts), scale=c)

    def times(pairs):
        for name, src, by in pairs:
            ts(R(name), R(src), by, A.mult)

    def table(h):
        return R("JT", W + 512 * h, V + 512 * h)

    def note_slots(c):
        cp(IND(R("JT", 0, V), R("rl", c, c + 4)), R("jn", 16 * c, 16 * c + 64))

    def read_slots(h):
        tt(R("jm"), IND(table(h), R(("rl", "jo")[h], 8, 16)), R("mask"), A.mult)

    def list_slots(h):
        ts(R(("PM1", "pm2")[h]), R("js", 15, 128, 16), 128.0, A.add)

    def mark(c):
        ts(R("t256", 512 * c, 512 * c + 512), R("Y", 512 * c, 512 * c + 512), 256.0, A.mult, 256.0, A.min)

    def mirror(c):
        y, z, m, bank = (R("Y", 512 * c, 512 * c + 512), R("Z", 512 * c, 512 * c + 512),
                         R("t256", 512 * c, 512 * c + 512), R(ZBANK[c]))
        if c in ZADD:
            mm(bank, R("nI"), y, True)
            tt(z, bank, m, A.add)
        else:
            mms(bank, [(R("nI"), y), (R("I"), m)])
            act(z, bank)

    mset(ones, 1.0)
    mset(table(0), 0.0)
    iota(R("ic", 0, 1), [[0, 1]], 0, 1, False)
    iota(R("jn"), [[1, 128]], -128, 0)
    iota(R("cols", 0, 4), [[-1, 4]], -127, 1)
    iota(R("R16"), [[0, 8], [1, 16]], 0, 0)
    iota(R("G16"), [[1, 8], [0, 16]], 0, 0)
    iota(R("Q97"), [[0, 32], [1, 8]], 0, 0)
    send([(STEP[1], R("trk", 0, 16), R("RT"), "me")], 3.0)
    mset(table(1), 0.0)
    ts(R("ic", 2, 3), R("ic", 0, 1), 15, A.bitwise_and)
    ts(R("ic", 3, 4), R("ic", 0, 1), 4, A.arith_shift_right)
    cp(R("cols", 4, 6), R("ic", 2, 4))
    ts(R("I"), R("jn"), pm128, A.is_equal)
    for k in sorted(set(KS)):
        for lo in (0, 128, 256):
            const(R("st%d" % k, lo, min(lo + 128, 264)), -float(W))
    const(R("c33", 0, 8, 1, 32), 14.75 * UNIT, 32)
    for k in sorted(set(KS)):
        for at, c in ((0, BIG), (4, -W - 15.5 * UNIT), (k, -W + 15.5 * UNIT), (32, 31.0 * W + 2048 + 97 * 256)):
            const(R("st%d" % k, at, 264, 33), c)
    act(R("rst"), R("R16"), F.Sign)
    times([("nI", "I", -1.0), ("nI256", "I", -256.0), ("m4k", "I", -4096.0)])
    ts(R("LT"), R("R16", 0, 16), tier, A.is_gt)
    ts(R("mask"), R("R16"), tier, A.is_equal)
    ts(R("GE"), R("R16", 0, 16), tier, A.is_le, -256.0, A.mult)
    act(b256, c15, scale=256.0)
    act(bars, c15, scale=38912.0, bias=-6144.0)
    act(wcol, c15, scale=-15.0 * UNIT, bias=16.0 * UNIT)
    ts(R("Bo"), R("G16"), yard, A.is_equal)
    ts(R("nBo"), R("G16"), yard, A.is_equal, -1.0, A.mult)
    ts(R("nU1"), R("jn"), pm129, A.is_equal, R("GE", 1, 2), A.mult)
    act(R("off"), R("mask"), scale=-OFF, bias=OFF)
    act(nBoR, R("nBo"), scale=c15)
    act(R("Wv", 0, 8), grp, scale=wcol)
    act(R("Ws", 0, 8), R("Wv", 0, 8), scale=0.5)
    act(R("W33", 0, 8), R("RD", 0, 128, 16), scale=-BIG / 2)
    for (c0, c1, first) in DSEG[1:]:
        for c in range(c0, c1, 16):
            act(R("RD", c, c + 16), R("nBo", first - 16, first))
    act(cap, R("mask"), scale=W + OFF, bias=-OFF)
    act(sq, tier, F.Square, bias=-2.0)
    const(R("tri", 128, DW), 0.0)
    cp(R("SL", 8, 16), R("trk", 0, 8))
    ts(R("jo"), R("trk", 8, 24), float(W), A.subtract)

    for c in range(MID):
        if c == 3:
            cp(IND(table(1), R("jo", 0, 8)), R("jn"))
        mark(c)
    read_slots(1)
    for c in range(MID):
        mirror(c)
    cp(R("rc0"), IND(Yw, src_list(0)))
    send([(STEP[0], R("rc0"), R("RC"), "b0")])
    sel(R("turn"), ones, [[-1, 16], [-16, 8]], A.is_equal, 0, 1)
    iota(R("W97", 0, 264), [[0, 264]], -97, 0)
    act(R("so"), R("rc0"), F.Sign)
    for c in range(MID, 9):
        mark(c)
    mirror(MID)
    mms(R(BP, 0, 128), [(R("I"), R("rc0")), (R("nI256"), R("so"))])
    act(part("zz", 0), R(BP, 0, 128), scale=-1.0)
    send([(STEP[0], part("zz", 0), part("ZR", 0), "z0")])
    sel(R("W97", 0, 264), R("W97", 0, 264), [[-16, 8], [0, 33]], A.is_equal, 0, 1)
    dma("y", T.cnd[:, 256:768], T.cand[:, 256:768], R("cnd", 256, 768), behind=part("ZR", 0)[1])

    def narrow(t, h=None):
        lo, hi = (256 * t, 256 * t + 256) if h is None else (256 * t + 128 * h, 256 * t + 128 * h + 128)
        ts(R("P16", lo, hi), R("cnd", lo, hi), 2048.0, A.subtract)

    def turn1(t):
        bank = BD if t else KEY
        for q in range(8):
            a, c0 = q // 2, (q % 2) * 128
            mm(rows(bank, a, c0, c0 + 128), R("P16", 256 * t + q, 256 * t + 256, 8), R("turn"), True)
        return lambda: cp(R("X", 256 * t, 256 * t + 256), R(bank, 0, 256))

    def turn2(t):
        for a in range(4):
            for gg in range(8):
                mm(rows(KEY, a, 33 * gg, 33 * gg + 32), R("X", 256 * t + gg, 256 * t + 256, 8),
                   R("I", 32 * a, 32 * a + 32), kind="sum")

    def tier_sum(k, x, w):
        mm(R(KEY, k, 264, 33), x, R(w, 0, 8), kind="sum")

    def tops(o, x, two=False):
        mm(o, R("I"), x, not two)
        mm(o, R("nU2" if two else "nU1"), x)

    narrow(0)
    ts(R("Q97"), R("Q97"), yard, A.is_equal, -97.0, A.mult)
    scan(R("js"), R("rst"), R("jm"), A.mult, A.add)
    for name, at, by in [("nU2", pm130, R("GE", 2, 3)), ("D1", pm127, b256)]:
        ts(R(name), R("jn"), at, A.is_equal, by, A.mult)
    list_slots(1)
    ts(R("tri", 0, 128), R("R16"), tier, A.is_le, bars, A.mult)
    ts(R("ex"), R("jn", 0, 8), 128.0, A.add)
    ts(c256, sq, 1.0, A.is_equal, 256.0, A.mult)
    for c in range(MID + 1, 9):
        mirror(c)
    turn1(0)()

    def to_days(z, dz, buf):
        mms(R(BF, 0, 128), [(R("I"), z), (R("I"), dz)])
        act(R("ra"), R(BF, 0, 128), F.Sign)
        mms(R(BF, 128, 256), [(R("I"), z), (R("I"), dz), (R("nI256"), R("ra"))])
        return lambda: act(R(buf), R(BF, 128, 256), scale=-1.0)

    def put_days(lo, h, a, b=None):
        out, x = IND(Yall, R("SL", lo + 4 * h, lo + 4 * h + 4)), R(a, 64 * h, 64 * h + 64)
        if b:
            tt(out, x, R(b, 64 * h, 64 * h + 64), A.add)
        else:
            cp(out, x)

    def take_tops(t, window):
        if t == 2 or DIRECT:
            tt(R("gg"), R(KEY, 0, 128), part("RG", t), A.mult)
            tt(part("uu", t), shift, R("gg"), A.mult)
        else:
            tt(R(KEY, 128, 256), shift, R("gg"), A.mult)
            tt(part("uu", t), R(KEY, 128, 256), part("RG", t), A.mult)
        tt(IND(window, src_list(t)), part("zp", t), part("uu", t), A.add)

    LISTS = [(0, CUT, R(BR, 0, CUT), R(BD, 0, CUT)),
             (CUT, 256, R(BE, 0, 256 - CUT), R(BU, 0, 256 - CUT))]
    spread, twice, shift = R(BP, 0, 128), [R(BQ, 0, 128), R(BQ, 128, 256)], R(BF, 0, 128)
    LIFT = 135.0 * W + 2304

    for t in range(3):
        last = t == 2
        zo, zr, zp = part("zz", t), part("ZR", t), part("zp", t)
        thr0 = R("thr", 0, 128)
        if t:
            tt(R("t2"), IND(R("WD", 144 * (t - 1), 144 * t), R("PM%d" % t, 0, 8)), part("RN", t - 1), A.max)
            if AFTER:
                turned()
                ts(src_list(t), R("mx", 0, 8), 2048.0, A.add)
        for j, (lo, hi, la, lb) in enumerate(LISTS):
            p16 = R("P16", 256 * t + lo, 256 * t + hi)
            mm(la, R("I"), p16, True)
            mm(lb, R("I"), p16, True)
        if t == 0:
            tops(R(BF, 0, 128), R("RC"))
            act(R("rc"), R(BF, 0, 128), F.Relu)
            mms(spread, [(R("I"), R("off")), (R("rc"), R("Bo"))])
            act(R("xm"), spread, F.Relu, scale=-1.0, bias=256.0)
            for x in twice:
                mm(x, R("nBo"), R("rc"), x is twice[0])
            act(R("thr", 0, 256), R(BQ, 0, 256), scale=c15, bias=b256)
        else:
            rb, zq, uq = part("RB", t - 1), part("zp", t - 1), part("uu", t - 1)
            mms(spread, [(R("nI"), R("off")), (rb, R("Bo"))])
            for x in twice:
                mm(x, R("Bo"), rb, x is twice[0])
            mm(spread, R("t2"), R("Wall"))
            for x in twice:
                mm(x, R("Wall"), R("t2"))
            act(R("xm"), spread, F.Relu)
            take_tops(t - 1, Zall)
            act(R("thr", 0, 256), R(BQ, 0, 256), scale=c15)
        sel(R("thr", 256, 512), R("thr", 0, 256), [[0, 256]], A.is_ge, 0, 0)
        for (lo, hi, la, lb) in LISTS:
            q = R("q", lo, hi)
            mm(la, R("xm"), R("Q97", lo, hi))
            mm(lb, R("xm"), R("Q97", lo, hi))
            act(q, la, bias=135.0 + 513.0 / 8192, scale=1.0 / W)
            mm(lb, R("m4k"), q)
        ts(R("cu", 0, CUT), LISTS[0][3], LIFT, A.add)
        if last and AFTER:
            put_days(48, 0, "rd", "rf")
        if t == 1:
            act(R("ld"), part("RN", 0), F.Relu)
        if t:
            act(zo, IND(Zw, src_list(t)))
            send([(STEP[t], zo, zr, "z%d" % t)])
        else:
            cp(R("rl", 0, 8), R("RT", 0, 8))
            ts(R("rl", 8, 16), R("RT", 8, 16), float(W), A.subtract)
            iota(R("Mb"), [[0, 8], [-1, 16]], 2, 0)
            sel(R("nC1"), R("nBo"), [[0, 8], [1, 16]], A.is_equal, -1, 0)
            sel(R("Mb"), R("Mb"), [[0, 8], [-1, 16]], A.is_ge, 3, 0)
            sel(R("C2"), R("Bo"), [[0, 8], [1, 16]], A.is_equal, -2, 0)
            sel(R("Mb"), R("Mb"), [[-16, 8], [0, 16]], A.is_ge, 0, 1)
            sel(R("IUp"), R("nBo"), [[-1, 128]], A.is_equal, -1, 1)
            sel(R("Mb"), R("Mb"), [[16, 8], [0, 16]], A.is_ge, 15, -1)
            sel(R("Ma"), R("Mb"), [[0, 8], [1, 16]], A.is_ge, -1, 0)
            sel(R("IUp"), R("IUp"), [[-1, 128]], A.not_equal, 0, 1, 1.0)
            iota(R("nL"), [[16, 8]], V - 2048, 1)
        mm(R(KEY, 0, 264), thr0, R("W97", 0, 264), True)
        mm(R(KEY, 32, 264, 33), rows("ones", 0), rows("c33", 0, 0, 8), kind="sum")
        turn2(t)
        for (k0, k1) in VCH[t]:
            tt(R("cmp", 128 * k0, 128 * k1), IND(Zc, R("cu", 8 * k0, 8 * k1)), R("thr", 0, 128 * (k1 - k0)), A.is_gt)
            if k0 == 0:
                ts(R("cu", CUT, 256), LISTS[1][3], LIFT, A.add)
            for k in range(k0, k1):
                tier_sum(k, part("cmp", k), "Wv")
        for j, sign in ((0, False), (1, False), (0, True), (2, False), (1, True), (2, True)):
            k0, k1 = SCH[t][j]
            n = 128 * (k1 - k0)
            raw, bank = R("raw", 512 * j, 512 * j + n), R((BR, BQ, BP)[j], 0, n)
            if not sign:
                act(raw, IND(Zc, R("cu", 8 * k0, 8 * k1)))
                mms(bank, [(R("nI"), R("thr", 0, n)), (R("I"), raw)])
                continue
            if j == 2:
                mms(R(BD, 0, 128), [(R("nI"), thr0), (R("I"), zr)])
                act(R("s33"), R(BD, 0, 128), F.Sign, bias=-0.5)
                tier_sum(32, R("s33"), "W33")
            act(R("cmp", 128 * k0, 128 * k1), bank, F.Sign, bias=-0.5)
            for k in range(k0, k1):
                tier_sum(k, part("cmp", k), "Ws")
        aim, vs = R(BU, 0, 128), R(BF, 0, 128)
        res, s1, s2 = part("res", t % 2), part("s12", 0), part("s12", 1)
        if t:
            done = to_days(zq, uq, "re")
        if not last:
            tops(R(BR, 0, 128), zr)
            tops(R(BR, 128, 256), zr, True)
            act(R("s12"), R(BR, 0, 256), F.Relu)
            act(part("zz", 3), IND(R("Z", W, V), R("jo", 8 * t, 8 * t + 8)))
            tops(R(BQ, 0, 128), part("zz", 3))
        if t:
            done()
        mm(R(BD, 128, 256), nBoR, R("s33"), True)
        act(R("nask"), R(BD, 128, 256), F.Relu, bias=-14.0 * HIT, scale=HIT)
        if last:
            mms(R(BR, 0, 128), [(R("I"), R("bar0")), (R("I"), R("nask")), (R("I"), R("nask"))])
            act(R("bar"), R(BR, 0, 128))
        else:
            act(res, R(BQ, 0, 128), F.Relu)
            send([(STEP[t + 1], res, part("RB", t), "s%d" % t)])
            both = [(R("I"), R("ld"))] * t + [(R("nC1"), s2), (R("nI"), R("nask"))]
            mms(R(BP, 0, 128), [(R("Mb"), s1)] + both + [(R("C2"), res)])
            mms(vs, [(R("Ma"), s1)] + both)
        if t:
            act(R("so"), zo, F.Sign)
        else:
            act(R("B4k"), R("Bo"), scale=4096.0)
            act(R("nE0"), R("nBo"), scale=R("LT", 1, 2))
            const(R("farm"), -BIG)
            act(wrow, tier, F.Square, bias=-1.5)
            act(R("farm", 0, 128, 16), R("nL"))
            act(wrow, wrow, bias=-1.25)
            act(R("WD", 128, 144), R("ones", 0, 16), scale=0.0, bias=c256)
            act(wrow, R("mask", 0, 1), scale=-0.5, bias=wrow)
        if t == 0:
            note_slots(0)
        if last:
            put_days(48, 1, "rd", "rf")
        scan(R("sc"), R("st%d" % KS[t], 0, 264), R(KEY, 0, 264), A.add, A.min)
        if not last:
            narrow(t + 1, 0)
        ts(R("km"), R("sc", 32, 264, 33), (3 << 22) | (W - 1), A.bitwise_and)
        if not last:
            narrow(t + 1, 1)
        ts(R("A16"), IND(R("km"), R("ex")), 8192.0, A.min, 2048.0, A.subtract)
        if t == 0:
            times([("Row4", "nBo", R("mask", 4, 5)), ("Up", "nU1", -1.0 / 256)])
        if t == 1:
            ts(R("bar0"), R("off"), float(W), A.add)
        tt(R("B16"), cap, R("A16"), A.min)
        if t:
            put_days(24 * t - 16, 0, "re")
        else:
            note_slots(4)
        mm(R(BD, 128, 136), R("off"), grp, True)
        mm(R(BD, 0, 128), R("A16"), R("I"))
        mm(R(BD, 128, 136), R("B16"), grp)
        mms(R(BE, 0, DW), [(R("off"), R("RD")), (R("I"), R("tri"))])
        for (c0, c1, first) in DSEG:
            mm(R(BE, c0, c1), R("A16"), R("I", first, 128))
        mm(R(BE, 0, DW), R("B16"), R("RD"))
        act(R("sp"), R(BE, 0, DW), F.Sign, bias=0.5)
        act(R("sm"), R(BE, 0, DW), F.Sign, bias=0.5, scale=-1.0)
        if not last:
            act(R("T2"), R(BP, 0, 128), bias=c256)
        mms(aim, [(R("I"), R("off")), (R("A16"), R("I"))])
        sums = BU if last else BF
        for q in range(-1, NV + 1):
            if q == (-1 if last else NV):
                ts(R("dU"), R(BD, 128, 136), 2048.0, A.add, float(W - 1), A.min)
            if 0 <= q < NV:
                e = R("E", EOFF[q], EOFF[q + 1])
                ts(e, R(BD, 16 * q + 16, 128), R(BD, 128 + q, 129 + q), A.is_equal, 2.0, A.mult)
                mm(R(sums, 16 * q + 16, 128), R("B4k"), e, kind="sum")
        for x in ("sp", "sm"):
            for (c0, c1, first) in DSEG:
                mm(R(sums, first, 128), R("B4k"), R(x, c0, c1), kind="sum")
        if t:
            put_days(24 * t - 16, 1, "re")
        else:
            read_slots(0)
        gone = part("G", t)
        if last:
            tt(gone, aim, R("bar"), A.is_lt)
        else:
            nl = part("NL", t)
            tt(nl, R("T2"), vs, A.subtract)
            ts(part("wn", t), vs, 0.0, A.min, c256, A.add)
            ts(gone, vs, 1024.0, A.is_le)
            send([(STEP[t + 1], nl, part("RN", t), "n%d" % t),
                  (STEP[t + 1] - STEP[t], part("wn", t), part("WD", t, 144), "w%d" % t)])
            mm(aim, R("Row4"), nl)
        if t == 0:
            scan(R("js"), R("rst"), R("jm"), A.mult, A.add)
            ts(R("far"), R("trk", 8, 24), 2048.0, A.subtract)
        send([(-STEP[t], gone, part("RG", t), "g%d" % t)])
        if t == 0:
            send([(STEP[2], R("pm2"), R("PM2"), "p2")])
        lo = 0 if last else 24 * (t + 1)
        scan(R("ll"), R("farm"), aim, A.max, A.min)
        if t == 0:
            list_slots(0)
        ts(R("SL", lo, lo + 8), R("ll", 15, 128, 16), 2048.0, A.add)
        if not last:
            tt(R("mx", 0, 8), R("ll", 15, 128, 16), R("far", 8 * t, 8 * t + 8), A.min)
        St, Sw = (Yall, Yw) if last else (Zall, Zw)
        first = [(R("nI256"), R("ed")), (R("D1"), R("ed"))]
        act(R("ed"), IND(Zc, R("dU")), F.Relu, bias=1.0, scale=-1.0)
        if not last:
            act(R("zd"), IND(Sw, R("dU")))
        mms(R(BR, 0, 128), [(R("E0" if last else "nE0"), thr0)] + first)
        act(R("fd"), R(BR, 0, 128), F.Relu, scale=-1.0, bias=0.0 if last else -256.0)
        if last:
            act(R("zd"), IND(Sw, R("dU")))
        tt(IND(St, R("SL", lo, lo + 8)), R("zd"), R("fd"), A.add)
        if not last and not AFTER:
            ts(R("SL", lo + 8, lo + 16), R("mx", 0, 8), 2048.0, A.add)
        if t == 0:
            ts(R("Wall"), R("Bo"), wrow, A.mult, lt4, A.mult)
            act(R("E0"), R("nE0"), scale=-1.0)
            act(R("WD", 272, 288), R("ones", 0, 16), scale=0.0, bias=c256)
        mms(R(KEY, 0, 128), [(R("Up"), R("so")), (R("nE0"), R("so"))])
        if not last:
            if not DIRECT:
                act(R("gg"), R(KEY, 0, 128))
            turned = turn1(t + 1)
            if not AFTER:
                turned()
        if t == 1:
            mms(R(BR, 128, 256), [(R("nI256"), R("ed")), (R("nI"), R("zd"))])
            mms(R(BR, 256, 384), [(R("E0"), thr0)] + first)
            act(R("rd"), R(BR, 128, 256), bias=256.0)
            act(R("rf"), R(BR, 256, 384), F.Relu, scale=-1.0)
            if not AFTER:
                put_days(lo, 0, "rd", "rf")
        act(zp, IND(Sw, src_list(t)))
        mm(shift, R("IUp"), zp, True)

    take_tops(2, Yall)
    dma("y", T.y[:], T.Y[:, 0:V], Yw, store=True)

    cnt = {s: 0 for s in ESEM.values()}
    known = {e: {} for e in Q}
    clock = {}
    hist = {}
    dmas = []

    def need(e, toks):
        kn = known[e]
        best = {}
        for (s, c) in toks:
            if kn.get(s, 0) < c and best.get(s, 0) < c:
                best[s] = c
        for s in sorted(best, key=lambda x: -len(clock.get((x, best[x]), {}))):
            c = best[s]
            if kn.get(s, 0) >= c:
                continue
            Q[e].wait_ge(T.sem[s], c)
            kn[s] = c
            for s2, c2 in clock.get((s, c), {}).items():
                if kn.get(s2, 0) < c2:
                    kn[s2] = c2

    def note(c, tok):
        for regs, wr in ((c["reads"], False), (c["writes"], True)):
            for (n, lo, hi) in regs:
                hist.setdefault(n, []).append((lo, hi, wr, c["e"], tok))

    for c in calls:
        if c["kind"] == "land":
            note(c, (c["lands"], landed[c["lands"]]))
    if not ORDER:
        ORDER.extend(plan(calls))
    closing = set(SCRATCH)
    for j in reversed(ORDER):
        c = calls[j]
        if c["e"] == "p":
            bank = c["writes"][0][0]
            if bank in closing:
                c["stop"].append(True)
                closing.remove(bank)
            if c["start"]:
                closing.add(bank)
    for j in ORDER:
        c = calls[j]
        e = c["e"]
        need(e, [tok for (e2, tok, wait) in clashes(hist, e, c["reads"], c["writes"]) if wait])
        if c["kind"] == "send":
            c["issue"]()
            continue
        if c["kind"] == "dma":
            tok = ("d%d" % len(dmas), 16)
            dmas.append(tok)
        else:
            cnt[ESEM[e]] += 1
            tok = (ESEM[e], cnt[ESEM[e]])
        c["issue"]().then_inc(T.sem[tok[0]], 16 if c["kind"] == "dma" else 1)
        clock[tok] = dict(known[e])
        note(c, tok)
    need("y", dmas[-1:])
    need("g", list(landed.items()) + list(cnt.items()) + dmas[:-1] + [("sent", sent[0])])
